import numpy as np
import ml_dtypes


def mxq(x, axis, fmt="e4m3"):
    dtype, down = {"e4m3": (ml_dtypes.float8_e4m3fn, 7), "e5m2": (ml_dtypes.float8_e5m2, 14)}[fmt]
    v = np.moveaxis(np.asarray(x, np.float32).astype(ml_dtypes.bfloat16).astype(np.float64), axis, -1)
    blocks = v.reshape(v.shape[:-1] + (-1, 32))
    amax = np.abs(blocks).max(-1, keepdims=True)
    byte = np.maximum(np.where(amax > 0, np.frexp(amax)[1] - 1 + 127, 0) - down, 1)
    scale = np.exp2(byte - 127.0)
    codes = (blocks / scale).astype(np.float32).astype(dtype).astype(np.float64)
    return np.moveaxis((codes * scale).reshape(v.shape), -1, axis)


WIDE = False


def mx_kscale(k):
    if not WIDE:
        return np.ones(k)
    levels = np.array([30, -30])
    if k % 512:
        return np.exp2(np.random.permutation(np.resize(levels, k // 32))).repeat(32)
    a = np.empty((k // 512, 16))
    for p in range(k // 512):
        a[p, :8] = np.random.permutation(np.resize(levels, 8))
        for g in range(8):
            far = levels[np.abs(levels - a[p, g]) >= 10]
            a[p, g + 8] = far[np.random.randint(len(far))]
    return np.exp2(a.ravel()).repeat(32)


def f64(x):
    return np.asarray(x).astype(np.float64)


def striped(idx):
    return np.tile(idx.reshape(-1, 16).T, (8, 1)).astype(np.uint16)


def unstriped(offs):
    return offs[:16].T.reshape(-1).astype(np.int64)


E2M1 = np.array([0.0, 0.5, 1.0, 1.5, 2.0, 3.0, 4.0, 6.0, -0.0, -0.5, -1.0, -1.5, -2.0, -3.0, -4.0, -6.0])


def pack_weight(w, fmt):
    k, n = w.shape
    w = f64(np.asarray(w, np.float32).astype(ml_dtypes.bfloat16)).reshape(k // 32, 32, n)
    amax = np.abs(w).max(1)
    if fmt == "e4m3":
        byte = np.frexp(amax)[1] - 1 + 127 - 7
    else:
        mant, ex = np.frexp(amax / 6.0)
        byte = np.where(mant > 0.5, ex, ex - 1) + 127
    byte = np.clip(np.where(amax > 0, byte, 1), 1, 254)
    scaled = (w * np.exp2(127.0 - byte)[:, None, :]).reshape(k, n).astype(np.float32)
    by_word = np.ascontiguousarray(scaled.reshape(k // 512, 128, 4, n).transpose(0, 1, 3, 2))
    if fmt == "e4m3":
        words = by_word.astype(ml_dtypes.float8_e4m3fn).view(np.uint8)
    else:
        c = by_word.astype(ml_dtypes.float4_e2m1fn).view(np.uint8) & 0xF
        words = (c[..., 0::2] | (c[..., 1::2] << 4)).reshape(k // 512, 128, 2 * n)
    return np.ascontiguousarray(words), np.ascontiguousarray(byte.astype(np.uint8).reshape(k // 512, 16, n))


def unpack_weight(words, scales, fmt):
    g, _, n = scales.shape
    words = np.ascontiguousarray(words).reshape(g, 128, n, -1)
    if fmt == "e4m3":
        vals = words.view(ml_dtypes.float8_e4m3fn).astype(np.float64)
    else:
        nib = np.empty((g, 128, n, 4), np.uint8)
        nib[..., 0::2] = words & 0xF
        nib[..., 1::2] = words >> 4
        vals = E2M1[nib]
    vals = vals * np.repeat(np.exp2(scales.astype(np.float64) - 127.0), 8, axis=1)[..., None]
    return vals.transpose(0, 1, 3, 2).reshape(g * 512, n)


def d_relu2(v):
    return 2.0 * np.maximum(v, 0.0)


K, T, E, C, H, N = 128, 1024, 4, 512, 512, 1536


def by_expert(wq, xq):
    return np.concatenate([wq[e].T @ xq[:, e * C:(e + 1) * C] for e in range(E)], axis=1)


def setup_inputs():
    n = np.random.standard_normal
    s = mx_kscale(N)[:, None]
    u = mx_kscale(H)
    first = np.random.permutation(np.repeat(np.arange(E), T // E))
    second = (first + 1 + np.random.permutation(np.repeat(np.arange(E - 1), -(-T // (E - 1)))[:T])) % E
    while np.bincount(second, minlength=E).max() != T // E:
        load = np.bincount(second, minlength=E); hi, lo = int(load.argmax()), int(load.argmin())
        t = np.flatnonzero((second == hi) & (first != lo))[0]; second[t] = lo
    slot_token = np.empty(E * C, np.int64); pos = np.empty((2, T), np.int64); fill = np.zeros(E, np.int64)
    place = np.stack([np.random.permutation(C) for _ in range(E)])
    for r, deal in enumerate((first, second)):
        for t in np.random.permutation(T):
            e = deal[t]; j = e * C + place[e, fill[e]]; fill[e] += 1; slot_token[j] = t; pos[r, t] = j
    g = np.random.uniform(0.2, 0.8, T)
    w_slot = np.empty(E * C); w_slot[pos[0]] = g; w_slot[pos[1]] = 1.0 - g
    w2 = [pack_weight(m, "e2m1") for m in n((E, N, H)) / np.sqrt(N) / s[None] * u[None, None, :]]
    w1 = [pack_weight(m, "e2m1") for m in n((E, H, K)) / np.sqrt(H) / u[None, :, None]]
    return {
        "dyT": (n((N, T)) * s).astype(np.float32),
        "a": n((H, E * C)).astype(np.float32),
        "w2_words": np.stack([m[0] for m in w2]),
        "w2_scales": np.stack([m[1] for m in w2]),
        "w1_words": np.stack([m[0] for m in w1]),
        "w1_scales": np.stack([m[1] for m in w1]),
        "gate": np.tile(w_slot, (N, 1)).astype(np.float32),
        "offs": striped(slot_token),
        "pos1": striped(pos[0]),
        "pos2": striped(pos[1]),
    }


def reference(dyT, a, w2_words, w2_scales, w1_words, w1_scales, gate, offs, pos1, pos2):
    idx = unstriped(offs)
    w2 = np.stack([unpack_weight(w2_words[e], w2_scales[e], "e2m1") for e in range(E)])
    w1 = np.stack([unpack_weight(w1_words[e], w1_scales[e], "e2m1") for e in range(E)])
    gq = mxq(f64(gate) * f64(dyT)[:, idx], 0, "e5m2")
    dh = by_expert(w2, gq)
    da = dh * d_relu2(f64(a))
    dx = by_expert(w1, mxq(da, 0, "e5m2"))
    return dx[:, unstriped(pos1)] + dx[:, unstriped(pos2)]

@@ -1,0 +1,416 @@
+from contextlib import ExitStack
+
+import concourse.mybir as mybir
+from concourse.masks import make_identity
+
+K, T, E, C, H, N = 128, 1024, 4, 512, 512, 1536
+P = 128
+PACK = 4
+SLOTS = E * C
+PASSES = N // 512
+QT = C // P
+
+FLOPS = 2 * SLOTS * (N * H + H * K)
+BYTES = (
+    4 * N * T + 4 * H * SLOTS + E * PASSES * (128 * 1024 + 16 * 512)
+    + E * (128 * 256 + 16 * 128) + 4 * SLOTS + 2 * 128 * (128 + 64 + 64) + 4 * K * T
+)
+
+F32 = mybir.dt.float32
+BF16 = mybir.dt.bfloat16
+I32 = mybir.dt.int32
+U32 = mybir.dt.uint32
+U16 = mybir.dt.uint16
+U8 = mybir.dt.uint8
+E5M2 = mybir.dt.float8_e5m2_x4
+E2M1 = mybir.dt.float4_e2m1fn_x4
+MULT = mybir.AluOpType.mult
+ADD = mybir.AluOpType.add
+COPY = mybir.ActivationFunctionType.Copy
+RELU = mybir.ActivationFunctionType.Relu
+
+
+def tile_moe_bdx_mlp_relu2_kernel(
+    tc, dyT, a, w2_words, w2_scales, w1_words, w1_scales, gate, offs, pos1, pos2, out
+):
+    nc = tc.nc
+    PAIR = 2 * C
+    with ExitStack() as ctx:
+        keep = ctx.enter_context(tc.tile_pool(name="keep", bufs=1))
+        gathered = ctx.enter_context(tc.tile_pool(name="gathered", bufs=2))
+        grouped = ctx.enter_context(tc.tile_pool(name="grouped", bufs=2))
+        coded = ctx.enter_context(tc.tile_pool(name="coded", bufs=4))
+        hidden = ctx.enter_context(tc.tile_pool(name="hidden", bufs=4))
+        a_pool = ctx.enter_context(tc.tile_pool(name="a_pool", bufs=2))
+        last_da = ctx.enter_context(tc.tile_pool(name="last_da", bufs=2))
+        da_codes_pool = ctx.enter_context(tc.tile_pool(name="da_codes_pool", bufs=3))
+        slope_pool = ctx.enter_context(tc.tile_pool(name="slope_pool", bufs=4))
+        dh_psum = ctx.enter_context(tc.psum_pool(name="dh_psum", bufs=5))
+        tr_psum = ctx.enter_context(tc.psum_pool(name="tr_psum", bufs=3))
+
+        offs_sb = keep.tile([P, SLOTS // 16], U16, name="offs_sb")
+        pos1_sb = keep.tile([P, T // 16], U16, name="pos1_sb")
+        pos2_sb = keep.tile([P, T // 16], U16, name="pos2_sb")
+        gates = [keep.tile([P, PAIR], F32, name=f"gate{e}") for e in range(2)]
+        planes = [
+            [keep.tile([P, T + 8], F32, name=f"dy{s}_{t}") for t in range(PACK)] for s in range(PASSES)
+        ]
+        w2_sb = [keep.tile([P, PASSES * 1024], U8, name=f"w2_{e}", align_bytes=64) for e in range(E)]
+        w2_sc = keep.tile([P, E * PASSES * H], U8, name="w2_sc", align_bytes=64)
+        w1_sb = keep.tile([P, E * 256], U8, name="w1_sb", align_bytes=64)
+        w1_sc = keep.tile([P, E * K], U8, name="w1_sc", align_bytes=64)
+        a_sb = {}
+        ident = keep.tile([P, P], F32, name="ident")
+        ident_bf = keep.tile([P, P], BF16, name="ident_bf")
+        dx_sb = keep.tile([P, SLOTS], F32, name="dx_sb")
+
+        for s in range(PASSES):
+            for t in range(PACK):
+                nc.vector.memset(planes[s][t][:, T : T + 8], 0.0)
+        nc.gpsimd.memset(w2_sc[:].bitcast(I32), 0)
+        nc.gpsimd.memset(w1_sc[:].bitcast(I32), 0)
+        make_identity(nc, ident[:])
+        make_identity(nc, ident_bf[:])
+
+        dy_rows = dyT.rearrange("(s p t) j -> s t p j", p=P, t=PACK)
+
+        def load_plane(s, t):
+            nc.sync.dma_start(out=planes[s][t][:, 0:T], in_=dy_rows[s, t])
+
+        def load_gate(e):
+            nc.sync.dma_start(
+                out=gates[e // 2][:, (e % 2) * C : (e % 2 + 1) * C], in_=gate[0:P, e * C : (e + 1) * C]
+            )
+
+        def load_w2(e):
+            nc.sync.dma_start(
+                out=w2_sb[e][:].bitcast(I32).rearrange("p (s w) -> p s w", s=PASSES),
+                in_=w2_words.bitcast(I32)[e].rearrange("s p w -> p s w"),
+            )
+
+        def load_a(e):
+            a_sb[e] = a_pool.tile([P, PACK, C], F32, name="a")
+            nc.sync.dma_start(
+                out=a_sb[e][:], in_=a[:, e * C : (e + 1) * C].rearrange("(p t) c -> p t c", t=PACK)
+            )
+
+        def load_scales():
+            src2 = w2_scales.bitcast(I32).rearrange("e s f w -> f (e s) w")
+            src1 = w1_scales.bitcast(I32).rearrange("e s f w -> f (e s) w")
+            for q in range(4):
+                rows = slice(32 * q, 32 * q + 4)
+                nc.sync.dma_start(
+                    out=w2_sc[rows, :].bitcast(I32).rearrange("f (g w) -> f g w", g=E * PASSES),
+                    in_=src2[4 * q : 4 * q + 4],
+                )
+            for q in range(4):
+                rows = slice(32 * q, 32 * q + 4)
+                nc.sync.dma_start(
+                    out=w1_sc[rows, :].bitcast(I32).rearrange("f (g w) -> f g w", g=E),
+                    in_=src1[4 * q : 4 * q + 4],
+                )
+
+        nc.sync.dma_start(offs_sb[:], offs)
+        load_gate(0)
+        load_plane(0, 0)
+        load_gate(1)
+        for t in range(1, PACK):
+            load_plane(0, t)
+        load_a(0)
+        for t in range(PACK):
+            load_plane(1, t)
+        load_a(1)
+        load_gate(2)
+        load_gate(3)
+        for t in range(PACK):
+            load_plane(2, t)
+
+        codes = {}
+        dh_banks = {}
+        slopes = {}
+        da_parts = {}
+
+        def gather(g32, s, t, slot0, n):
+            base = slot0 % PAIR
+            here = slot0 % g32.shape[2]
+            nc.vector.tensor_tensor(
+                g32[:, t, here : here + n],
+                planes[s][t][:].indirect(offs_sb[:, slot0 // 16 : (slot0 + n) // 16]),
+                gates[slot0 // PAIR][:, base : base + n],
+                MULT,
+            )
+
+        def interleave(g32, n):
+            gb = grouped.tile([P, n, PACK], BF16, name="gb", align_bytes=64)
+            nc.scalar.activation(
+                gb[:].rearrange("p (c i) t -> p c t i", i=4),
+                g32[:].rearrange("p t (c i) -> p c t i", i=4),
+                COPY,
+            )
+            return gb
+
+        def quantise(gb, n):
+            words = coded.tile([P, n], U32, name="g_words", align_bytes=64)
+            scales = coded.tile([P, n], U8, name="g_scales", align_bytes=64)
+            nc.vector.quantize_mx(
+                out=words[:].bitcast(E5M2),
+                scales=scales[:],
+                in_=gb[:].rearrange("p c t -> p (c t)"),
+            )
+            return words, scales
+
+        def multiply2(e, s, qs=range(QT)):
+            words, scales, base = codes[e, s]
+            for q in qs:
+                if s == 0:
+                    dh_banks[e, q] = dh_psum.tile([P, H], F32, name="dh")
+                cols = slice(base + q * P, base + (q + 1) * P)
+                nc.tensor.matmul_mx(
+                    out=dh_banks[e, q][:],
+                    lhsT=words[:, cols].bitcast(E5M2),
+                    lhsT_scale=scales[:, cols],
+                    rhs=w2_sb[e][:, s * 1024 : (s + 1) * 1024].bitcast(E2M1),
+                    rhs_scale=w2_sc[:, (e * PASSES + s) * H : (e * PASSES + s + 1) * H],
+                    start=(s == 0),
+                    stop=(s == PASSES - 1),
+                )
+
+        def slope(e):
+            slopes[e] = slope_pool.tile([P, QT, PACK, P], F32, name="slope")
+            for q in range(QT):
+                bank = tr_psum.tile([P, PACK, P], F32, name="turned")
+                for t in range(PACK):
+                    nc.tensor.transpose(bank[:, t, :], a_sb[e][:, t, q * P : (q + 1) * P], ident[:])
+                nc.scalar.activation(slopes[e][:, q, :, :], bank[:], RELU, scale=2.0)
+
+        by_slot = {}
+
+        def make_da(e):
+            da_parts[e] = (
+                last_da.tile([P, C, PACK], BF16, name="da", align_bytes=64),
+                da_codes_pool.tile([P, C], U32, name="da_words", align_bytes=64),
+                da_codes_pool.tile([P, C], U8, name="da_scales", align_bytes=64),
+                0,
+            )
+
+        def times(e, q):
+            if e == 2 and q >= 2:
+                by_slot[e, q] = grouped.tile([P, PACK, P], BF16, name="gb", align_bytes=64)
+            else:
+                by_slot[e, q] = hidden.tile([P, PACK, P], BF16, name="by_slot")
+            nc.vector.tensor_tensor(
+                by_slot[e, q][:],
+                dh_banks[e, q][:].rearrange("p (m t) -> p t m", t=PACK),
+                slopes[e][:, q, :, :],
+                MULT,
+            )
+
+        def turn(e, q, copy):
+            if e not in da_parts:
+                make_da(e)
+            bank = tr_psum.tile([P, PACK, P], BF16, name="turned")
+            for t in range(PACK):
+                nc.tensor.transpose(bank[:, t, :], by_slot[e, q][:, t, :], ident_bf[:])
+            copy(da_parts[e][0][:, q * P : (q + 1) * P, :], bank[:].rearrange("p t c -> p c t"))
+
+        def quantise_da(e, c0, c1):
+            da, words, scales, base = da_parts[e]
+            nc.vector.quantize_mx(
+                out=words[:, c0:c1].bitcast(E5M2),
+                scales=scales[:, c0:c1],
+                in_=da[:, c0:c1, :].rearrange("p c t -> p (c t)"),
+            )
+
+        def multiply1(e):
+            da, words, scales, base = da_parts[e]
+            dx = tr_psum.tile([P, C], F32, name="turned")
+            nc.tensor.matmul_mx(
+                out=dx[:],
+                lhsT=w1_sb[:, e * 256 : (e + 1) * 256].bitcast(E2M1),
+                lhsT_scale=w1_sc[:, e * K : (e + 1) * K],
+                rhs=words[:, base : base + C].bitcast(E5M2),
+                rhs_scale=scales[:, base : base + C],
+                start=True,
+                stop=True,
+            )
+            nc.scalar.activation(dx_sb[:, e * C : (e + 1) * C], dx[:], COPY)
+
+        def finish(e):
+            quantise_da(e, 0, C)
+            multiply1(e)
+
+        def pair_gathers(pair, s, g32, ts):
+            for t in ts:
+                if pair == 0 and s == 0 and t == 0:
+                    gather(g32, s, t, 0, C)
+                    gather(g32, s, t, C, C)
+                else:
+                    gather(g32, s, t, pair * PAIR, PAIR)
+
+        def pair_tile():
+            return gathered.tile([P, PACK, PAIR], F32, name="g32")
+
+        def pair_codes(gb, pair, s):
+            words, scales = quantise(gb, PAIR)
+            for x in range(2):
+                codes[2 * pair + x, s] = (words, scales, x * C)
+
+        def interleave_half(g32):
+            gb = grouped.tile([P, C, PACK], BF16, name="gb", align_bytes=64)
+            nc.scalar.activation(
+                gb[:].rearrange("p (c i) t -> p c t i", i=4),
+                g32[:].rearrange("p t (c i) -> p c t i", i=4),
+                COPY,
+            )
+            return gb
+
+        g = pair_tile()
+        pair_gathers(0, 0, g, range(4))
+        b = interleave(g, PAIR)
+        slope(0)
+        load_a(2)
+        load_scales()
+        load_w2(0)
+        load_w2(1)
+        nc.sync.dma_start(
+            out=w1_sb[:].bitcast(I32).rearrange("p (e w) -> p e w", e=E),
+            in_=w1_words.bitcast(I32).rearrange("e s p w -> p (e s) w"),
+        )
+        load_w2(2)
+        load_w2(3)
+        nc.sync.dma_start(pos1_sb[:], pos1)
+        nc.sync.dma_start(pos2_sb[:], pos2)
+        for s in (1, 2):
+            g = pair_tile()
+            pair_gathers(0, s, g, range(3))
+            pair_codes(b, 0, s - 1)
+            multiply2(0, s - 1)
+            pair_gathers(0, s, g, range(3, 4))
+            b = interleave(g, PAIR)
+            slope(s)
+            if s == 1:
+                load_a(3)
+        def single(e, s):
+            g1 = gathered.tile([P, PACK, C], F32, name="g32")
+            for t in range(4):
+                gather(g1, s, t, e * C, C)
+            return g1
+
+        def single_codes(e, s, gb):
+            codes[e, s] = quantise(gb, C) + (0,)
+
+        g = pair_tile()
+        pair_gathers(1, 0, g, range(4))
+        b_next = interleave(g, PAIR)
+        pair_codes(b, 0, 2)
+        b = b_next
+        multiply2(0, 2)
+        for q in range(QT):
+            times(0, q)
+        for q in range(QT):
+            for s in range(PASSES):
+                multiply2(1, s, (q,))
+            turn(0, q, nc.scalar.copy)
+        slope(3)
+        g = single(2, 1)
+        b21 = interleave_half(g)
+        for q in range(QT):
+            times(1, q)
+        pair_codes(b, 1, 0)
+        multiply2(2, 0)
+        for q in range(QT):
+            turn(1, q, nc.scalar.copy)
+        quantise_da(0, 0, C)
+        multiply1(0)
+        g = single(2, 2)
+        b22 = interleave_half(g)
+        single_codes(2, 1, b21)
+        multiply2(2, 1)
+        quantise_da(1, 0, C)
+        multiply1(1)
+        g = single(3, 1)
+        single_codes(2, 2, b22)
+        multiply2(2, 2)
+        b31 = interleave_half(g)
+        for q in range(2):
+            times(2, q)
+            turn(2, q, nc.scalar.copy)
+        multiply2(3, 0, range(2))
+        HALF = C // 2
+        b32 = [
+            grouped.tile([P, HALF, PACK], BF16, name="gb", align_bytes=64),
+            hidden.tile([P, HALF, PACK], BF16, name="b32_late", align_bytes=64),
+        ]
+        words32 = coded.tile([P, C], U32, name="g_words", align_bytes=64)
+        scales32 = coded.tile([P, C], U8, name="g_scales", align_bytes=64)
+        codes[3, 2] = (words32, scales32, 0)
+
+        def last_gather(h):
+            if h == 0:
+                g1 = gathered.tile([P, PACK, HALF], F32, name="g32")
+            else:
+                g1 = grouped.tile([P, PACK, HALF], F32, name="gb", align_bytes=64)
+            for t in range(4):
+                gather(g1, 2, t, 3 * C + h * HALF, HALF)
+            return g1
+
+        def last_interleave(g1, h):
+            nc.scalar.activation(
+                b32[h][:].rearrange("p (c i) t -> p c t i", i=4),
+                g1[:].rearrange("p t (c i) -> p c t i", i=4),
+                COPY,
+            )
+
+        def last_quantise(h):
+            cols = slice(h * HALF, (h + 1) * HALF)
+            nc.vector.quantize_mx(
+                out=words32[:, cols].bitcast(E5M2),
+                scales=scales32[:, cols],
+                in_=b32[h][:].rearrange("p c t -> p (c t)"),
+            )
+
+        g = last_gather(0)
+        last_interleave(g, 0)
+        single_codes(3, 1, b31)
+        multiply2(3, 1, range(2))
+        g = last_gather(1)
+        last_quantise(0)
+        multiply2(3, 2, range(2))
+        last_interleave(g, 1)
+        times(2, 2)
+        turn(2, 2, nc.scalar.copy)
+        for q in range(2):
+            times(3, q)
+            turn(3, q, nc.scalar.copy)
+        multiply2(3, 0, (2,))
+        multiply2(3, 1, (2,))
+        last_quantise(1)
+        multiply2(3, 2, (2,))
+        times(2, 3)
+        turn(2, 3, nc.scalar.copy)
+        multiply2(3, 0, (3,))
+        multiply2(3, 1, (3,))
+        multiply2(3, 2, (3,))
+        times(3, 2)
+        turn(3, 2, nc.vector.tensor_copy)
+        times(3, 3)
+        quantise_da(2, 0, C)
+        multiply1(2)
+        turn(3, 3, nc.vector.tensor_copy)
+        quantise_da(3, 0, C // 2)
+        quantise_da(3, C // 2, C)
+        multiply1(3)
+
+        first = slope_pool.tile([P, T], F32, name="slope")
+        second = slope_pool.tile([P, T], F32, name="slope")
+        total = slope_pool.tile([P, T], F32, name="slope")
+        nc.vector.tensor_copy(first[:], dx_sb[:].indirect(pos1_sb[:]))
+        lo = 0
+        for width, adder in ((640, nc.gpsimd), (384, nc.vector)):
+            cols = slice(lo, lo + width)
+            nc.vector.tensor_copy(
+                second[:, cols], dx_sb[:].indirect(pos2_sb[:, lo // 16 : (lo + width) // 16])
+            )
+            adder.tensor_tensor(total[:, cols], first[:, cols], second[:, cols], ADD)
+            nc.sync.dma_start(out=out[:, cols], in_=total[:, cols])
+            lo += width

@@ -9,6 +9,8 @@ PACK = 4
 SLOTS = E * C
 PASSES = N // 512
 QT = C // P
+PAIR = 2 * C
+PAD = 8
 
 FLOPS = 2 * SLOTS * (N * H + H * K)
 BYTES = (
@@ -34,53 +36,52 @@ def tile_moe_bdx_mlp_relu2_kernel(
     tc, dyT, a, w2_words, w2_scales, w1_words, w1_scales, gate, offs, pos1, pos2, out
 ):
     nc = tc.nc
-    PAIR = 2 * C
     with ExitStack() as ctx:
         keep = ctx.enter_context(tc.tile_pool(name="keep", bufs=1))
-        gathered = ctx.enter_context(tc.tile_pool(name="gathered", bufs=2))
+        arena = ctx.enter_context(tc.tile_pool(name="arena", bufs=1))
         grouped = ctx.enter_context(tc.tile_pool(name="grouped", bufs=2))
-        coded = ctx.enter_context(tc.tile_pool(name="coded", bufs=4))
+        coded = ctx.enter_context(tc.tile_pool(name="coded", bufs=5))
         hidden = ctx.enter_context(tc.tile_pool(name="hidden", bufs=4))
-        a_pool = ctx.enter_context(tc.tile_pool(name="a_pool", bufs=2))
-        last_da = ctx.enter_context(tc.tile_pool(name="last_da", bufs=2))
-        da_codes_pool = ctx.enter_context(tc.tile_pool(name="da_codes_pool", bufs=3))
-        slope_pool = ctx.enter_context(tc.tile_pool(name="slope_pool", bufs=4))
-        dh_psum = ctx.enter_context(tc.psum_pool(name="dh_psum", bufs=5))
-        tr_psum = ctx.enter_context(tc.psum_pool(name="tr_psum", bufs=3))
+        da_pool = ctx.enter_context(tc.tile_pool(name="da_pool", bufs=3))
+        psum = ctx.enter_context(tc.psum_pool(name="psum", bufs=1))
+
+        G32_BYTES = 4 * PACK * PAIR
+        SLOPE_BYTES = 4 * QT * H
+        SLOPE_AT = 2 * G32_BYTES
+
+        def bank(b):
+            return psum.tile([P, 512], F32, name=f"bank{b}")
 
         offs_sb = keep.tile([P, SLOTS // 16], U16, name="offs_sb")
         pos1_sb = keep.tile([P, T // 16], U16, name="pos1_sb")
         pos2_sb = keep.tile([P, T // 16], U16, name="pos2_sb")
         gates = [keep.tile([P, PAIR], F32, name=f"gate{e}") for e in range(2)]
         planes = [
-            [keep.tile([P, T + 8], F32, name=f"dy{s}_{t}") for t in range(PACK)] for s in range(PASSES)
+            [keep.tile([P, T + PAD], F32, name=f"dy{s}_{t}") for t in range(PACK)] for s in range(PASSES)
         ]
         w2_sb = [keep.tile([P, PASSES * 1024], U8, name=f"w2_{e}", align_bytes=64) for e in range(E)]
         w2_sc = keep.tile([P, E * PASSES * H], U8, name="w2_sc", align_bytes=64)
         w1_sb = keep.tile([P, E * 256], U8, name="w1_sb", align_bytes=64)
         w1_sc = keep.tile([P, E * K], U8, name="w1_sc", align_bytes=64)
-        a_sb = {}
         ident = keep.tile([P, P], F32, name="ident")
-        ident_bf = keep.tile([P, P], BF16, name="ident_bf")
-        dx_sb = keep.tile([P, SLOTS], F32, name="dx_sb")
+        da_scales = keep.tile([P, 3 * C], U8, name="da_scales", align_bytes=64)
 
         for s in range(PASSES):
             for t in range(PACK):
-                nc.vector.memset(planes[s][t][:, T : T + 8], 0.0)
+                nc.vector.memset(planes[s][t][:, T : T + PAD], 0.0)
         nc.gpsimd.memset(w2_sc[:].bitcast(I32), 0)
         nc.gpsimd.memset(w1_sc[:].bitcast(I32), 0)
         make_identity(nc, ident[:])
-        make_identity(nc, ident_bf[:])
 
         dy_rows = dyT.rearrange("(s p t) j -> s t p j", p=P, t=PACK)
+        a_sb = {}
 
         def load_plane(s, t):
             nc.sync.dma_start(out=planes[s][t][:, 0:T], in_=dy_rows[s, t])
 
-        def load_gate(e):
-            nc.sync.dma_start(
-                out=gates[e // 2][:, (e % 2) * C : (e % 2 + 1) * C], in_=gate[0:P, e * C : (e + 1) * C]
-            )
+        def load_gate(lo, hi):
+            base = lo % PAIR
+            nc.sync.dma_start(out=gates[lo // PAIR][:, base : base + hi - lo], in_=gate[0:P, lo:hi])
 
         def load_w2(e):
             nc.sync.dma_start(
@@ -89,328 +90,281 @@ def tile_moe_bdx_mlp_relu2_kernel(
             )
 
         def load_a(e):
-            a_sb[e] = a_pool.tile([P, PACK, C], F32, name="a")
+            a_sb[e] = keep.tile([P, PACK, C], F32, name=f"a{e}", align_bytes=64)
             nc.sync.dma_start(
                 out=a_sb[e][:], in_=a[:, e * C : (e + 1) * C].rearrange("(p t) c -> p t c", t=PACK)
             )
 
-        def load_scales():
-            src2 = w2_scales.bitcast(I32).rearrange("e s f w -> f (e s) w")
-            src1 = w1_scales.bitcast(I32).rearrange("e s f w -> f (e s) w")
+        def load_scales(plane, source, groups):
+            src = source.bitcast(I32).rearrange("e s f w -> f (e s) w")
             for q in range(4):
-                rows = slice(32 * q, 32 * q + 4)
                 nc.sync.dma_start(
-                    out=w2_sc[rows, :].bitcast(I32).rearrange("f (g w) -> f g w", g=E * PASSES),
-                    in_=src2[4 * q : 4 * q + 4],
-                )
-            for q in range(4):
-                rows = slice(32 * q, 32 * q + 4)
-                nc.sync.dma_start(
-                    out=w1_sc[rows, :].bitcast(I32).rearrange("f (g w) -> f g w", g=E),
-                    in_=src1[4 * q : 4 * q + 4],
+                    out=plane[32 * q : 32 * q + 4, :].bitcast(I32).rearrange("f (g w) -> f g w", g=groups),
+                    in_=src[4 * q : 4 * q + 4],
                 )
 
+        FIRST = 384
         nc.sync.dma_start(offs_sb[:], offs)
-        load_gate(0)
         load_plane(0, 0)
-        load_gate(1)
-        for t in range(1, PACK):
-            load_plane(0, t)
-        load_a(0)
-        for t in range(PACK):
-            load_plane(1, t)
-        load_a(1)
-        load_gate(2)
-        load_gate(3)
-        for t in range(PACK):
-            load_plane(2, t)
+        load_gate(0, FIRST)
+        load_gate(FIRST, PAIR)
+        for s in range(PASSES):
+            for t in range(PACK):
+                if (s, t) != (0, 0):
+                    load_plane(s, t)
+            if s > 0:
+                load_a(s - 1)
+        load_gate(PAIR, SLOTS)
+        load_scales(w2_sc, w2_scales, E * PASSES)
+        load_w2(0)
+        load_a(2)
+        load_a(3)
+        for e in range(1, E):
+            load_w2(e)
 
         codes = {}
-        dh_banks = {}
+        dh = {}
         slopes = {}
-        da_parts = {}
+        by_slot = {}
 
-        def gather(g32, s, t, slot0, n):
-            base = slot0 % PAIR
-            here = slot0 % g32.shape[2]
+        def gather(g32, s, t, slot0, lo, n):
+            first = slot0 + lo
+            base = first % PAIR
             nc.vector.tensor_tensor(
-                g32[:, t, here : here + n],
-                planes[s][t][:].indirect(offs_sb[:, slot0 // 16 : (slot0 + n) // 16]),
-                gates[slot0 // PAIR][:, base : base + n],
+                g32[:, t, lo : lo + n],
+                planes[s][t][:].indirect(offs_sb[:, first // 16 : (first + n) // 16]),
+                gates[first // PAIR][:, base : base + n],
                 MULT,
             )
 
-        def interleave(g32, n):
-            gb = grouped.tile([P, n, PACK], BF16, name="gb", align_bytes=64)
+        def g32_tile(s, pair, at):
+            return arena.tile([P, PACK, PAIR], F32, name=f"g32_{pair}_{s}", offset=at, align_bytes=64)
+
+        def gathers(s, pair, at):
+            g32 = g32_tile(s, pair, at)
+            for t in range(PACK):
+                if (s, pair, t) == (0, 0, 0):
+                    gather(g32, s, t, 0, 0, FIRST)
+                    gather(g32, s, t, 0, FIRST, PAIR - FIRST)
+                else:
+                    gather(g32, s, t, pair * PAIR, 0, PAIR)
+            return g32
+
+        def interleave(g32, lo, n, after_a=None):
+            if after_a is None:
+                gb = grouped.tile([P, n, PACK], BF16, name="gb", align_bytes=64)
+            else:
+                gb = keep.tile([P, n, PACK], BF16, name=f"a{after_a}", align_bytes=64)
             nc.scalar.activation(
                 gb[:].rearrange("p (c i) t -> p c t i", i=4),
-                g32[:].rearrange("p t (c i) -> p c t i", i=4),
+                g32[:, :, lo : lo + n].rearrange("p t (c i) -> p c t i", i=4),
                 COPY,
             )
             return gb
 
-        def quantise(gb, n):
-            words = coded.tile([P, n], U32, name="g_words", align_bytes=64)
+        def quantise(gb, s, slot0, n, at=None):
+            if at is None:
+                words = coded.tile([P, n], U32, name="g_words", align_bytes=64)
+            else:
+                words = arena.tile([P, n], U32, name="late_words", offset=at, align_bytes=64)
             scales = coded.tile([P, n], U8, name="g_scales", align_bytes=64)
             nc.vector.quantize_mx(
                 out=words[:].bitcast(E5M2),
                 scales=scales[:],
                 in_=gb[:].rearrange("p c t -> p (c t)"),
             )
-            return words, scales
+            for j in range(n // P):
+                codes[slot0 // P + j, s] = (words, scales, j * P)
 
-        def multiply2(e, s, qs=range(QT)):
-            words, scales, base = codes[e, s]
-            for q in qs:
-                if s == 0:
-                    dh_banks[e, q] = dh_psum.tile([P, H], F32, name="dh")
-                cols = slice(base + q * P, base + (q + 1) * P)
-                nc.tensor.matmul_mx(
-                    out=dh_banks[e, q][:],
-                    lhsT=words[:, cols].bitcast(E5M2),
-                    lhsT_scale=scales[:, cols],
-                    rhs=w2_sb[e][:, s * 1024 : (s + 1) * 1024].bitcast(E2M1),
-                    rhs_scale=w2_sc[:, (e * PASSES + s) * H : (e * PASSES + s + 1) * H],
-                    start=(s == 0),
-                    stop=(s == PASSES - 1),
-                )
-
-        def slope(e):
-            slopes[e] = slope_pool.tile([P, QT, PACK, P], F32, name="slope")
-            for q in range(QT):
-                bank = tr_psum.tile([P, PACK, P], F32, name="turned")
-                for t in range(PACK):
-                    nc.tensor.transpose(bank[:, t, :], a_sb[e][:, t, q * P : (q + 1) * P], ident[:])
-                nc.scalar.activation(slopes[e][:, q, :, :], bank[:], RELU, scale=2.0)
-
-        by_slot = {}
-
-        def make_da(e):
-            da_parts[e] = (
-                last_da.tile([P, C, PACK], BF16, name="da", align_bytes=64),
-                da_codes_pool.tile([P, C], U32, name="da_words", align_bytes=64),
-                da_codes_pool.tile([P, C], U8, name="da_scales", align_bytes=64),
-                0,
+        def multiply2(block, s, b=None):
+            e = block // QT
+            words, scales, base = codes[block, s]
+            if s == 0:
+                dh[block] = bank(b)
+            cols = slice(base, base + P)
+            nc.tensor.matmul_mx(
+                out=dh[block][:],
+                lhsT=words[:, cols].bitcast(E5M2),
+                lhsT_scale=scales[:, cols],
+                rhs=w2_sb[e][:, s * 1024 : (s + 1) * 1024].bitcast(E2M1),
+                rhs_scale=w2_sc[:, (e * PASSES + s) * H : (e * PASSES + s + 1) * H],
+                start=(s == 0),
+                stop=(s == PASSES - 1),
             )
 
-        def times(e, q):
-            if e == 2 and q >= 2:
-                by_slot[e, q] = grouped.tile([P, PACK, P], BF16, name="gb", align_bytes=64)
+        def slope(e):
+            slopes[e] = arena.tile(
+                [P, QT, H], F32, name=f"slope{e}", offset=SLOPE_AT + e * SLOPE_BYTES, align_bytes=64
+            )
+            for q in range(QT):
+                turned = bank(4 + q)
+                for t in range(PACK):
+                    nc.tensor.transpose(
+                        turned[:, t * P : (t + 1) * P], a_sb[e][:, t, q * P : (q + 1) * P], ident[:]
+                    )
+                nc.scalar.activation(
+                    slopes[e][:, q, :].rearrange("p (u m d) -> p u m d", u=2, d=2),
+                    turned[:].rearrange("p (u d m) -> p u m d", u=2, d=2),
+                    RELU,
+                    scale=2.0,
+                )
+
+        def times(block):
+            if block < QT:
+                by_slot[block] = first_products[:, block * H : (block + 1) * H]
             else:
-                by_slot[e, q] = hidden.tile([P, PACK, P], BF16, name="by_slot")
+                by_slot[block] = hidden.tile([P, H], BF16, name="by_slot")[:]
             nc.vector.tensor_tensor(
-                by_slot[e, q][:],
-                dh_banks[e, q][:].rearrange("p (m t) -> p t m", t=PACK),
-                slopes[e][:, q, :, :],
+                by_slot[block].rearrange("p (u m d) -> p u m d", u=2, d=2),
+                dh[block][:].rearrange("p (m u d) -> p u m d", u=2, d=2),
+                slopes[block // QT][:, block % QT, :].rearrange("p (u m d) -> p u m d", u=2, d=2),
                 MULT,
             )
 
-        def turn(e, q, copy):
-            if e not in da_parts:
-                make_da(e)
-            bank = tr_psum.tile([P, PACK, P], BF16, name="turned")
-            for t in range(PACK):
-                nc.tensor.transpose(bank[:, t, :], by_slot[e, q][:, t, :], ident_bf[:])
-            copy(da_parts[e][0][:, q * P : (q + 1) * P, :], bank[:].rearrange("p t c -> p c t"))
-
-        def quantise_da(e, c0, c1):
-            da, words, scales, base = da_parts[e]
-            nc.vector.quantize_mx(
-                out=words[:, c0:c1].bitcast(E5M2),
-                scales=scales[:, c0:c1],
-                in_=da[:, c0:c1, :].rearrange("p c t -> p (c t)"),
+        def turn(blocks, b, da, lo):
+            turned = bank(b)
+            for j, block in enumerate(blocks):
+                pairs = by_slot[block].bitcast(F32)
+                for u in range(2):
+                    nc.tensor.transpose(
+                        turned[:, (2 * j + u) * P : (2 * j + u + 1) * P], pairs[:, u * P : (u + 1) * P], ident[:]
+                    )
+            n = len(blocks) * P
+            nc.scalar.copy(
+                da[:].bitcast(F32)[:, 2 * lo : 2 * (lo + n)].rearrange("p (j c u) -> p j c u", c=P, u=2),
+                turned[:, 0 : 2 * n].rearrange("p (j u c) -> p j c u", c=P, u=2),
             )
 
-        def multiply1(e):
-            da, words, scales, base = da_parts[e]
-            dx = tr_psum.tile([P, C], F32, name="turned")
+        def da_tile(n):
+            return da_pool.tile([P, n * PACK], BF16, name="da", align_bytes=64)
+
+        def quantise_da(da, words, scales, lo, n):
+            nc.vector.quantize_mx(
+                out=words[:, lo : lo + n].bitcast(E5M2), scales=scales[:, lo : lo + n], in_=da[:]
+            )
+
+        def multiply1(e, b, words, scales, lo):
+            dx = bank(b)
             nc.tensor.matmul_mx(
                 out=dx[:],
                 lhsT=w1_sb[:, e * 256 : (e + 1) * 256].bitcast(E2M1),
                 lhsT_scale=w1_sc[:, e * K : (e + 1) * K],
-                rhs=words[:, base : base + C].bitcast(E5M2),
-                rhs_scale=scales[:, base : base + C],
+                rhs=words[:, lo : lo + C].bitcast(E5M2),
+                rhs_scale=scales[:, lo : lo + C],
                 start=True,
                 stop=True,
             )
-            nc.scalar.activation(dx_sb[:, e * C : (e + 1) * C], dx[:], COPY)
+            return dx
 
-        def finish(e):
-            quantise_da(e, 0, C)
-            multiply1(e)
-
-        def pair_gathers(pair, s, g32, ts):
-            for t in ts:
-                if pair == 0 and s == 0 and t == 0:
-                    gather(g32, s, t, 0, C)
-                    gather(g32, s, t, C, C)
-                else:
-                    gather(g32, s, t, pair * PAIR, PAIR)
-
-        def pair_tile():
-            return gathered.tile([P, PACK, PAIR], F32, name="g32")
-
-        def pair_codes(gb, pair, s):
-            words, scales = quantise(gb, PAIR)
-            for x in range(2):
-                codes[2 * pair + x, s] = (words, scales, x * C)
-
-        def interleave_half(g32):
-            gb = grouped.tile([P, C, PACK], BF16, name="gb", align_bytes=64)
-            nc.scalar.activation(
-                gb[:].rearrange("p (c i) t -> p c t i", i=4),
-                g32[:].rearrange("p t (c i) -> p c t i", i=4),
-                COPY,
-            )
-            return gb
-
-        g = pair_tile()
-        pair_gathers(0, 0, g, range(4))
-        b = interleave(g, PAIR)
+        gb_a0 = interleave(gathers(0, 0, 0), 0, PAIR)
+        gb_a1 = interleave(gathers(1, 0, G32_BYTES), 0, PAIR)
         slope(0)
-        load_a(2)
-        load_scales()
-        load_w2(0)
-        load_w2(1)
+        slope(1)
+        load_scales(w1_sc, w1_scales, E)
         nc.sync.dma_start(
             out=w1_sb[:].bitcast(I32).rearrange("p (e w) -> p e w", e=E),
             in_=w1_words.bitcast(I32).rearrange("e s p w -> p (e s) w"),
         )
-        load_w2(2)
-        load_w2(3)
         nc.sync.dma_start(pos1_sb[:], pos1)
         nc.sync.dma_start(pos2_sb[:], pos2)
-        for s in (1, 2):
-            g = pair_tile()
-            pair_gathers(0, s, g, range(3))
-            pair_codes(b, 0, s - 1)
-            multiply2(0, s - 1)
-            pair_gathers(0, s, g, range(3, 4))
-            b = interleave(g, PAIR)
-            slope(s)
-            if s == 1:
-                load_a(3)
-        def single(e, s):
-            g1 = gathered.tile([P, PACK, C], F32, name="g32")
-            for t in range(4):
-                gather(g1, s, t, e * C, C)
-            return g1
-
-        def single_codes(e, s, gb):
-            codes[e, s] = quantise(gb, C) + (0,)
-
-        g = pair_tile()
-        pair_gathers(1, 0, g, range(4))
-        b_next = interleave(g, PAIR)
-        pair_codes(b, 0, 2)
-        b = b_next
-        multiply2(0, 2)
-        for q in range(QT):
-            times(0, q)
-        for q in range(QT):
-            for s in range(PASSES):
-                multiply2(1, s, (q,))
-            turn(0, q, nc.scalar.copy)
+        quantise(gb_a0, 0, 0, PAIR)
+        gb_a2 = interleave(gathers(2, 0, 0), 0, PAIR, 1)
+        quantise(gb_a1, 1, 0, PAIR)
+        for s in range(2):
+            for block in range(QT):
+                multiply2(block, s, block)
+        slope(2)
         slope(3)
-        g = single(2, 1)
-        b21 = interleave_half(g)
-        for q in range(QT):
-            times(1, q)
-        pair_codes(b, 1, 0)
-        multiply2(2, 0)
-        for q in range(QT):
-            turn(1, q, nc.scalar.copy)
-        quantise_da(0, 0, C)
-        multiply1(0)
-        g = single(2, 2)
-        b22 = interleave_half(g)
-        single_codes(2, 1, b21)
-        multiply2(2, 1)
-        quantise_da(1, 0, C)
-        multiply1(1)
-        g = single(3, 1)
-        single_codes(2, 2, b22)
-        multiply2(2, 2)
-        b31 = interleave_half(g)
-        for q in range(2):
-            times(2, q)
-            turn(2, q, nc.scalar.copy)
-        multiply2(3, 0, range(2))
+        dx_sb = keep.tile([P, SLOTS], F32, name="a0", align_bytes=64)
+        da_words = grouped.tile([P, 3 * C], U32, name="gb", align_bytes=64)
+        for s in range(2):
+            for block in range(QT, 2 * QT):
+                multiply2(block, s, block)
+        gb_b0 = interleave(gathers(0, 1, G32_BYTES), 0, PAIR, 2)
+        quantise(gb_a2, 2, 0, PAIR)
+        for block in range(2 * QT):
+            multiply2(block, 2)
+        gb_b1 = interleave(gathers(1, 1, 0), 0, PAIR, 3)
+        quantise(gb_b0, 0, PAIR, PAIR)
+
         HALF = C // 2
-        b32 = [
-            grouped.tile([P, HALF, PACK], BF16, name="gb", align_bytes=64),
-            hidden.tile([P, HALF, PACK], BF16, name="b32_late", align_bytes=64),
-        ]
-        words32 = coded.tile([P, C], U32, name="g_words", align_bytes=64)
-        scales32 = coded.tile([P, C], U8, name="g_scales", align_bytes=64)
-        codes[3, 2] = (words32, scales32, 0)
+        first_products = keep.tile([P, QT * H], BF16, name="a2", align_bytes=64)
+        for block in range(0, 4):
+            times(block)
+        da0 = da_tile(C)
+        turn((0, 1), 0, da0, 0)
+        turn((2, 3), 1, da0, HALF)
+        for block, b in ((8, 2), (9, 3), (10, 0), (11, 1)):
+            multiply2(block, 0, b)
+        g_last = g32_tile(2, 1, G32_BYTES + 64)
+        for t in range(PACK):
+            gather(g_last, 2, t, PAIR, 0, PAIR)
+            if t == 1:
+                quantise(gb_b1, 1, PAIR, PAIR, SLOPE_AT + 64)
+                for block in range(8, 12):
+                    multiply2(block, 1)
+        gb_2 = interleave(g_last, 0, C)
+        gb_3 = interleave(g_last, C, C, 1)
+        for block in range(4, 8):
+            times(block)
+        da1 = da_tile(C)
+        turn((4, 5), 4, da1, 0)
+        turn((6, 7), 5, da1, HALF)
+        quantise(gb_2, 2, 2 * C, C)
+        for block in range(8, 12):
+            multiply2(block, 2)
+        for block, b in ((12, 6), (13, 7), (14, 4), (15, 5)):
+            multiply2(block, 0, b)
+            multiply2(block, 1)
+        quantise_da(da0, da_words, da_scales, 0, C)
+        da2 = da_tile(C)
+        times(8)
+        times(9)
+        turn((8, 9), 2, da2, 0)
+        quantise(gb_3, 2, 3 * C, C)
+        for block in range(12, 16):
+            multiply2(block, 2)
+        nc.scalar.copy(dx_sb[:, 0:C], multiply1(0, 3, da_words, da_scales, 0)[:])
+        times(10)
+        times(11)
+        turn((10, 11), 0, da2, HALF)
+        quantise_da(da1, da_words, da_scales, C, C)
+        nc.scalar.copy(dx_sb[:, C : 2 * C], multiply1(1, 1, da_words, da_scales, C)[:])
+        times(12)
+        times(13)
+        da3a = da_tile(HALF)
+        turn((12, 13), 6, da3a, 0)
+        times(14)
+        da3b = hidden.tile([P, P * PACK], BF16, name="da_block", align_bytes=64)
+        turn((14,), 7, da3b, 0)
+        times(15)
+        da3c = hidden.tile([P, P * PACK], BF16, name="da_block", align_bytes=64)
+        turn((15,), 4, da3c, 0)
+        late_words = arena.tile([P, C], U32, name="da2_words", offset=SLOPE_AT + 3 * SLOPE_BYTES, align_bytes=64)
+        late_scales = arena.tile(
+            [P, C], U8, name="da2_scales", offset=SLOPE_AT + 3 * SLOPE_BYTES + 4 * C, align_bytes=64
+        )
+        quantise_da(da2, late_words, late_scales, 0, C)
+        nc.scalar.copy(dx_sb[:, 2 * C : 3 * C], multiply1(2, 2, late_words, late_scales, 0)[:])
+        quantise_da(da3a, da_words, da_scales, 2 * C, HALF)
+        quantise_da(da3b, da_words, da_scales, 2 * C + HALF, P)
+        most = multiply1(3, 3, da_words, da_scales, 2 * C - P)
+        quantise_da(da3c, da_words, da_scales, 3 * C - P, P)
+        rest = multiply1(3, 0, da_words, da_scales, 2 * C)
+        nc.vector.tensor_copy(dx_sb[:, 3 * C : SLOTS - P], most[:, P:C])
+        nc.scalar.copy(dx_sb[:, SLOTS - P : SLOTS], rest[:, C - P : C])
 
-        def last_gather(h):
-            if h == 0:
-                g1 = gathered.tile([P, PACK, HALF], F32, name="g32")
-            else:
-                g1 = grouped.tile([P, PACK, HALF], F32, name="gb", align_bytes=64)
-            for t in range(4):
-                gather(g1, 2, t, 3 * C + h * HALF, HALF)
-            return g1
+        first = arena.tile([P, T], F32, name="first", offset=0, align_bytes=64)
+        total = arena.tile([P, T], F32, name="total", offset=4 * T, align_bytes=64)
+        cuts = (0, 512, 896, T)
 
-        def last_interleave(g1, h):
-            nc.scalar.activation(
-                b32[h][:].rearrange("p (c i) t -> p c t i", i=4),
-                g1[:].rearrange("p t (c i) -> p c t i", i=4),
-                COPY,
+        def fetch_second(i):
+            lo, hi = cuts[i], cuts[i + 1]
+            nc.vector.tensor_tensor(
+                total[:, lo:hi], dx_sb[:].indirect(pos2_sb[:, lo // 16 : hi // 16]), first[:, lo:hi], ADD
             )
+            nc.sync.dma_start(out=out[:, lo:hi], in_=total[:, lo:hi])
 
-        def last_quantise(h):
-            cols = slice(h * HALF, (h + 1) * HALF)
-            nc.vector.quantize_mx(
-                out=words32[:, cols].bitcast(E5M2),
-                scales=scales32[:, cols],
-                in_=b32[h][:].rearrange("p c t -> p (c t)"),
-            )
-
-        g = last_gather(0)
-        last_interleave(g, 0)
-        single_codes(3, 1, b31)
-        multiply2(3, 1, range(2))
-        g = last_gather(1)
-        last_quantise(0)
-        multiply2(3, 2, range(2))
-        last_interleave(g, 1)
-        times(2, 2)
-        turn(2, 2, nc.scalar.copy)
-        for q in range(2):
-            times(3, q)
-            turn(3, q, nc.scalar.copy)
-        multiply2(3, 0, (2,))
-        multiply2(3, 1, (2,))
-        last_quantise(1)
-        multiply2(3, 2, (2,))
-        times(2, 3)
-        turn(2, 3, nc.scalar.copy)
-        multiply2(3, 0, (3,))
-        multiply2(3, 1, (3,))
-        multiply2(3, 2, (3,))
-        times(3, 2)
-        turn(3, 2, nc.vector.tensor_copy)
-        times(3, 3)
-        quantise_da(2, 0, C)
-        multiply1(2)
-        turn(3, 3, nc.vector.tensor_copy)
-        quantise_da(3, 0, C // 2)
-        quantise_da(3, C // 2, C)
-        multiply1(3)
-
-        first = slope_pool.tile([P, T], F32, name="slope")
-        second = slope_pool.tile([P, T], F32, name="slope")
-        total = slope_pool.tile([P, T], F32, name="slope")
         nc.vector.tensor_copy(first[:], dx_sb[:].indirect(pos1_sb[:]))
-        lo = 0
-        for width, adder in ((640, nc.gpsimd), (384, nc.vector)):
-            cols = slice(lo, lo + width)
-            nc.vector.tensor_copy(
-                second[:, cols], dx_sb[:].indirect(pos2_sb[:, lo // 16 : (lo + width) // 16])
-            )
-            adder.tensor_tensor(total[:, cols], first[:, cols], second[:, cols], ADD)
-            nc.sync.dma_start(out=out[:, cols], in_=total[:, cols])
-            lo += width
+        for i in range(3):
+            fetch_second(i)

@@ -46,8 +46,11 @@ def tile_moe_bdx_mlp_relu2_kernel(
         psum = ctx.enter_context(tc.psum_pool(name="psum", bufs=1))
 
         G32_BYTES = 4 * PACK * PAIR
-        SLOPE_BYTES = 4 * QT * H
-        SLOPE_AT = 2 * G32_BYTES
+        SLOPE_BYTES = 4 * H
+        G32_AT = (SLOPE_BYTES, 2 * SLOPE_BYTES + G32_BYTES)
+        slope_at = {1: 0, 0: G32_AT[0] + G32_BYTES}
+        for block in range(2, E * QT):
+            slope_at[block] = G32_AT[1] + G32_BYTES + (block - 2) * SLOPE_BYTES
 
         def bank(b):
             return psum.tile([P, 512], F32, name=f"bank{b}")
@@ -193,17 +196,18 @@ def tile_moe_bdx_mlp_relu2_kernel(
             )
 
         def slope(e):
-            slopes[e] = arena.tile(
-                [P, QT, H], F32, name=f"slope{e}", offset=SLOPE_AT + e * SLOPE_BYTES, align_bytes=64
-            )
             for q in range(QT):
+                block = e * QT + q
+                slopes[block] = arena.tile(
+                    [P, H], F32, name=f"slope{block}", offset=slope_at[block], align_bytes=64
+                )
                 turned = bank(4 + q)
                 for t in range(PACK):
                     nc.tensor.transpose(
                         turned[:, t * P : (t + 1) * P], a_sb[e][:, t, q * P : (q + 1) * P], ident[:]
                     )
                 nc.scalar.activation(
-                    slopes[e][:, q, :].rearrange("p (u m d) -> p u m d", u=2, d=2),
+                    slopes[block][:].rearrange("p (u m d) -> p u m d", u=2, d=2),
                     turned[:].rearrange("p (u d m) -> p u m d", u=2, d=2),
                     RELU,
                     scale=2.0,
@@ -217,7 +221,7 @@ def tile_moe_bdx_mlp_relu2_kernel(
             nc.vector.tensor_tensor(
                 by_slot[block].rearrange("p (u m d) -> p u m d", u=2, d=2),
                 dh[block][:].rearrange("p (m u d) -> p u m d", u=2, d=2),
-                slopes[block // QT][:, block % QT, :].rearrange("p (u m d) -> p u m d", u=2, d=2),
+                slopes[block][:].rearrange("p (u m d) -> p u m d", u=2, d=2),
                 MULT,
             )
 
@@ -256,8 +260,8 @@ def tile_moe_bdx_mlp_relu2_kernel(
             )
             return dx
 
-        gb_a0 = interleave(gathers(0, 0, 0), 0, PAIR)
-        gb_a1 = interleave(gathers(1, 0, G32_BYTES), 0, PAIR)
+        gb_a0 = interleave(gathers(0, 0, G32_AT[0]), 0, PAIR)
+        gb_a1 = interleave(gathers(1, 0, G32_AT[1]), 0, PAIR)
         slope(0)
         slope(1)
         load_scales(w1_sc, w1_scales, E)
@@ -268,7 +272,7 @@ def tile_moe_bdx_mlp_relu2_kernel(
         nc.sync.dma_start(pos1_sb[:], pos1)
         nc.sync.dma_start(pos2_sb[:], pos2)
         quantise(gb_a0, 0, 0, PAIR)
-        gb_a2 = interleave(gathers(2, 0, 0), 0, PAIR, 1)
+        gb_a2 = interleave(gathers(2, 0, G32_AT[0]), 0, PAIR, 1)
         quantise(gb_a1, 1, 0, PAIR)
         for s in range(2):
             for block in range(QT):
@@ -276,19 +280,19 @@ def tile_moe_bdx_mlp_relu2_kernel(
         slope(2)
         slope(3)
         dx_sb = keep.tile([P, SLOTS], F32, name="a0", align_bytes=64)
-        da_words = grouped.tile([P, 3 * C], U32, name="gb", align_bytes=64)
         for s in range(2):
             for block in range(QT, 2 * QT):
                 multiply2(block, s, block)
-        gb_b0 = interleave(gathers(0, 1, G32_BYTES), 0, PAIR, 2)
+        gb_b0 = interleave(gathers(0, 1, G32_AT[1]), 0, PAIR, 2)
         quantise(gb_a2, 2, 0, PAIR)
         for block in range(2 * QT):
             multiply2(block, 2)
-        gb_b1 = interleave(gathers(1, 1, 0), 0, PAIR, 3)
+        gb_b1 = interleave(gathers(1, 1, G32_AT[0]), 0, PAIR, 3)
         quantise(gb_b0, 0, PAIR, PAIR)
 
         HALF = C // 2
-        first_products = keep.tile([P, QT * H], BF16, name="a2", align_bytes=64)
+        da_words = arena.tile([P, 3 * C], U32, name="da_words", offset=G32_AT[0] + 4 * PAIR, align_bytes=64)
+        first_products = arena.tile([P, QT * H], BF16, name="products0", offset=G32_AT[1], align_bytes=64)
         for block in range(0, 4):
             times(block)
         da0 = da_tile(C)
@@ -296,34 +300,49 @@ def tile_moe_bdx_mlp_relu2_kernel(
         turn((2, 3), 1, da0, HALF)
         for block, b in ((8, 2), (9, 3), (10, 0), (11, 1)):
             multiply2(block, 0, b)
-        g_last = g32_tile(2, 1, G32_BYTES + 64)
-        for t in range(PACK):
-            gather(g_last, 2, t, PAIR, 0, PAIR)
-            if t == 1:
-                quantise(gb_b1, 1, PAIR, PAIR, SLOPE_AT + 64)
-                for block in range(8, 12):
-                    multiply2(block, 1)
-        gb_2 = interleave(g_last, 0, C)
-        gb_3 = interleave(g_last, C, C, 1)
-        for block in range(4, 8):
-            times(block)
+        def last_gathers(g32, slot0, n):
+            for t in range(PACK):
+                gather(g32, 2, t, slot0, 0, n)
+            return interleave(g32, 0, n)
+
+        g_2 = arena.tile([P, PACK, C], F32, name="g32_2", offset=slope_at[2] + 64 - 4 * PACK * C, align_bytes=64)
+        gb_2 = last_gathers(g_2, 2 * C, C)
+        quantise(gb_b1, 1, PAIR, PAIR, G32_AT[0] - 64)
+        for block in range(8, 12):
+            multiply2(block, 1)
+        g_3a = arena.tile(
+            [P, PACK, HALF], F32, name="g32_3a", offset=slope_at[0] + 64 - 4 * PACK * HALF, align_bytes=64
+        )
+        gb_3a = last_gathers(g_3a, 3 * C, HALF)
+        times(4)
+        times(5)
         da1 = da_tile(C)
         turn((4, 5), 4, da1, 0)
-        turn((6, 7), 5, da1, HALF)
         quantise(gb_2, 2, 2 * C, C)
         for block in range(8, 12):
             multiply2(block, 2)
-        for block, b in ((12, 6), (13, 7), (14, 4), (15, 5)):
+        for block, b in ((12, 5), (13, 4)):
+            multiply2(block, 0, b)
+            multiply2(block, 1)
+        g_3b = arena.tile([P, PACK, HALF], F32, name="g32_3b", offset=slope_at[4], align_bytes=64)
+        gb_3b = last_gathers(g_3b, 3 * C + HALF, HALF)
+        quantise(gb_3a, 2, 3 * C, HALF)
+        multiply2(12, 2)
+        multiply2(13, 2)
+        times(6)
+        times(7)
+        turn((6, 7), 6, da1, HALF)
+        for block, b in ((14, 7), (15, 6)):
             multiply2(block, 0, b)
             multiply2(block, 1)
         quantise_da(da0, da_words, da_scales, 0, C)
+        quantise(gb_3b, 2, 3 * C + HALF, HALF)
+        multiply2(14, 2)
+        multiply2(15, 2)
         da2 = da_tile(C)
         times(8)
         times(9)
         turn((8, 9), 2, da2, 0)
-        quantise(gb_3, 2, 3 * C, C)
-        for block in range(12, 16):
-            multiply2(block, 2)
         nc.scalar.copy(dx_sb[:, 0:C], multiply1(0, 3, da_words, da_scales, 0)[:])
         times(10)
         times(11)
@@ -333,16 +352,16 @@ def tile_moe_bdx_mlp_relu2_kernel(
         times(12)
         times(13)
         da3a = da_tile(HALF)
-        turn((12, 13), 6, da3a, 0)
+        turn((12, 13), 5, da3a, 0)
         times(14)
         da3b = hidden.tile([P, P * PACK], BF16, name="da_block", align_bytes=64)
-        turn((14,), 7, da3b, 0)
+        turn((14,), 4, da3b, 0)
         times(15)
         da3c = hidden.tile([P, P * PACK], BF16, name="da_block", align_bytes=64)
-        turn((15,), 4, da3c, 0)
-        late_words = arena.tile([P, C], U32, name="da2_words", offset=SLOPE_AT + 3 * SLOPE_BYTES, align_bytes=64)
+        turn((15,), 7, da3c, 0)
+        late_words = arena.tile([P, C], U32, name="da2_words", offset=slope_at[14], align_bytes=64)
         late_scales = arena.tile(
-            [P, C], U8, name="da2_scales", offset=SLOPE_AT + 3 * SLOPE_BYTES + 4 * C, align_bytes=64
+            [P, C], U8, name="da2_scales", offset=slope_at[13], align_bytes=64
         )
         quantise_da(da2, late_words, late_scales, 0, C)
         nc.scalar.copy(dx_sb[:, 2 * C : 3 * C], multiply1(2, 2, late_words, late_scales, 0)[:])
@@ -354,8 +373,8 @@ def tile_moe_bdx_mlp_relu2_kernel(
         nc.vector.tensor_copy(dx_sb[:, 3 * C : SLOTS - P], most[:, P:C])
         nc.scalar.copy(dx_sb[:, SLOTS - P : SLOTS], rest[:, C - P : C])
 
-        first = arena.tile([P, T], F32, name="first", offset=0, align_bytes=64)
-        total = arena.tile([P, T], F32, name="total", offset=4 * T, align_bytes=64)
+        first = arena.tile([P, T], F32, name="first", offset=slope_at[6], align_bytes=64)
+        total = arena.tile([P, T], F32, name="total", offset=slope_at[8], align_bytes=64)
         cuts = (0, 512, 896, T)
 
         def fetch_second(i):

@@ -47,10 +47,10 @@ def tile_moe_bdx_mlp_relu2_kernel(
 
         G32_BYTES = 4 * PACK * PAIR
         SLOPE_BYTES = 4 * H
-        G32_AT = (SLOPE_BYTES, 2 * SLOPE_BYTES + G32_BYTES)
-        slope_at = {1: 0, 0: G32_AT[0] + G32_BYTES}
-        for block in range(2, E * QT):
-            slope_at[block] = G32_AT[1] + G32_BYTES + (block - 2) * SLOPE_BYTES
+        G32_AT = (SLOPE_BYTES, SLOPE_BYTES + G32_BYTES)
+        slope_at = {0: 0}
+        for block in range(1, E * QT):
+            slope_at[block] = G32_AT[1] + G32_BYTES + (block - 1) * SLOPE_BYTES
 
         def bank(b):
             return psum.tile([P, 512], F32, name=f"bank{b}")
@@ -67,7 +67,7 @@ def tile_moe_bdx_mlp_relu2_kernel(
         w1_sb = keep.tile([P, E * 256], U8, name="w1_sb", align_bytes=64)
         w1_sc = keep.tile([P, E * K], U8, name="w1_sc", align_bytes=64)
         ident = keep.tile([P, P], F32, name="ident")
-        da_scales = keep.tile([P, 3 * C], U8, name="da_scales", align_bytes=64)
+        da_scales = keep.tile([P, 2 * C], U8, name="da_scales", align_bytes=64)
 
         for s in range(PASSES):
             for t in range(PACK):
@@ -129,6 +129,7 @@ def tile_moe_bdx_mlp_relu2_kernel(
         dh = {}
         slopes = {}
         by_slot = {}
+        parked = {}
 
         def gather(g32, s, t, slot0, lo, n):
             first = slot0 + lo
@@ -213,17 +214,25 @@ def tile_moe_bdx_mlp_relu2_kernel(
                     scale=2.0,
                 )
 
-        def times(block):
-            if block < QT:
-                by_slot[block] = first_products[:, block * H : (block + 1) * H]
-            else:
-                by_slot[block] = hidden.tile([P, H], BF16, name="by_slot")[:]
-            nc.vector.tensor_tensor(
-                by_slot[block].rearrange("p (u m d) -> p u m d", u=2, d=2),
-                dh[block][:].rearrange("p (m u d) -> p u m d", u=2, d=2),
-                slopes[block][:].rearrange("p (u m d) -> p u m d", u=2, d=2),
-                MULT,
-            )
+        def paired(ap):
+            return ap.rearrange("p (u m d) -> p u m d", u=2, d=2)
+
+        def dh_paired(block):
+            return dh[block][:].rearrange("p (m u d) -> p u m d", u=2, d=2)
+
+        def times(block, dest=None):
+            if dest is None:
+                dest = hidden.tile([P, H], BF16, name="by_slot")[:]
+            by_slot[block] = dest
+            nc.vector.tensor_tensor(paired(dest), dh_paired(block), paired(slopes[block][:]), MULT)
+
+        def park(block, dest):
+            nc.scalar.copy(paired(dest), dh_paired(block))
+            parked[block] = dest
+
+        def times_parked(block, dest):
+            by_slot[block] = dest
+            nc.gpsimd.tensor_tensor(dest, parked[block], slopes[block][:], MULT)
 
         def turn(blocks, b, da, lo):
             turned = bank(b)
@@ -278,98 +287,118 @@ def tile_moe_bdx_mlp_relu2_kernel(
             for block in range(QT):
                 multiply2(block, s, block)
         slope(2)
-        slope(3)
         dx_sb = keep.tile([P, SLOTS], F32, name="a0", align_bytes=64)
-        for s in range(2):
-            for block in range(QT, 2 * QT):
-                multiply2(block, s, block)
         gb_b0 = interleave(gathers(0, 1, G32_AT[1]), 0, PAIR, 2)
         quantise(gb_a2, 2, 0, PAIR)
-        for block in range(2 * QT):
+        parked01 = keep.tile([P, 2 * H], F32, name="a1", align_bytes=64)
+        for block in reversed(range(QT)):
             multiply2(block, 2)
+        park(3, parked01[:, 0:H])
+        slope(3)
+        for block in range(QT, 2 * QT):
+            for s in range(PASSES):
+                multiply2(block, s, block)
+        park(7, parked01[:, H : 2 * H])
         gb_b1 = interleave(gathers(1, 1, G32_AT[0]), 0, PAIR, 3)
         quantise(gb_b0, 0, PAIR, PAIR)
 
         HALF = C // 2
-        da_words = arena.tile([P, 3 * C], U32, name="da_words", offset=G32_AT[0] + 4 * PAIR, align_bytes=64)
-        first_products = arena.tile([P, QT * H], BF16, name="products0", offset=G32_AT[1], align_bytes=64)
-        for block in range(0, 4):
-            times(block)
+        da_words = arena.tile([P, 2 * C], U32, name="da_words", offset=G32_AT[0] + 4 * PAIR, align_bytes=64)
+        first_products = arena.tile([P, 3 * H], BF16, name="products0", offset=G32_AT[1], align_bytes=64)
+        product3 = keep.tile([P, H], BF16, name="dy1_3")
+        times_parked(3, product3[:])
+        for block in range(3):
+            times(block, first_products[:, block * H : (block + 1) * H])
         da0 = da_tile(C)
         turn((0, 1), 0, da0, 0)
         turn((2, 3), 1, da0, HALF)
-        for block, b in ((8, 2), (9, 3), (10, 0), (11, 1)):
+        for block, b in ((8, 3), (9, 2), (10, 0), (11, 1)):
             multiply2(block, 0, b)
+
         def last_gathers(g32, slot0, n):
             for t in range(PACK):
                 gather(g32, 2, t, slot0, 0, n)
             return interleave(g32, 0, n)
 
-        g_2 = arena.tile([P, PACK, C], F32, name="g32_2", offset=slope_at[2] + 64 - 4 * PACK * C, align_bytes=64)
+        g_2 = arena.tile([P, PACK, C], F32, name="g32_2", offset=slope_at[1] + 64 - 4 * PACK * C, align_bytes=64)
         gb_2 = last_gathers(g_2, 2 * C, C)
         quantise(gb_b1, 1, PAIR, PAIR, G32_AT[0] - 64)
         for block in range(8, 12):
             multiply2(block, 1)
+        multiply2(12, 0, 7)
+        multiply2(12, 1)
         g_3a = arena.tile(
-            [P, PACK, HALF], F32, name="g32_3a", offset=slope_at[0] + 64 - 4 * PACK * HALF, align_bytes=64
+            [P, PACK, HALF], F32, name="g32_3a", offset=G32_AT[0] + G32_BYTES - 4 * PACK * HALF, align_bytes=64
         )
         gb_3a = last_gathers(g_3a, 3 * C, HALF)
-        times(4)
-        times(5)
-        da1 = da_tile(C)
-        turn((4, 5), 4, da1, 0)
         quantise(gb_2, 2, 2 * C, C)
-        for block in range(8, 12):
+        for block in (11, 8, 9, 10):
             multiply2(block, 2)
-        for block, b in ((12, 5), (13, 4)):
-            multiply2(block, 0, b)
-            multiply2(block, 1)
-        g_3b = arena.tile([P, PACK, HALF], F32, name="g32_3b", offset=slope_at[4], align_bytes=64)
-        gb_3b = last_gathers(g_3b, 3 * C + HALF, HALF)
+        parked23 = keep.tile([P, 2 * H], F32, name="a3", align_bytes=64)
+        park(11, parked23[:, 0:H])
+        multiply2(13, 0, 1)
+        multiply2(13, 1)
+        g_3b = arena.tile([P, PACK, HALF], F32, name="g32_3b", offset=slope_at[1] - 4 * PACK * HALF, align_bytes=64)
+        for t in range(PACK):
+            gather(g_3b, 2, t, 3 * C + HALF, 0, HALF)
+        gb_3b = interleave(g_3b, 0, HALF, 2)
         quantise(gb_3a, 2, 3 * C, HALF)
         multiply2(12, 2)
         multiply2(13, 2)
-        times(6)
-        times(7)
+        park(12, parked23[:, H : 2 * H])
+        product7 = keep.tile([P, H], BF16, name="dy2_3")
+        times_parked(7, product7[:])
+        second_products = keep.tile([P, 3 * H], BF16, name="dy2_2")
+        for block in range(4, 7):
+            times(block, second_products[:, (block - 4) * H : (block - 3) * H])
+        da1 = da_tile(C)
+        turn((4, 5), 4, da1, 0)
+        multiply2(14, 0, 5)
+        multiply2(14, 1)
         turn((6, 7), 6, da1, HALF)
-        for block, b in ((14, 7), (15, 6)):
-            multiply2(block, 0, b)
-            multiply2(block, 1)
+        multiply2(15, 0, 4)
+        multiply2(15, 1)
         quantise_da(da0, da_words, da_scales, 0, C)
         quantise(gb_3b, 2, 3 * C + HALF, HALF)
         multiply2(14, 2)
         multiply2(15, 2)
+        products = keep.tile([P, 2 * H], BF16, name="a2", align_bytes=64)
+        times_parked(11, products[:, 0:H])
+        times_parked(12, products[:, H : 2 * H])
+        nc.scalar.copy(dx_sb[:, 0:C], multiply1(0, 7, da_words, da_scales, 0)[:])
+
+        def late_codes(e, words_on, scales_on):
+            return (
+                arena.tile([P, C], U32, name=f"da{e}_words", offset=slope_at[words_on], align_bytes=64),
+                arena.tile([P, C], U8, name=f"da{e}_scales", offset=slope_at[scales_on], align_bytes=64),
+            )
+
         da2 = da_tile(C)
         times(8)
         times(9)
-        turn((8, 9), 2, da2, 0)
-        nc.scalar.copy(dx_sb[:, 0:C], multiply1(0, 3, da_words, da_scales, 0)[:])
+        turn((8, 9), 3, da2, 0)
         times(10)
-        times(11)
-        turn((10, 11), 0, da2, HALF)
-        quantise_da(da1, da_words, da_scales, C, C)
-        nc.scalar.copy(dx_sb[:, C : 2 * C], multiply1(1, 1, da_words, da_scales, C)[:])
-        times(12)
+        turn((10, 11), 2, da2, HALF)
         times(13)
-        da3a = da_tile(HALF)
-        turn((12, 13), 5, da3a, 0)
+        da3a = keep.tile([P, HALF * PACK], BF16, name="da3a", align_bytes=64)
+        turn((12, 13), 0, da3a, 0)
         times(14)
-        da3b = hidden.tile([P, P * PACK], BF16, name="da_block", align_bytes=64)
-        turn((14,), 4, da3b, 0)
+        da3b = keep.tile([P, P * PACK], BF16, name="da3b", align_bytes=64)
+        turn((14,), 1, da3b, 0)
+        words1, scales1 = late_codes(1, 13, 10)
+        quantise_da(da1, words1, scales1, 0, C)
+        nc.scalar.copy(dx_sb[:, C : 2 * C], multiply1(1, 6, words1, scales1, 0)[:])
         times(15)
-        da3c = hidden.tile([P, P * PACK], BF16, name="da_block", align_bytes=64)
-        turn((15,), 7, da3c, 0)
-        late_words = arena.tile([P, C], U32, name="da2_words", offset=slope_at[14], align_bytes=64)
-        late_scales = arena.tile(
-            [P, C], U8, name="da2_scales", offset=slope_at[13], align_bytes=64
-        )
-        quantise_da(da2, late_words, late_scales, 0, C)
-        nc.scalar.copy(dx_sb[:, 2 * C : 3 * C], multiply1(2, 2, late_words, late_scales, 0)[:])
-        quantise_da(da3a, da_words, da_scales, 2 * C, HALF)
-        quantise_da(da3b, da_words, da_scales, 2 * C + HALF, P)
-        most = multiply1(3, 3, da_words, da_scales, 2 * C - P)
-        quantise_da(da3c, da_words, da_scales, 3 * C - P, P)
-        rest = multiply1(3, 0, da_words, da_scales, 2 * C)
+        da3c = keep.tile([P, P * PACK], BF16, name="da3c", align_bytes=64)
+        turn((15,), 5, da3c, 0)
+        words2, scales2 = late_codes(2, 14, 9)
+        quantise_da(da2, words2, scales2, 0, C)
+        nc.scalar.copy(dx_sb[:, 2 * C : 3 * C], multiply1(2, 7, words2, scales2, 0)[:])
+        quantise_da(da3a, da_words, da_scales, C, HALF)
+        quantise_da(da3b, da_words, da_scales, C + HALF, P)
+        most = multiply1(3, 3, da_words, da_scales, C - P)
+        quantise_da(da3c, da_words, da_scales, 2 * C - P, P)
+        rest = multiply1(3, 0, da_words, da_scales, C)
         nc.vector.tensor_copy(dx_sb[:, 3 * C : SLOTS - P], most[:, P:C])
         nc.scalar.copy(dx_sb[:, SLOTS - P : SLOTS], rest[:, C - P : C])
 

@@ -72,8 +72,8 @@ def tile_moe_bdx_mlp_relu2_kernel(
         for s in range(PASSES):
             for t in range(PACK):
                 nc.vector.memset(planes[s][t][:, T : T + PAD], 0.0)
-        nc.gpsimd.memset(w2_sc[:].bitcast(I32), 0)
-        nc.gpsimd.memset(w1_sc[:].bitcast(I32), 0)
+        nc.vector.memset(w2_sc[:].bitcast(I32), 0)
+        nc.vector.memset(w1_sc[:].bitcast(I32), 0)
         make_identity(nc, ident[:])
 
         dy_rows = dyT.rearrange("(s p t) j -> s t p j", p=P, t=PACK)
@@ -154,8 +154,10 @@ def tile_moe_bdx_mlp_relu2_kernel(
                     gather(g32, s, t, pair * PAIR, 0, PAIR)
             return g32
 
-        def interleave(g32, lo, n, after_a=None):
-            if after_a is None:
+        def interleave(g32, lo, n, after_a=None, at=None):
+            if at is not None:
+                gb = arena.tile([P, n, PACK], BF16, name="gb_placed", offset=at, align_bytes=64)
+            elif after_a is None:
                 gb = grouped.tile([P, n, PACK], BF16, name="gb", align_bytes=64)
             else:
                 gb = keep.tile([P, n, PACK], BF16, name=f"a{after_a}", align_bytes=64)
@@ -305,7 +307,7 @@ def tile_moe_bdx_mlp_relu2_kernel(
         HALF = C // 2
         da_words = arena.tile([P, 2 * C], U32, name="da_words", offset=G32_AT[0] + 4 * PAIR, align_bytes=64)
         first_products = arena.tile([P, 3 * H], BF16, name="products0", offset=G32_AT[1], align_bytes=64)
-        product3 = keep.tile([P, H], BF16, name="dy1_3")
+        product3 = keep.tile([P, H], BF16, name="a2", align_bytes=64)
         times_parked(3, product3[:])
         for block in range(3):
             times(block, first_products[:, block * H : (block + 1) * H])
@@ -330,7 +332,9 @@ def tile_moe_bdx_mlp_relu2_kernel(
         g_3a = arena.tile(
             [P, PACK, HALF], F32, name="g32_3a", offset=G32_AT[0] + G32_BYTES - 4 * PACK * HALF, align_bytes=64
         )
-        gb_3a = last_gathers(g_3a, 3 * C, HALF)
+        for t in range(PACK):
+            gather(g_3a, 2, t, 3 * C, 0, HALF)
+        gb_3a = interleave(g_3a, 0, HALF, at=G32_AT[0] + 8 * PAIR)
         quantise(gb_2, 2, 2 * C, C)
         for block in (11, 8, 9, 10):
             multiply2(block, 2)
@@ -346,7 +350,7 @@ def tile_moe_bdx_mlp_relu2_kernel(
         multiply2(12, 2)
         multiply2(13, 2)
         park(12, parked23[:, H : 2 * H])
-        product7 = keep.tile([P, H], BF16, name="dy2_3")
+        product7 = arena.tile([P, H], BF16, name="product7", offset=G32_AT[0] + 8 * PAIR, align_bytes=64)
         times_parked(7, product7[:])
         second_products = keep.tile([P, 3 * H], BF16, name="dy2_2")
         for block in range(4, 7):
@@ -385,12 +389,12 @@ def tile_moe_bdx_mlp_relu2_kernel(
         times(14)
         da3b = keep.tile([P, P * PACK], BF16, name="da3b", align_bytes=64)
         turn((14,), 1, da3b, 0)
-        words1, scales1 = late_codes(1, 13, 10)
-        quantise_da(da1, words1, scales1, 0, C)
-        nc.scalar.copy(dx_sb[:, C : 2 * C], multiply1(1, 6, words1, scales1, 0)[:])
         times(15)
         da3c = keep.tile([P, P * PACK], BF16, name="da3c", align_bytes=64)
         turn((15,), 5, da3c, 0)
+        words1, scales1 = late_codes(1, 13, 10)
+        quantise_da(da1, words1, scales1, 0, C)
+        nc.scalar.copy(dx_sb[:, C : 2 * C], multiply1(1, 6, words1, scales1, 0)[:])
         words2, scales2 = late_codes(2, 14, 9)
         quantise_da(da2, words2, scales2, 0, C)
         nc.scalar.copy(dx_sb[:, 2 * C : 3 * C], multiply1(2, 7, words2, scales2, 0)[:])

@@ -8,9 +8,15 @@ P = 128
 PACK = 4
 SLOTS = E * C
 PASSES = N // 512
-QT = C // P
+BLOCKS = C // P
 PAIR = 2 * C
+HALF = C // 2
 PAD = 8
+W2_PASS_BYTES = 2 * H
+W1_BYTES = 2 * K
+ALIGN = 64
+FIRST_CUTS = (0, 128, 384, PAIR)
+OUT_CUTS = (0, 512, 896, T)
 
 FLOPS = 2 * SLOTS * (N * H + H * K)
 BYTES = (
@@ -31,6 +37,11 @@ ADD = mybir.AluOpType.add
 COPY = mybir.ActivationFunctionType.Copy
 RELU = mybir.ActivationFunctionType.Relu
 
+ROOM_BYTES = 4 * PACK * PAIR
+SLOPE_BYTES = 4 * H
+ROOM = (SLOPE_BYTES, SLOPE_BYTES + ROOM_BYTES)
+SLOPE_AT = (0,) + tuple(ROOM[1] + ROOM_BYTES + place * SLOPE_BYTES for place in range(E * BLOCKS - 1))
+
 
 def tile_moe_bdx_mlp_relu2_kernel(
     tc, dyT, a, w2_words, w2_scales, w1_words, w1_scales, gate, offs, pos1, pos2, out
@@ -38,49 +49,48 @@ def tile_moe_bdx_mlp_relu2_kernel(
     nc = tc.nc
     with ExitStack() as ctx:
         keep = ctx.enter_context(tc.tile_pool(name="keep", bufs=1))
-        arena = ctx.enter_context(tc.tile_pool(name="arena", bufs=1))
-        grouped = ctx.enter_context(tc.tile_pool(name="grouped", bufs=2))
+        placed = ctx.enter_context(tc.tile_pool(name="placed", bufs=1))
+        rounded_pool = ctx.enter_context(tc.tile_pool(name="rounded_pool", bufs=2))
         coded = ctx.enter_context(tc.tile_pool(name="coded", bufs=5))
-        hidden = ctx.enter_context(tc.tile_pool(name="hidden", bufs=4))
+        product_pool = ctx.enter_context(tc.tile_pool(name="product_pool", bufs=4))
         da_pool = ctx.enter_context(tc.tile_pool(name="da_pool", bufs=3))
         psum = ctx.enter_context(tc.psum_pool(name="psum", bufs=1))
-
-        G32_BYTES = 4 * PACK * PAIR
-        SLOPE_BYTES = 4 * H
-        G32_AT = (SLOPE_BYTES, SLOPE_BYTES + G32_BYTES)
-        slope_at = {0: 0}
-        for block in range(1, E * QT):
-            slope_at[block] = G32_AT[1] + G32_BYTES + (block - 1) * SLOPE_BYTES
 
         def bank(b):
             return psum.tile([P, 512], F32, name=f"bank{b}")
 
+        def place(shape, dtype, name, at):
+            return placed.tile(shape, dtype, name=name, offset=at, align_bytes=ALIGN)
+
+        def on_a(e, shape, dtype):
+            return keep.tile(shape, dtype, name=f"a{e}", align_bytes=ALIGN)
+
         offs_sb = keep.tile([P, SLOTS // 16], U16, name="offs_sb")
         pos1_sb = keep.tile([P, T // 16], U16, name="pos1_sb")
         pos2_sb = keep.tile([P, T // 16], U16, name="pos2_sb")
-        gates = [keep.tile([P, PAIR], F32, name=f"gate{e}") for e in range(2)]
+        gates = [keep.tile([P, PAIR], F32, name=f"gate{pair}") for pair in range(2)]
         planes = [
-            [keep.tile([P, T + PAD], F32, name=f"dy{s}_{t}") for t in range(PACK)] for s in range(PASSES)
+            [keep.tile([P, T + PAD], F32, name=f"dy{s}_{d}") for d in range(PACK)] for s in range(PASSES)
         ]
-        w2_sb = [keep.tile([P, PASSES * 1024], U8, name=f"w2_{e}", align_bytes=64) for e in range(E)]
-        w2_sc = keep.tile([P, E * PASSES * H], U8, name="w2_sc", align_bytes=64)
-        w1_sb = keep.tile([P, E * 256], U8, name="w1_sb", align_bytes=64)
-        w1_sc = keep.tile([P, E * K], U8, name="w1_sc", align_bytes=64)
+        w2_sb = [keep.tile([P, PASSES * W2_PASS_BYTES], U8, name=f"w2_{e}", align_bytes=ALIGN) for e in range(E)]
+        w2_sc = keep.tile([P, E * PASSES * H], U8, name="w2_sc", align_bytes=ALIGN)
+        w1_sb = keep.tile([P, E * W1_BYTES], U8, name="w1_sb", align_bytes=ALIGN)
+        w1_sc = keep.tile([P, E * K], U8, name="w1_sc", align_bytes=ALIGN)
         ident = keep.tile([P, P], F32, name="ident")
-        da_scales = keep.tile([P, 2 * C], U8, name="da_scales", align_bytes=64)
+        scales03 = keep.tile([P, 2 * C], U8, name="scales03", align_bytes=ALIGN)
 
         for s in range(PASSES):
-            for t in range(PACK):
-                nc.vector.memset(planes[s][t][:, T : T + PAD], 0.0)
+            for d in range(PACK):
+                nc.vector.memset(planes[s][d][:, T : T + PAD], 0.0)
         nc.vector.memset(w2_sc[:].bitcast(I32), 0)
         nc.vector.memset(w1_sc[:].bitcast(I32), 0)
         make_identity(nc, ident[:])
 
-        dy_rows = dyT.rearrange("(s p t) j -> s t p j", p=P, t=PACK)
+        dy_rows = dyT.rearrange("(s p d) j -> s d p j", p=P, d=PACK)
         a_sb = {}
 
-        def load_plane(s, t):
-            nc.sync.dma_start(out=planes[s][t][:, 0:T], in_=dy_rows[s, t])
+        def load_plane(s, d):
+            nc.sync.dma_start(out=planes[s][d][:, 0:T], in_=dy_rows[s, d])
 
         def load_gate(lo, hi):
             base = lo % PAIR
@@ -93,28 +103,27 @@ def tile_moe_bdx_mlp_relu2_kernel(
             )
 
         def load_a(e):
-            a_sb[e] = keep.tile([P, PACK, C], F32, name=f"a{e}", align_bytes=64)
+            a_sb[e] = on_a(e, [P, PACK, C], F32)
             nc.sync.dma_start(
-                out=a_sb[e][:], in_=a[:, e * C : (e + 1) * C].rearrange("(p t) c -> p t c", t=PACK)
+                out=a_sb[e][:], in_=a[:, e * C : (e + 1) * C].rearrange("(p d) c -> p d c", d=PACK)
             )
 
-        def load_scales(plane, source, groups):
+        def load_scales(tile, source, groups):
             src = source.bitcast(I32).rearrange("e s f w -> f (e s) w")
             for q in range(4):
                 nc.sync.dma_start(
-                    out=plane[32 * q : 32 * q + 4, :].bitcast(I32).rearrange("f (g w) -> f g w", g=groups),
+                    out=tile[32 * q : 32 * q + 4, :].bitcast(I32).rearrange("f (g w) -> f g w", g=groups),
                     in_=src[4 * q : 4 * q + 4],
                 )
 
-        FIRST = 384
         nc.sync.dma_start(offs_sb[:], offs)
         load_plane(0, 0)
-        load_gate(0, FIRST)
-        load_gate(FIRST, PAIR)
+        for lo, hi in zip(FIRST_CUTS, FIRST_CUTS[1:]):
+            load_gate(lo, hi)
         for s in range(PASSES):
-            for t in range(PACK):
-                if (s, t) != (0, 0):
-                    load_plane(s, t)
+            for d in range(PACK):
+                if (s, d) != (0, 0):
+                    load_plane(s, d)
             if s > 0:
                 load_a(s - 1)
         load_gate(PAIR, SLOTS)
@@ -128,93 +137,70 @@ def tile_moe_bdx_mlp_relu2_kernel(
         codes = {}
         dh = {}
         slopes = {}
-        by_slot = {}
+        products = {}
         parked = {}
 
-        def gather(g32, s, t, slot0, lo, n):
+        def gather(g32, s, d, slot0, lo, hi):
             first = slot0 + lo
             base = first % PAIR
             nc.vector.tensor_tensor(
-                g32[:, t, lo : lo + n],
-                planes[s][t][:].indirect(offs_sb[:, first // 16 : (first + n) // 16]),
-                gates[first // PAIR][:, base : base + n],
+                g32[:, d, lo:hi],
+                planes[s][d][:].indirect(offs_sb[:, first // 16 : (slot0 + hi) // 16]),
+                gates[first // PAIR][:, base : base + hi - lo],
                 MULT,
             )
 
-        def g32_tile(s, pair, at):
-            return arena.tile([P, PACK, PAIR], F32, name=f"g32_{pair}_{s}", offset=at, align_bytes=64)
-
-        def gathers(s, pair, at):
-            g32 = g32_tile(s, pair, at)
-            for t in range(PACK):
-                if (s, pair, t) == (0, 0, 0):
-                    gather(g32, s, t, 0, 0, FIRST)
-                    gather(g32, s, t, 0, FIRST, PAIR - FIRST)
-                else:
-                    gather(g32, s, t, pair * PAIR, 0, PAIR)
+        def gathers(s, slot0, n, at):
+            g32 = place([P, PACK, n], F32, f"g32_{s}_{slot0}", at)
+            for d in range(PACK):
+                cuts = FIRST_CUTS if (s, slot0, d) == (0, 0, 0) else (0, n)
+                for lo, hi in zip(cuts, cuts[1:]):
+                    gather(g32, s, d, slot0, lo, hi)
             return g32
 
-        def interleave(g32, lo, n, after_a=None, at=None):
-            if at is not None:
-                gb = arena.tile([P, n, PACK], BF16, name="gb_placed", offset=at, align_bytes=64)
-            elif after_a is None:
-                gb = grouped.tile([P, n, PACK], BF16, name="gb", align_bytes=64)
-            else:
-                gb = keep.tile([P, n, PACK], BF16, name=f"a{after_a}", align_bytes=64)
+        def ring_tile(n):
+            return rounded_pool.tile([P, n, PACK], BF16, name="rounded", align_bytes=ALIGN)
+
+        def round_g(g32, rounded):
             nc.scalar.activation(
-                gb[:].rearrange("p (c i) t -> p c t i", i=4),
-                g32[:, :, lo : lo + n].rearrange("p t (c i) -> p c t i", i=4),
+                rounded[:].rearrange("p (c i) d -> p c d i", i=4),
+                g32[:].rearrange("p d (c i) -> p c d i", i=4),
                 COPY,
             )
-            return gb
+            return rounded
 
-        def quantise(gb, s, slot0, n, at=None):
-            if at is None:
-                words = coded.tile([P, n], U32, name="g_words", align_bytes=64)
-            else:
-                words = arena.tile([P, n], U32, name="late_words", offset=at, align_bytes=64)
-            scales = coded.tile([P, n], U8, name="g_scales", align_bytes=64)
+        def ring_words(n):
+            return coded.tile([P, n], U32, name="g_words", align_bytes=ALIGN)
+
+        def quantise_g(rounded, s, slot0, words):
+            n = rounded.shape[1]
+            scales = coded.tile([P, n], U8, name="g_scales", align_bytes=ALIGN)
             nc.vector.quantize_mx(
                 out=words[:].bitcast(E5M2),
                 scales=scales[:],
-                in_=gb[:].rearrange("p c t -> p (c t)"),
+                in_=rounded[:].rearrange("p c d -> p (c d)"),
             )
             for j in range(n // P):
                 codes[slot0 // P + j, s] = (words, scales, j * P)
 
-        def multiply2(block, s, b=None):
-            e = block // QT
+        def multiply2(block, s):
+            e = block // BLOCKS
             words, scales, base = codes[block, s]
-            if s == 0:
-                dh[block] = bank(b)
             cols = slice(base, base + P)
             nc.tensor.matmul_mx(
                 out=dh[block][:],
                 lhsT=words[:, cols].bitcast(E5M2),
                 lhsT_scale=scales[:, cols],
-                rhs=w2_sb[e][:, s * 1024 : (s + 1) * 1024].bitcast(E2M1),
+                rhs=w2_sb[e][:, s * W2_PASS_BYTES : (s + 1) * W2_PASS_BYTES].bitcast(E2M1),
                 rhs_scale=w2_sc[:, (e * PASSES + s) * H : (e * PASSES + s + 1) * H],
                 start=(s == 0),
                 stop=(s == PASSES - 1),
             )
 
-        def slope(e):
-            for q in range(QT):
-                block = e * QT + q
-                slopes[block] = arena.tile(
-                    [P, H], F32, name=f"slope{block}", offset=slope_at[block], align_bytes=64
-                )
-                turned = bank(4 + q)
-                for t in range(PACK):
-                    nc.tensor.transpose(
-                        turned[:, t * P : (t + 1) * P], a_sb[e][:, t, q * P : (q + 1) * P], ident[:]
-                    )
-                nc.scalar.activation(
-                    slopes[block][:].rearrange("p (u m d) -> p u m d", u=2, d=2),
-                    turned[:].rearrange("p (u d m) -> p u m d", u=2, d=2),
-                    RELU,
-                    scale=2.0,
-                )
+        def open_dh(block, b, passes):
+            dh[block] = bank(b)
+            for s in range(passes):
+                multiply2(block, s)
 
         def paired(ap):
             return ap.rearrange("p (u m d) -> p u m d", u=2, d=2)
@@ -222,24 +208,41 @@ def tile_moe_bdx_mlp_relu2_kernel(
         def dh_paired(block):
             return dh[block][:].rearrange("p (m u d) -> p u m d", u=2, d=2)
 
-        def times(block, dest=None):
-            if dest is None:
-                dest = hidden.tile([P, H], BF16, name="by_slot")[:]
-            by_slot[block] = dest
+        def slope(e):
+            for q in range(BLOCKS):
+                block = e * BLOCKS + q
+                slopes[block] = place([P, H], F32, f"slope{block}", SLOPE_AT[block])
+                turned = bank(4 + q)
+                for j in range(PACK):
+                    nc.tensor.transpose(
+                        turned[:, j * P : (j + 1) * P], a_sb[e][:, j, q * P : (q + 1) * P], ident[:]
+                    )
+                nc.scalar.activation(
+                    paired(slopes[block][:]),
+                    turned[:].rearrange("p (u d m) -> p u m d", u=2, d=2),
+                    RELU,
+                    scale=2.0,
+                )
+
+        def times(block, dest):
+            products[block] = dest
             nc.vector.tensor_tensor(paired(dest), dh_paired(block), paired(slopes[block][:]), MULT)
+
+        def times_in_ring(block):
+            times(block, product_pool.tile([P, H], BF16, name="product")[:])
 
         def park(block, dest):
             nc.scalar.copy(paired(dest), dh_paired(block))
             parked[block] = dest
 
-        def times_parked(block, dest):
-            by_slot[block] = dest
+        def times_on_gpsimd(block, dest):
+            products[block] = dest
             nc.gpsimd.tensor_tensor(dest, parked[block], slopes[block][:], MULT)
 
         def turn(blocks, b, da, lo):
             turned = bank(b)
             for j, block in enumerate(blocks):
-                pairs = by_slot[block].bitcast(F32)
+                pairs = products[block].bitcast(F32)
                 for u in range(2):
                     nc.tensor.transpose(
                         turned[:, (2 * j + u) * P : (2 * j + u + 1) * P], pairs[:, u * P : (u + 1) * P], ident[:]
@@ -250,10 +253,11 @@ def tile_moe_bdx_mlp_relu2_kernel(
                 turned[:, 0 : 2 * n].rearrange("p (j u c) -> p j c u", c=P, u=2),
             )
 
-        def da_tile(n):
-            return da_pool.tile([P, n * PACK], BF16, name="da", align_bytes=64)
+        def da_tile():
+            return da_pool.tile([P, C * PACK], BF16, name="da", align_bytes=ALIGN)
 
-        def quantise_da(da, words, scales, lo, n):
+        def quantise_da(da, words, scales, lo):
+            n = da.shape[1] // PACK
             nc.vector.quantize_mx(
                 out=words[:, lo : lo + n].bitcast(E5M2), scales=scales[:, lo : lo + n], in_=da[:]
             )
@@ -262,7 +266,7 @@ def tile_moe_bdx_mlp_relu2_kernel(
             dx = bank(b)
             nc.tensor.matmul_mx(
                 out=dx[:],
-                lhsT=w1_sb[:, e * 256 : (e + 1) * 256].bitcast(E2M1),
+                lhsT=w1_sb[:, e * W1_BYTES : (e + 1) * W1_BYTES].bitcast(E2M1),
                 lhsT_scale=w1_sc[:, e * K : (e + 1) * K],
                 rhs=words[:, lo : lo + C].bitcast(E5M2),
                 rhs_scale=scales[:, lo : lo + C],
@@ -271,8 +275,8 @@ def tile_moe_bdx_mlp_relu2_kernel(
             )
             return dx
 
-        gb_a0 = interleave(gathers(0, 0, G32_AT[0]), 0, PAIR)
-        gb_a1 = interleave(gathers(1, 0, G32_AT[1]), 0, PAIR)
+        rounded_01_0 = round_g(gathers(0, 0, PAIR, ROOM[0]), ring_tile(PAIR))
+        rounded_01_1 = round_g(gathers(1, 0, PAIR, ROOM[1]), ring_tile(PAIR))
         slope(0)
         slope(1)
         load_scales(w1_sc, w1_scales, E)
@@ -282,141 +286,113 @@ def tile_moe_bdx_mlp_relu2_kernel(
         )
         nc.sync.dma_start(pos1_sb[:], pos1)
         nc.sync.dma_start(pos2_sb[:], pos2)
-        quantise(gb_a0, 0, 0, PAIR)
-        gb_a2 = interleave(gathers(2, 0, G32_AT[0]), 0, PAIR, 1)
-        quantise(gb_a1, 1, 0, PAIR)
-        for s in range(2):
-            for block in range(QT):
-                multiply2(block, s, block)
+        quantise_g(rounded_01_0, 0, 0, ring_words(PAIR))
+        rounded_01_2 = round_g(gathers(2, 0, PAIR, ROOM[0]), on_a(1, [P, PAIR, PACK], BF16))
+        quantise_g(rounded_01_1, 1, 0, ring_words(PAIR))
+        for block in range(BLOCKS):
+            open_dh(block, block, 1)
+        for block in range(BLOCKS):
+            multiply2(block, 1)
         slope(2)
-        dx_sb = keep.tile([P, SLOTS], F32, name="a0", align_bytes=64)
-        gb_b0 = interleave(gathers(0, 1, G32_AT[1]), 0, PAIR, 2)
-        quantise(gb_a2, 2, 0, PAIR)
-        parked01 = keep.tile([P, 2 * H], F32, name="a1", align_bytes=64)
-        for block in reversed(range(QT)):
+        dx_sb = on_a(0, [P, SLOTS], F32)
+        rounded_23_0 = round_g(gathers(0, PAIR, PAIR, ROOM[1]), on_a(2, [P, PAIR, PACK], BF16))
+        quantise_g(rounded_01_2, 2, 0, ring_words(PAIR))
+        parked_01 = on_a(1, [P, 2 * H], F32)
+        for block in reversed(range(BLOCKS)):
             multiply2(block, 2)
-        park(3, parked01[:, 0:H])
+        park(3, parked_01[:, 0:H])
         slope(3)
-        for block in range(QT, 2 * QT):
-            for s in range(PASSES):
-                multiply2(block, s, block)
-        park(7, parked01[:, H : 2 * H])
-        gb_b1 = interleave(gathers(1, 1, G32_AT[0]), 0, PAIR, 3)
-        quantise(gb_b0, 0, PAIR, PAIR)
+        for block in range(BLOCKS, 2 * BLOCKS):
+            open_dh(block, block, PASSES)
+        park(7, parked_01[:, H : 2 * H])
+        rounded_23_1 = round_g(gathers(1, PAIR, PAIR, ROOM[0]), on_a(3, [P, PAIR, PACK], BF16))
+        quantise_g(rounded_23_0, 0, PAIR, ring_words(PAIR))
 
-        HALF = C // 2
-        da_words = arena.tile([P, 2 * C], U32, name="da_words", offset=G32_AT[0] + 4 * PAIR, align_bytes=64)
-        first_products = arena.tile([P, 3 * H], BF16, name="products0", offset=G32_AT[1], align_bytes=64)
-        product3 = keep.tile([P, H], BF16, name="a2", align_bytes=64)
-        times_parked(3, product3[:])
+        words03 = place([P, 2 * C], U32, "words03", ROOM[0] + 4 * PAIR)
+        products_0 = place([P, 3 * H], BF16, "products_0", ROOM[1])
+        times_on_gpsimd(3, on_a(2, [P, H], BF16)[:])
         for block in range(3):
-            times(block, first_products[:, block * H : (block + 1) * H])
-        da0 = da_tile(C)
+            times(block, products_0[:, block * H : (block + 1) * H])
+        da0 = da_tile()
         turn((0, 1), 0, da0, 0)
         turn((2, 3), 1, da0, HALF)
-        for block, b in ((8, 3), (9, 2), (10, 0), (11, 1)):
-            multiply2(block, 0, b)
+        for block, b in zip(range(8, 12), (3, 2, 0, 1)):
+            open_dh(block, b, 1)
 
-        def last_gathers(g32, slot0, n):
-            for t in range(PACK):
-                gather(g32, 2, t, slot0, 0, n)
-            return interleave(g32, 0, n)
-
-        g_2 = arena.tile([P, PACK, C], F32, name="g32_2", offset=slope_at[1] + 64 - 4 * PACK * C, align_bytes=64)
-        gb_2 = last_gathers(g_2, 2 * C, C)
-        quantise(gb_b1, 1, PAIR, PAIR, G32_AT[0] - 64)
+        rounded_2 = round_g(gathers(2, 2 * C, C, SLOPE_AT[1] + ALIGN - 4 * PACK * C), ring_tile(C))
+        quantise_g(rounded_23_1, 1, PAIR, place([P, PAIR], U32, "words_23_1", ROOM[0] - ALIGN))
         for block in range(8, 12):
             multiply2(block, 1)
-        multiply2(12, 0, 7)
-        multiply2(12, 1)
-        g_3a = arena.tile(
-            [P, PACK, HALF], F32, name="g32_3a", offset=G32_AT[0] + G32_BYTES - 4 * PACK * HALF, align_bytes=64
-        )
-        for t in range(PACK):
-            gather(g_3a, 2, t, 3 * C, 0, HALF)
-        gb_3a = interleave(g_3a, 0, HALF, at=G32_AT[0] + 8 * PAIR)
-        quantise(gb_2, 2, 2 * C, C)
+        open_dh(12, 7, 2)
+        g32_3a = gathers(2, 3 * C, HALF, ROOM[1] - 4 * PACK * HALF)
+        rounded_3a_at = ROOM[0] + 4 * PAIR + 4 * 2 * C
+        rounded_3a = round_g(g32_3a, place([P, HALF, PACK], BF16, "rounded_3a", rounded_3a_at))
+        quantise_g(rounded_2, 2, 2 * C, ring_words(C))
         for block in (11, 8, 9, 10):
             multiply2(block, 2)
-        parked23 = keep.tile([P, 2 * H], F32, name="a3", align_bytes=64)
-        park(11, parked23[:, 0:H])
-        multiply2(13, 0, 1)
-        multiply2(13, 1)
-        g_3b = arena.tile([P, PACK, HALF], F32, name="g32_3b", offset=slope_at[1] - 4 * PACK * HALF, align_bytes=64)
-        for t in range(PACK):
-            gather(g_3b, 2, t, 3 * C + HALF, 0, HALF)
-        gb_3b = interleave(g_3b, 0, HALF, 2)
-        quantise(gb_3a, 2, 3 * C, HALF)
+        parked_23 = on_a(3, [P, 2 * H], F32)
+        park(11, parked_23[:, 0:H])
+        open_dh(13, 1, 2)
+        rounded_3b = round_g(
+            gathers(2, 3 * C + HALF, HALF, SLOPE_AT[1] - 4 * PACK * HALF), on_a(2, [P, HALF, PACK], BF16)
+        )
+        quantise_g(rounded_3a, 2, 3 * C, ring_words(HALF))
         multiply2(12, 2)
         multiply2(13, 2)
-        park(12, parked23[:, H : 2 * H])
-        product7 = arena.tile([P, H], BF16, name="product7", offset=G32_AT[0] + 8 * PAIR, align_bytes=64)
-        times_parked(7, product7[:])
-        second_products = keep.tile([P, 3 * H], BF16, name="dy2_2")
+        park(12, parked_23[:, H : 2 * H])
+
+        times_on_gpsimd(7, place([P, H], BF16, "product_7", rounded_3a_at)[:])
+        products_1 = keep.tile([P, 3 * H], BF16, name=f"dy{PASSES - 1}_{PACK - 2}")
         for block in range(4, 7):
-            times(block, second_products[:, (block - 4) * H : (block - 3) * H])
-        da1 = da_tile(C)
+            times(block, products_1[:, (block - 4) * H : (block - 3) * H])
+        da1 = da_tile()
         turn((4, 5), 4, da1, 0)
-        multiply2(14, 0, 5)
-        multiply2(14, 1)
+        open_dh(14, 5, 2)
         turn((6, 7), 6, da1, HALF)
-        multiply2(15, 0, 4)
-        multiply2(15, 1)
-        quantise_da(da0, da_words, da_scales, 0, C)
-        quantise(gb_3b, 2, 3 * C + HALF, HALF)
+        open_dh(15, 4, 2)
+        quantise_da(da0, words03, scales03, 0)
+        quantise_g(rounded_3b, 2, 3 * C + HALF, ring_words(HALF))
         multiply2(14, 2)
         multiply2(15, 2)
-        products = keep.tile([P, 2 * H], BF16, name="a2", align_bytes=64)
-        times_parked(11, products[:, 0:H])
-        times_parked(12, products[:, H : 2 * H])
-        nc.scalar.copy(dx_sb[:, 0:C], multiply1(0, 7, da_words, da_scales, 0)[:])
 
-        def late_codes(e, words_on, scales_on):
-            return (
-                arena.tile([P, C], U32, name=f"da{e}_words", offset=slope_at[words_on], align_bytes=64),
-                arena.tile([P, C], U8, name=f"da{e}_scales", offset=slope_at[scales_on], align_bytes=64),
-            )
-
-        da2 = da_tile(C)
-        times(8)
-        times(9)
+        products_gpsimd = on_a(2, [P, 2 * H], BF16)
+        times_on_gpsimd(11, products_gpsimd[:, 0:H])
+        times_on_gpsimd(12, products_gpsimd[:, H : 2 * H])
+        nc.scalar.copy(dx_sb[:, 0:C], multiply1(0, 7, words03, scales03, 0)[:])
+        da2 = da_tile()
+        times_in_ring(8)
+        times_in_ring(9)
         turn((8, 9), 3, da2, 0)
-        times(10)
+        times_in_ring(10)
         turn((10, 11), 2, da2, HALF)
-        times(13)
-        da3a = keep.tile([P, HALF * PACK], BF16, name="da3a", align_bytes=64)
-        turn((12, 13), 0, da3a, 0)
-        times(14)
-        da3b = keep.tile([P, P * PACK], BF16, name="da3b", align_bytes=64)
-        turn((14,), 1, da3b, 0)
-        times(15)
-        da3c = keep.tile([P, P * PACK], BF16, name="da3c", align_bytes=64)
-        turn((15,), 5, da3c, 0)
-        words1, scales1 = late_codes(1, 13, 10)
-        quantise_da(da1, words1, scales1, 0, C)
-        nc.scalar.copy(dx_sb[:, C : 2 * C], multiply1(1, 6, words1, scales1, 0)[:])
-        words2, scales2 = late_codes(2, 14, 9)
-        quantise_da(da2, words2, scales2, 0, C)
-        nc.scalar.copy(dx_sb[:, 2 * C : 3 * C], multiply1(2, 7, words2, scales2, 0)[:])
-        quantise_da(da3a, da_words, da_scales, C, HALF)
-        quantise_da(da3b, da_words, da_scales, C + HALF, P)
-        most = multiply1(3, 3, da_words, da_scales, C - P)
-        quantise_da(da3c, da_words, da_scales, 2 * C - P, P)
-        rest = multiply1(3, 0, da_words, da_scales, C)
-        nc.vector.tensor_copy(dx_sb[:, 3 * C : SLOTS - P], most[:, P:C])
-        nc.scalar.copy(dx_sb[:, SLOTS - P : SLOTS], rest[:, C - P : C])
+        times_in_ring(13)
+        da_12_13 = keep.tile([P, HALF * PACK], BF16, name="da_12_13", align_bytes=ALIGN)
+        turn((12, 13), 0, da_12_13, 0)
+        times_in_ring(14)
+        da_14 = keep.tile([P, P * PACK], BF16, name="da_14", align_bytes=ALIGN)
+        turn((14,), 1, da_14, 0)
+        times_in_ring(15)
+        da_15 = keep.tile([P, P * PACK], BF16, name="da_15", align_bytes=ALIGN)
+        turn((15,), 5, da_15, 0)
 
-        first = arena.tile([P, T], F32, name="first", offset=slope_at[6], align_bytes=64)
-        total = arena.tile([P, T], F32, name="total", offset=slope_at[8], align_bytes=64)
-        cuts = (0, 512, 896, T)
+        for e, da, words_on, scales_on, b in ((1, da1, 13, 10, 6), (2, da2, 14, 9, 7)):
+            words = place([P, C], U32, f"words{e}", SLOPE_AT[words_on])
+            scales = place([P, C], U8, f"scales{e}", SLOPE_AT[scales_on])
+            quantise_da(da, words, scales, 0)
+            nc.scalar.copy(dx_sb[:, e * C : (e + 1) * C], multiply1(e, b, words, scales, 0)[:])
+        quantise_da(da_12_13, words03, scales03, C)
+        quantise_da(da_14, words03, scales03, C + HALF)
+        dx_12_14 = multiply1(3, 3, words03, scales03, C - P)
+        quantise_da(da_15, words03, scales03, 2 * C - P)
+        dx_15 = multiply1(3, 0, words03, scales03, C)
+        nc.vector.tensor_copy(dx_sb[:, 3 * C : SLOTS - P], dx_12_14[:, P:C])
+        nc.scalar.copy(dx_sb[:, SLOTS - P : SLOTS], dx_15[:, C - P : C])
 
-        def fetch_second(i):
-            lo, hi = cuts[i], cuts[i + 1]
+        first = place([P, T], F32, "first", SLOPE_AT[6])
+        total = place([P, T], F32, "total", SLOPE_AT[8])
+        nc.vector.tensor_copy(first[:], dx_sb[:].indirect(pos1_sb[:]))
+        for lo, hi in zip(OUT_CUTS, OUT_CUTS[1:]):
             nc.vector.tensor_tensor(
                 total[:, lo:hi], dx_sb[:].indirect(pos2_sb[:, lo // 16 : hi // 16]), first[:, lo:hi], ADD
             )
             nc.sync.dma_start(out=out[:, lo:hi], in_=total[:, lo:hi])
-
-        nc.vector.tensor_copy(first[:], dx_sb[:].indirect(pos1_sb[:]))
-        for i in range(3):
-            fetch_second(i)

@@ -8,7 +8,7 @@ P = 128
 PACK = 4
 SLOTS = E * C
 PASSES = N // 512
-BLOCKS = C // P
+GROUPS = C // P
 PAIR = 2 * C
 HALF = C // 2
 PAD = 8
@@ -40,7 +40,7 @@ RELU = mybir.ActivationFunctionType.Relu
 ROOM_BYTES = 4 * PACK * PAIR
 SLOPE_BYTES = 4 * H
 ROOM = (SLOPE_BYTES, SLOPE_BYTES + ROOM_BYTES)
-SLOPE_AT = (0,) + tuple(ROOM[1] + ROOM_BYTES + place * SLOPE_BYTES for place in range(E * BLOCKS - 1))
+SLOPE_AT = (0,) + tuple(ROOM[1] + ROOM_BYTES + x * SLOPE_BYTES for x in range(E * GROUPS - 1))
 
 
 def tile_moe_bdx_mlp_relu2_kernel(
@@ -86,7 +86,7 @@ def tile_moe_bdx_mlp_relu2_kernel(
         nc.vector.memset(w1_sc[:].bitcast(I32), 0)
         make_identity(nc, ident[:])
 
-        dy_rows = dyT.rearrange("(s p d) j -> s d p j", p=P, d=PACK)
+        dy_rows = dyT.rearrange("(s p d) t -> s d p t", p=P, d=PACK)
         a_sb = {}
 
         def load_plane(s, d):
@@ -108,11 +108,11 @@ def tile_moe_bdx_mlp_relu2_kernel(
                 out=a_sb[e][:], in_=a[:, e * C : (e + 1) * C].rearrange("(p d) c -> p d c", d=PACK)
             )
 
-        def load_scales(tile, source, groups):
+        def load_scales(tile, source, runs):
             src = source.bitcast(I32).rearrange("e s f w -> f (e s) w")
             for q in range(4):
                 nc.sync.dma_start(
-                    out=tile[32 * q : 32 * q + 4, :].bitcast(I32).rearrange("f (g w) -> f g w", g=groups),
+                    out=tile[32 * q : 32 * q + 4, :].bitcast(I32).rearrange("f (x w) -> f x w", x=runs),
                     in_=src[4 * q : 4 * q + 4],
                 )
 
@@ -141,54 +141,54 @@ def tile_moe_bdx_mlp_relu2_kernel(
         parked = {}
 
         def gather(g32, s, d, slot0, lo, hi):
-            first = slot0 + lo
-            base = first % PAIR
+            start = slot0 + lo
+            base = start % PAIR
             nc.vector.tensor_tensor(
                 g32[:, d, lo:hi],
-                planes[s][d][:].indirect(offs_sb[:, first // 16 : (slot0 + hi) // 16]),
-                gates[first // PAIR][:, base : base + hi - lo],
+                planes[s][d][:].indirect(offs_sb[:, start // 16 : (slot0 + hi) // 16]),
+                gates[start // PAIR][:, base : base + hi - lo],
                 MULT,
             )
 
-        def gathers(s, slot0, n, at):
-            g32 = place([P, PACK, n], F32, f"g32_{s}_{slot0}", at)
+        def gathers(s, slot0, width, at):
+            g32 = place([P, PACK, width], F32, f"g32_{s}_{slot0}", at)
             for d in range(PACK):
-                cuts = FIRST_CUTS if (s, slot0, d) == (0, 0, 0) else (0, n)
+                cuts = FIRST_CUTS if (s, slot0, d) == (0, 0, 0) else (0, width)
                 for lo, hi in zip(cuts, cuts[1:]):
                     gather(g32, s, d, slot0, lo, hi)
             return g32
 
-        def ring_tile(n):
-            return rounded_pool.tile([P, n, PACK], BF16, name="rounded", align_bytes=ALIGN)
+        def ring_tile(width):
+            return rounded_pool.tile([P, width, PACK], BF16, name="rounded", align_bytes=ALIGN)
 
         def round_g(g32, rounded):
             nc.scalar.activation(
-                rounded[:].rearrange("p (c i) d -> p c d i", i=4),
-                g32[:].rearrange("p d (c i) -> p c d i", i=4),
+                rounded[:].rearrange("p (c r) d -> p c d r", r=4),
+                g32[:].rearrange("p d (c r) -> p c d r", r=4),
                 COPY,
             )
             return rounded
 
-        def ring_words(n):
-            return coded.tile([P, n], U32, name="g_words", align_bytes=ALIGN)
+        def ring_words(width):
+            return coded.tile([P, width], U32, name="g_words", align_bytes=ALIGN)
 
         def quantise_g(rounded, s, slot0, words):
-            n = rounded.shape[1]
-            scales = coded.tile([P, n], U8, name="g_scales", align_bytes=ALIGN)
+            width = rounded.shape[1]
+            scales = coded.tile([P, width], U8, name="g_scales", align_bytes=ALIGN)
             nc.vector.quantize_mx(
                 out=words[:].bitcast(E5M2),
                 scales=scales[:],
                 in_=rounded[:].rearrange("p c d -> p (c d)"),
             )
-            for j in range(n // P):
-                codes[slot0 // P + j, s] = (words, scales, j * P)
+            for x in range(width // P):
+                codes[slot0 // P + x, s] = (words, scales, x * P)
 
-        def multiply2(block, s):
-            e = block // BLOCKS
-            words, scales, base = codes[block, s]
+        def multiply2(group, s):
+            e = group // GROUPS
+            words, scales, base = codes[group, s]
             cols = slice(base, base + P)
             nc.tensor.matmul_mx(
-                out=dh[block][:],
+                out=dh[group][:],
                 lhsT=words[:, cols].bitcast(E5M2),
                 lhsT_scale=scales[:, cols],
                 rhs=w2_sb[e][:, s * W2_PASS_BYTES : (s + 1) * W2_PASS_BYTES].bitcast(E2M1),
@@ -197,69 +197,69 @@ def tile_moe_bdx_mlp_relu2_kernel(
                 stop=(s == PASSES - 1),
             )
 
-        def open_dh(block, b, passes):
-            dh[block] = bank(b)
+        def open_dh(group, b, passes):
+            dh[group] = bank(b)
             for s in range(passes):
-                multiply2(block, s)
+                multiply2(group, s)
 
         def paired(ap):
-            return ap.rearrange("p (u m d) -> p u m d", u=2, d=2)
+            return ap.rearrange("p (u m v) -> p u m v", u=2, v=2)
 
-        def dh_paired(block):
-            return dh[block][:].rearrange("p (m u d) -> p u m d", u=2, d=2)
+        def dh_paired(group):
+            return dh[group][:].rearrange("p (m u v) -> p u m v", u=2, v=2)
 
         def slope(e):
-            for q in range(BLOCKS):
-                block = e * BLOCKS + q
-                slopes[block] = place([P, H], F32, f"slope{block}", SLOPE_AT[block])
-                turned = bank(4 + q)
-                for j in range(PACK):
+            for within in range(GROUPS):
+                group = e * GROUPS + within
+                slopes[group] = place([P, H], F32, f"slope{group}", SLOPE_AT[group])
+                turned = bank(4 + within)
+                for d in range(PACK):
                     nc.tensor.transpose(
-                        turned[:, j * P : (j + 1) * P], a_sb[e][:, j, q * P : (q + 1) * P], ident[:]
+                        turned[:, d * P : (d + 1) * P], a_sb[e][:, d, within * P : (within + 1) * P], ident[:]
                     )
                 nc.scalar.activation(
-                    paired(slopes[block][:]),
-                    turned[:].rearrange("p (u d m) -> p u m d", u=2, d=2),
+                    paired(slopes[group][:]),
+                    turned[:].rearrange("p (u v m) -> p u m v", u=2, v=2),
                     RELU,
                     scale=2.0,
                 )
 
-        def times(block, dest):
-            products[block] = dest
-            nc.vector.tensor_tensor(paired(dest), dh_paired(block), paired(slopes[block][:]), MULT)
+        def times(group, dest):
+            products[group] = dest
+            nc.vector.tensor_tensor(paired(dest), dh_paired(group), paired(slopes[group][:]), MULT)
 
-        def times_in_ring(block):
-            times(block, product_pool.tile([P, H], BF16, name="product")[:])
+        def times_in_ring(group):
+            times(group, product_pool.tile([P, H], BF16, name="product")[:])
 
-        def park(block, dest):
-            nc.scalar.copy(paired(dest), dh_paired(block))
-            parked[block] = dest
+        def park(group, dest):
+            nc.scalar.copy(paired(dest), dh_paired(group))
+            parked[group] = dest
 
-        def times_on_gpsimd(block, dest):
-            products[block] = dest
-            nc.gpsimd.tensor_tensor(dest, parked[block], slopes[block][:], MULT)
+        def times_on_gpsimd(group, dest):
+            products[group] = dest
+            nc.gpsimd.tensor_tensor(dest, parked[group], slopes[group][:], MULT)
 
-        def turn(blocks, b, da, lo):
+        def turn(groups, b, da, lo):
             turned = bank(b)
-            for j, block in enumerate(blocks):
-                pairs = products[block].bitcast(F32)
+            for x, group in enumerate(groups):
+                pairs = products[group].bitcast(F32)
                 for u in range(2):
                     nc.tensor.transpose(
-                        turned[:, (2 * j + u) * P : (2 * j + u + 1) * P], pairs[:, u * P : (u + 1) * P], ident[:]
+                        turned[:, (2 * x + u) * P : (2 * x + u + 1) * P], pairs[:, u * P : (u + 1) * P], ident[:]
                     )
-            n = len(blocks) * P
+            width = len(groups) * P
             nc.scalar.copy(
-                da[:].bitcast(F32)[:, 2 * lo : 2 * (lo + n)].rearrange("p (j c u) -> p j c u", c=P, u=2),
-                turned[:, 0 : 2 * n].rearrange("p (j u c) -> p j c u", c=P, u=2),
+                da[:].bitcast(F32)[:, 2 * lo : 2 * (lo + width)].rearrange("p (x c u) -> p x c u", c=P, u=2),
+                turned[:, 0 : 2 * width].rearrange("p (x u c) -> p x c u", c=P, u=2),
             )
 
         def da_tile():
             return da_pool.tile([P, C * PACK], BF16, name="da", align_bytes=ALIGN)
 
         def quantise_da(da, words, scales, lo):
-            n = da.shape[1] // PACK
+            hi = lo + da.shape[1] // PACK
             nc.vector.quantize_mx(
-                out=words[:, lo : lo + n].bitcast(E5M2), scales=scales[:, lo : lo + n], in_=da[:]
+                out=words[:, lo:hi].bitcast(E5M2), scales=scales[:, lo:hi], in_=da[:]
             )
 
         def multiply1(e, b, words, scales, lo):
@@ -289,21 +289,21 @@ def tile_moe_bdx_mlp_relu2_kernel(
         quantise_g(rounded_01_0, 0, 0, ring_words(PAIR))
         rounded_01_2 = round_g(gathers(2, 0, PAIR, ROOM[0]), on_a(1, [P, PAIR, PACK], BF16))
         quantise_g(rounded_01_1, 1, 0, ring_words(PAIR))
-        for block in range(BLOCKS):
-            open_dh(block, block, 1)
-        for block in range(BLOCKS):
-            multiply2(block, 1)
+        for group in range(GROUPS):
+            open_dh(group, group, 1)
+        for group in range(GROUPS):
+            multiply2(group, 1)
         slope(2)
         dx_sb = on_a(0, [P, SLOTS], F32)
         rounded_23_0 = round_g(gathers(0, PAIR, PAIR, ROOM[1]), on_a(2, [P, PAIR, PACK], BF16))
         quantise_g(rounded_01_2, 2, 0, ring_words(PAIR))
         parked_01 = on_a(1, [P, 2 * H], F32)
-        for block in reversed(range(BLOCKS)):
-            multiply2(block, 2)
+        for group in reversed(range(GROUPS)):
+            multiply2(group, 2)
         park(3, parked_01[:, 0:H])
         slope(3)
-        for block in range(BLOCKS, 2 * BLOCKS):
-            open_dh(block, block, PASSES)
+        for group in range(GROUPS, 2 * GROUPS):
+            open_dh(group, group, PASSES)
         park(7, parked_01[:, H : 2 * H])
         rounded_23_1 = round_g(gathers(1, PAIR, PAIR, ROOM[0]), on_a(3, [P, PAIR, PACK], BF16))
         quantise_g(rounded_23_0, 0, PAIR, ring_words(PAIR))
@@ -311,25 +311,25 @@ def tile_moe_bdx_mlp_relu2_kernel(
         words03 = place([P, 2 * C], U32, "words03", ROOM[0] + 4 * PAIR)
         products_0 = place([P, 3 * H], BF16, "products_0", ROOM[1])
         times_on_gpsimd(3, on_a(2, [P, H], BF16)[:])
-        for block in range(3):
-            times(block, products_0[:, block * H : (block + 1) * H])
+        for group in range(3):
+            times(group, products_0[:, group * H : (group + 1) * H])
         da0 = da_tile()
         turn((0, 1), 0, da0, 0)
         turn((2, 3), 1, da0, HALF)
-        for block, b in zip(range(8, 12), (3, 2, 0, 1)):
-            open_dh(block, b, 1)
+        for group, b in zip(range(8, 12), (3, 2, 0, 1)):
+            open_dh(group, b, 1)
 
         rounded_2 = round_g(gathers(2, 2 * C, C, SLOPE_AT[1] + ALIGN - 4 * PACK * C), ring_tile(C))
         quantise_g(rounded_23_1, 1, PAIR, place([P, PAIR], U32, "words_23_1", ROOM[0] - ALIGN))
-        for block in range(8, 12):
-            multiply2(block, 1)
+        for group in range(8, 12):
+            multiply2(group, 1)
         open_dh(12, 7, 2)
         g32_3a = gathers(2, 3 * C, HALF, ROOM[1] - 4 * PACK * HALF)
         rounded_3a_at = ROOM[0] + 4 * PAIR + 4 * 2 * C
         rounded_3a = round_g(g32_3a, place([P, HALF, PACK], BF16, "rounded_3a", rounded_3a_at))
         quantise_g(rounded_2, 2, 2 * C, ring_words(C))
-        for block in (11, 8, 9, 10):
-            multiply2(block, 2)
+        for group in (11, 8, 9, 10):
+            multiply2(group, 2)
         parked_23 = on_a(3, [P, 2 * H], F32)
         park(11, parked_23[:, 0:H])
         open_dh(13, 1, 2)
@@ -343,8 +343,8 @@ def tile_moe_bdx_mlp_relu2_kernel(
 
         times_on_gpsimd(7, place([P, H], BF16, "product_7", rounded_3a_at)[:])
         products_1 = keep.tile([P, 3 * H], BF16, name=f"dy{PASSES - 1}_{PACK - 2}")
-        for block in range(4, 7):
-            times(block, products_1[:, (block - 4) * H : (block - 3) * H])
+        for group in range(4, 7):
+            times(group, products_1[:, (group - 4) * H : (group - 3) * H])
         da1 = da_tile()
         turn((4, 5), 4, da1, 0)
         open_dh(14, 5, 2)
@@ -375,7 +375,7 @@ def tile_moe_bdx_mlp_relu2_kernel(
         da_15 = keep.tile([P, P * PACK], BF16, name="da_15", align_bytes=ALIGN)
         turn((15,), 5, da_15, 0)
 
-        for e, da, words_on, scales_on, b in ((1, da1, 13, 10, 6), (2, da2, 14, 9, 7)):
+        for e, da, words_on, scales_on, b in ((1, da1, 14, 10, 6), (2, da2, 15, 9, 7)):
             words = place([P, C], U32, f"words{e}", SLOPE_AT[words_on])
             scales = place([P, C], U8, f"scales{e}", SLOPE_AT[scales_on])
             quantise_da(da, words, scales, 0)

@@ -37,10 +37,12 @@ ADD = mybir.AluOpType.add
 COPY = mybir.ActivationFunctionType.Copy
 RELU = mybir.ActivationFunctionType.Relu
 
-ROOM_BYTES = 4 * PACK * PAIR
+ROOM_BYTES = 4 * PACK * C
 SLOPE_BYTES = 4 * H
-ROOM = (SLOPE_BYTES, SLOPE_BYTES + ROOM_BYTES)
-SLOPE_AT = (0,) + tuple(ROOM[1] + ROOM_BYTES + x * SLOPE_BYTES for x in range(E * GROUPS - 1))
+KB = 1024
+ROOM = tuple(x * ROOM_BYTES for x in range(4))
+SLOPE_AT = tuple(4 * ROOM_BYTES + x * SLOPE_BYTES for x in range(E * GROUPS))
+A3_AT = SLOPE_AT[-1] + SLOPE_BYTES + 4 * KB
 
 
 def tile_moe_bdx_mlp_relu2_kernel(
@@ -50,10 +52,6 @@ def tile_moe_bdx_mlp_relu2_kernel(
     with ExitStack() as ctx:
         keep = ctx.enter_context(tc.tile_pool(name="keep", bufs=1))
         placed = ctx.enter_context(tc.tile_pool(name="placed", bufs=1))
-        rounded_pool = ctx.enter_context(tc.tile_pool(name="rounded_pool", bufs=2))
-        coded = ctx.enter_context(tc.tile_pool(name="coded", bufs=5))
-        product_pool = ctx.enter_context(tc.tile_pool(name="product_pool", bufs=4))
-        da_pool = ctx.enter_context(tc.tile_pool(name="da_pool", bufs=3))
         psum = ctx.enter_context(tc.psum_pool(name="psum", bufs=1))
 
         def bank(b):
@@ -65,13 +63,17 @@ def tile_moe_bdx_mlp_relu2_kernel(
         def on_a(e, shape, dtype):
             return keep.tile(shape, dtype, name=f"a{e}", align_bytes=ALIGN)
 
+        def on_plane(s, d, shape, dtype):
+            return keep.tile(shape, dtype, name=f"dy{s}_{d}", align_bytes=ALIGN)
+
+        def own(shape, dtype, name):
+            return keep.tile(shape, dtype, name=name, align_bytes=ALIGN)
+
         offs_sb = keep.tile([P, SLOTS // 16], U16, name="offs_sb")
         pos1_sb = keep.tile([P, T // 16], U16, name="pos1_sb")
         pos2_sb = keep.tile([P, T // 16], U16, name="pos2_sb")
-        gates = [keep.tile([P, PAIR], F32, name=f"gate{pair}") for pair in range(2)]
-        planes = [
-            [keep.tile([P, T + PAD], F32, name=f"dy{s}_{d}") for d in range(PACK)] for s in range(PASSES)
-        ]
+        gates = [own([P, PAIR], F32, f"gate{pair}") for pair in range(2)]
+        planes = [[on_plane(s, d, [P, T + PAD], F32) for d in range(PACK)] for s in range(PASSES)]
         w2_sb = [keep.tile([P, PASSES * W2_PASS_BYTES], U8, name=f"w2_{e}", align_bytes=ALIGN) for e in range(E)]
         w2_sc = keep.tile([P, E * PASSES * H], U8, name="w2_sc", align_bytes=ALIGN)
         w1_sb = keep.tile([P, E * W1_BYTES], U8, name="w1_sb", align_bytes=ALIGN)
@@ -103,7 +105,7 @@ def tile_moe_bdx_mlp_relu2_kernel(
             )
 
         def load_a(e):
-            a_sb[e] = on_a(e, [P, PACK, C], F32)
+            a_sb[e] = on_a(e, [P, PACK, C], F32) if e < E - 1 else place([P, PACK, C], F32, "a3", A3_AT)
             nc.sync.dma_start(
                 out=a_sb[e][:], in_=a[:, e * C : (e + 1) * C].rearrange("(p d) c -> p d c", d=PACK)
             )
@@ -124,15 +126,22 @@ def tile_moe_bdx_mlp_relu2_kernel(
             for d in range(PACK):
                 if (s, d) != (0, 0):
                     load_plane(s, d)
-            if s > 0:
-                load_a(s - 1)
+            if s == 1:
+                load_a(0)
+                load_a(1)
         load_gate(PAIR, SLOTS)
-        load_scales(w2_sc, w2_scales, E * PASSES)
-        load_w2(0)
         load_a(2)
         load_a(3)
-        for e in range(1, E):
+        load_scales(w2_sc, w2_scales, E * PASSES)
+        for e in range(E):
             load_w2(e)
+        load_scales(w1_sc, w1_scales, E)
+        nc.sync.dma_start(
+            out=w1_sb[:].bitcast(I32).rearrange("p (e w) -> p e w", e=E),
+            in_=w1_words.bitcast(I32).rearrange("e s p w -> p (e s) w"),
+        )
+        nc.sync.dma_start(pos1_sb[:], pos1)
+        nc.sync.dma_start(pos2_sb[:], pos2)
 
         codes = {}
         dh = {}
@@ -158,30 +167,35 @@ def tile_moe_bdx_mlp_relu2_kernel(
                     gather(g32, s, d, slot0, lo, hi)
             return g32
 
-        def ring_tile(width):
-            return rounded_pool.tile([P, width, PACK], BF16, name="rounded", align_bytes=ALIGN)
+        def plain_gathers(s, slot0, at):
+            g32 = place([P, PACK, C], F32, f"g32_{s}_{slot0}", at)
+            for d in range(PACK):
+                nc.vector.tensor_copy(
+                    g32[:, d, :], planes[s][d][:].indirect(offs_sb[:, slot0 // 16 : (slot0 + C) // 16])
+                )
+            return g32
 
         def round_g(g32, rounded):
             nc.scalar.activation(
-                rounded[:].rearrange("p (c r) d -> p c d r", r=4),
+                rounded.rearrange("p (c r) d -> p c d r", r=4),
                 g32[:].rearrange("p d (c r) -> p c d r", r=4),
                 COPY,
             )
+
+        def rounded_piece(s, slot0, width, at, rounded):
+            round_g(gathers(s, slot0, width, at), rounded[:])
             return rounded
 
-        def ring_words(width):
-            return coded.tile([P, width], U32, name="g_words", align_bytes=ALIGN)
-
-        def quantise_g(rounded, s, slot0, words):
-            width = rounded.shape[1]
-            scales = coded.tile([P, width], U8, name="g_scales", align_bytes=ALIGN)
-            nc.vector.quantize_mx(
-                out=words[:].bitcast(E5M2),
-                scales=scales[:],
-                in_=rounded[:].rearrange("p c d -> p (c d)"),
-            )
+        def quantise_g(rounded, s, slot0, words, scales_at=None):
+            width = words.shape[1]
+            name = f"g_scales_{s}_{slot0}"
+            scales = own([P, width], U8, name) if scales_at is None else place([P, width], U8, name, scales_at)
+            nc.vector.quantize_mx(out=words[:, 0:width].bitcast(E5M2), scales=scales[:], in_=rounded)
             for x in range(width // P):
                 codes[slot0 // P + x, s] = (words, scales, x * P)
+
+        def flat(rounded):
+            return rounded[:].rearrange("p c d -> p (c d)")
 
         def multiply2(group, s):
             e = group // GROUPS
@@ -212,7 +226,7 @@ def tile_moe_bdx_mlp_relu2_kernel(
             for within in range(GROUPS):
                 group = e * GROUPS + within
                 slopes[group] = place([P, H], F32, f"slope{group}", SLOPE_AT[group])
-                turned = bank(4 + within)
+                turned = bank(4 * (1 - e % 2) + within)
                 for d in range(PACK):
                     nc.tensor.transpose(
                         turned[:, d * P : (d + 1) * P], a_sb[e][:, d, within * P : (within + 1) * P], ident[:]
@@ -228,9 +242,6 @@ def tile_moe_bdx_mlp_relu2_kernel(
             products[group] = dest
             nc.vector.tensor_tensor(paired(dest), dh_paired(group), paired(slopes[group][:]), MULT)
 
-        def times_in_ring(group):
-            times(group, product_pool.tile([P, H], BF16, name="product")[:])
-
         def park(group, dest):
             nc.scalar.copy(paired(dest), dh_paired(group))
             parked[group] = dest
@@ -239,22 +250,43 @@ def tile_moe_bdx_mlp_relu2_kernel(
             products[group] = dest
             nc.gpsimd.tensor_tensor(dest, parked[group], slopes[group][:], MULT)
 
-        def turn(groups, b, da, lo):
+        def turn(sources, b, da, lo):
             turned = bank(b)
-            for x, group in enumerate(groups):
-                pairs = products[group].bitcast(F32)
+            for x, source in enumerate(sources):
+                pairs = source.bitcast(F32)
                 for u in range(2):
                     nc.tensor.transpose(
                         turned[:, (2 * x + u) * P : (2 * x + u + 1) * P], pairs[:, u * P : (u + 1) * P], ident[:]
                     )
-            width = len(groups) * P
+            width = len(sources) * P
             nc.scalar.copy(
                 da[:].bitcast(F32)[:, 2 * lo : 2 * (lo + width)].rearrange("p (x c u) -> p x c u", c=P, u=2),
                 turned[:, 0 : 2 * width].rearrange("p (x u c) -> p x c u", c=P, u=2),
             )
 
-        def da_tile():
-            return da_pool.tile([P, C * PACK], BF16, name="da", align_bytes=ALIGN)
+        def turn_da(groups, b, da, lo):
+            turn([products[group] for group in groups], b, da, lo)
+
+        def gate_turned(g32, e, gated, rounded, there, back, order):
+            banks = [bank(b) for b in there]
+            for within, d in order:
+                nc.tensor.transpose(
+                    banks[within][:, d * P : (d + 1) * P], g32[:, d, within * P : (within + 1) * P], ident[:]
+                )
+            for within in range(GROUPS):
+                column = (e - 2) * GROUPS + within
+                nc.scalar.activation(
+                    paired(gated[:, within, :]),
+                    banks[within][:].rearrange("p (u v m) -> p u m v", u=2, v=2),
+                    COPY,
+                    scale=gate_columns[:, column : column + 1],
+                )
+            for half in range(2):
+                turn([gated[:, 2 * half, :], gated[:, 2 * half + 1, :]], back[half], rounded, half * HALF)
+            return rounded
+
+        by_plane = [(within, d) for d in range(PACK) for within in range(GROUPS)]
+        by_group = [(within, d) for within in range(GROUPS) for d in range(PACK)]
 
         def quantise_da(da, words, scales, lo):
             hi = lo + da.shape[1] // PACK
@@ -275,116 +307,135 @@ def tile_moe_bdx_mlp_relu2_kernel(
             )
             return dx
 
-        rounded_01_0 = round_g(gathers(0, 0, PAIR, ROOM[0]), ring_tile(PAIR))
-        rounded_01_1 = round_g(gathers(1, 0, PAIR, ROOM[1]), ring_tile(PAIR))
+        rounded_01_0 = rounded_piece(0, 0, PAIR, ROOM[0], place([P, PAIR, PACK], BF16, "rounded_01_0", A3_AT + 8 * KB))
         slope(0)
         slope(1)
-        load_scales(w1_sc, w1_scales, E)
-        nc.sync.dma_start(
-            out=w1_sb[:].bitcast(I32).rearrange("p (e w) -> p e w", e=E),
-            in_=w1_words.bitcast(I32).rearrange("e s p w -> p (e s) w"),
-        )
-        nc.sync.dma_start(pos1_sb[:], pos1)
-        nc.sync.dma_start(pos2_sb[:], pos2)
-        quantise_g(rounded_01_0, 0, 0, ring_words(PAIR))
-        rounded_01_2 = round_g(gathers(2, 0, PAIR, ROOM[0]), on_a(1, [P, PAIR, PACK], BF16))
-        quantise_g(rounded_01_1, 1, 0, ring_words(PAIR))
-        for group in range(GROUPS):
-            open_dh(group, group, 1)
-        for group in range(GROUPS):
-            multiply2(group, 1)
+        rounded_01_1 = rounded_piece(1, 0, PAIR, ROOM[2], on_a(1, [P, PAIR, PACK], BF16))
+        quantise_g(flat(rounded_01_0), 0, 0, own([P, PAIR], U32, "words_01_0"))
+        gate_columns = keep.tile([P, 2 * GROUPS], F32, name="gate_columns")
+        for half in range(2):
+            turned = bank(4 + half)
+            for within in range(GROUPS):
+                at = (half * GROUPS + within) * P
+                nc.tensor.transpose(turned[:, within * P : (within + 1) * P], gates[1][:, at : at + P], ident[:])
+            nc.scalar.copy(gate_columns[:, half * GROUPS : (half + 1) * GROUPS], turned[:, 0:512:P])
         slope(2)
-        dx_sb = on_a(0, [P, SLOTS], F32)
-        rounded_23_0 = round_g(gathers(0, PAIR, PAIR, ROOM[1]), on_a(2, [P, PAIR, PACK], BF16))
-        quantise_g(rounded_01_2, 2, 0, ring_words(PAIR))
-        parked_01 = on_a(1, [P, 2 * H], F32)
-        for group in reversed(range(GROUPS)):
-            multiply2(group, 2)
-        park(3, parked_01[:, 0:H])
         slope(3)
-        for group in range(GROUPS, 2 * GROUPS):
-            open_dh(group, group, PASSES)
-        park(7, parked_01[:, H : 2 * H])
-        rounded_23_1 = round_g(gathers(1, PAIR, PAIR, ROOM[0]), on_a(3, [P, PAIR, PACK], BF16))
-        quantise_g(rounded_23_0, 0, PAIR, ring_words(PAIR))
+        rounded_01_2 = rounded_piece(2, 0, PAIR, ROOM[0], place([P, PAIR, PACK], BF16, "rounded_01_2", A3_AT - 4 * KB))
+        quantise_g(flat(rounded_01_1), 1, 0, own([P, PAIR], U32, "words_01_1"))
+        for group in range(2 * GROUPS):
+            open_dh(group, group, 2)
+        dx_sb = on_a(0, [P, SLOTS], F32)
 
-        words03 = place([P, 2 * C], U32, "words03", ROOM[0] + 4 * PAIR)
-        products_0 = place([P, 3 * H], BF16, "products_0", ROOM[1])
-        times_on_gpsimd(3, on_a(2, [P, H], BF16)[:])
-        for group in range(3):
-            times(group, products_0[:, group * H : (group + 1) * H])
-        da0 = da_tile()
-        turn((0, 1), 0, da0, 0)
-        turn((2, 3), 1, da0, HALF)
-        for group, b in zip(range(8, 12), (3, 2, 0, 1)):
-            open_dh(group, b, 1)
+        rounded_2_0 = rounded_piece(
+            0, 2 * C, C, ROOM[2], place([P, C, PACK], BF16, "rounded_2_0", A3_AT + 4 * KB)
+        )
+        quantise_g(flat(rounded_01_2), 2, 0, own([P, PAIR], U32, "words_01_2"))
+        g32_3_0 = gathers(0, 3 * C, C, ROOM[0])
+        parked_0 = on_a(2, [P, GROUPS * H], F32)
+        parked_1 = on_a(1, [P, 3 * H], F32)
+        for group in range(2 * GROUPS):
+            multiply2(group, 2)
+        for group in range(GROUPS):
+            park(group, parked_0[:, group * H : (group + 1) * H])
+        for group in range(4, 7):
+            park(group, parked_1[:, (group - 4) * H : (group - 3) * H])
+        rounded_3_0 = own([P, C, PACK], BF16, "words_01_2")
+        round_g(g32_3_0, rounded_3_0[:])
 
-        rounded_2 = round_g(gathers(2, 2 * C, C, SLOPE_AT[1] + ALIGN - 4 * PACK * C), ring_tile(C))
-        quantise_g(rounded_23_1, 1, PAIR, place([P, PAIR], U32, "words_23_1", ROOM[0] - ALIGN))
-        for group in range(8, 12):
-            multiply2(group, 1)
-        open_dh(12, 7, 2)
-        g32_3a = gathers(2, 3 * C, HALF, ROOM[1] - 4 * PACK * HALF)
-        rounded_3a_at = ROOM[0] + 4 * PAIR + 4 * 2 * C
-        rounded_3a = round_g(g32_3a, place([P, HALF, PACK], BF16, "rounded_3a", rounded_3a_at))
-        quantise_g(rounded_2, 2, 2 * C, ring_words(C))
+        g32_2_1 = plain_gathers(1, 2 * C, ROOM[1])
+        g32_3_1 = plain_gathers(1, 3 * C, ROOM[2])
+        products_0 = on_plane(0, 3, [P, GROUPS * H], BF16)
+        products_1 = on_plane(0, 2, [P, GROUPS * H], BF16)
+        for group in range(GROUPS):
+            times_on_gpsimd(group, products_0[:, group * H : (group + 1) * H])
+        for group in range(4, 7):
+            times_on_gpsimd(group, products_1[:, (group - 4) * H : (group - 3) * H])
+        times(7, products_1[:, 3 * H : 4 * H])
+        rounded_2_1 = gate_turned(
+            g32_2_1, 2, on_plane(0, 0, [P, GROUPS, H], BF16),
+            place([P, C * PACK], BF16, "rounded_2_1", A3_AT - 4 * KB),
+            (0, 1, 2, 3), (4, 5), by_plane,
+        )
+        da0 = on_a(3, [P, C * PACK], BF16)
+        turn_da((0, 1), 1, da0, 0)
+        turn_da((2, 3), 0, da0, HALF)
+        rounded_3_1 = gate_turned(
+            g32_3_1, 3, place([P, GROUPS, H], BF16, "gated_3", ROOM[3]), own([P, C * PACK], BF16, "gate0"),
+            (4, 1, 5, 0), (6, 7), by_group,
+        )
+        da1 = on_plane(1, 1, [P, C * PACK], BF16)
+        turn_da((4, 5), 4, da1, 0)
+        turn_da((6, 7), 1, da1, HALF)
+
+        rounded_2 = rounded_piece(
+            2, 2 * C, C, ROOM[0], place([P, C, PACK], BF16, "rounded_2", ROOM[3] + 2 * KB)
+        )
+        words_23_0 = on_plane(1, 2, [P, PAIR], U32)
+        quantise_g(flat(rounded_2_0), 0, 2 * C, words_23_0[:, 0:C], ROOM[3] + KB)
+        quantise_g(flat(rounded_3_0), 0, 3 * C, words_23_0[:, C:PAIR], ROOM[3] + KB + C)
+        quantise_g(rounded_2_1[:], 1, 2 * C, on_plane(1, 3, [P, C], U32))
+        for group, b in zip(range(8, 12), (2, 3, 5, 0)):
+            open_dh(group, b, 2)
+        quantise_g(rounded_3_1[:], 1, 3 * C, own([P, C], U32, "words_3_1"))
+        for group, b in zip(range(12, 16), (4, 1, 6, 7)):
+            open_dh(group, b, 2)
+        rounded_3a = rounded_piece(
+            2, 3 * C, HALF, ROOM[3] - 3 * KB, place([P, HALF, PACK], BF16, "rounded_3a", ROOM[1])
+        )
+        quantise_g(flat(rounded_2), 2, 2 * C, own([P, C], U32, "words_2_2"))
         for group in (11, 8, 9, 10):
             multiply2(group, 2)
-        parked_23 = on_a(3, [P, 2 * H], F32)
+        parked_23 = on_a(2, [P, 2 * H], F32)
         park(11, parked_23[:, 0:H])
-        open_dh(13, 1, 2)
-        rounded_3b = round_g(
-            gathers(2, 3 * C + HALF, HALF, SLOPE_AT[1] - 4 * PACK * HALF), on_a(2, [P, HALF, PACK], BF16)
+        rounded_3b = rounded_piece(
+            2, 3 * C + HALF, HALF, ROOM[0], place([P, HALF, PACK], BF16, "rounded_3b", ROOM[1] + 2 * KB)
         )
-        quantise_g(rounded_3a, 2, 3 * C, ring_words(HALF))
+        quantise_g(flat(rounded_3a), 2, 3 * C, own([P, HALF], U32, "words_3a"))
         multiply2(12, 2)
         multiply2(13, 2)
         park(12, parked_23[:, H : 2 * H])
-
-        times_on_gpsimd(7, place([P, H], BF16, "product_7", rounded_3a_at)[:])
-        products_1 = keep.tile([P, 3 * H], BF16, name=f"dy{PASSES - 1}_{PACK - 2}")
-        for group in range(4, 7):
-            times(group, products_1[:, (group - 4) * H : (group - 3) * H])
-        da1 = da_tile()
-        turn((4, 5), 4, da1, 0)
-        open_dh(14, 5, 2)
-        turn((6, 7), 6, da1, HALF)
-        open_dh(15, 4, 2)
+        words03 = place([P, 2 * C], U32, "words03", ROOM[3] - 4 * KB)
+        words1 = place([P, C], U32, "words1", ROOM[3])
+        scales1 = own([P, C], U8, "scales1")
         quantise_da(da0, words03, scales03, 0)
-        quantise_g(rounded_3b, 2, 3 * C + HALF, ring_words(HALF))
+        quantise_da(da1, words1, scales1, 0)
+        quantise_g(flat(rounded_3b), 2, 3 * C + HALF, own([P, HALF], U32, "words_3b"))
         multiply2(14, 2)
         multiply2(15, 2)
+        nc.scalar.copy(dx_sb[:, 0:C], multiply1(0, 0, words03, scales03, 0)[:])
+        nc.scalar.copy(dx_sb[:, C : 2 * C], multiply1(1, 4, words1, scales1, 0)[:])
 
-        products_gpsimd = on_a(2, [P, 2 * H], BF16)
+        products_gpsimd = place([P, 2 * H], BF16, "products_gpsimd", ROOM[1] + 2 * KB)
         times_on_gpsimd(11, products_gpsimd[:, 0:H])
         times_on_gpsimd(12, products_gpsimd[:, H : 2 * H])
-        nc.scalar.copy(dx_sb[:, 0:C], multiply1(0, 7, words03, scales03, 0)[:])
-        da2 = da_tile()
-        times_in_ring(8)
-        times_in_ring(9)
-        turn((8, 9), 3, da2, 0)
-        times_in_ring(10)
-        turn((10, 11), 2, da2, HALF)
-        times_in_ring(13)
-        da_12_13 = keep.tile([P, HALF * PACK], BF16, name="da_12_13", align_bytes=ALIGN)
-        turn((12, 13), 0, da_12_13, 0)
-        times_in_ring(14)
-        da_14 = keep.tile([P, P * PACK], BF16, name="da_14", align_bytes=ALIGN)
-        turn((14,), 1, da_14, 0)
-        times_in_ring(15)
-        da_15 = keep.tile([P, P * PACK], BF16, name="da_15", align_bytes=ALIGN)
-        turn((15,), 5, da_15, 0)
+        products_held = place([P, 4 * H], BF16, "products_held", ROOM[0])
+        products_last = place([P, 2 * H], BF16, "products_last", ROOM[0] + 4 * KB)
+        da2 = on_plane(2, 0, [P, C * PACK], BF16)
+        times(8, products_held[:, 0:H])
+        times(9, products_held[:, H : 2 * H])
+        turn_da((8, 9), 2, da2, 0)
+        times(10, products_held[:, 2 * H : 3 * H])
+        turn_da((10, 11), 3, da2, HALF)
+        times(13, products_held[:, 3 * H : 4 * H])
+        da_12_13 = on_plane(2, 1, [P, HALF * PACK], BF16)
+        turn_da((12, 13), 5, da_12_13, 0)
+        times(14, products_last[:, 0:H])
+        da_14 = on_plane(2, 2, [P, P * PACK], BF16)
+        turn_da((14,), 1, da_14, 0)
+        times(15, products_last[:, H : 2 * H])
+        da_15 = on_plane(2, 3, [P, P * PACK], BF16)
+        turn_da((15,), 6, da_15, 0)
 
-        for e, da, words_on, scales_on, b in ((1, da1, 14, 10, 6), (2, da2, 15, 9, 7)):
-            words = place([P, C], U32, f"words{e}", SLOPE_AT[words_on])
-            scales = place([P, C], U8, f"scales{e}", SLOPE_AT[scales_on])
-            quantise_da(da, words, scales, 0)
-            nc.scalar.copy(dx_sb[:, e * C : (e + 1) * C], multiply1(e, b, words, scales, 0)[:])
+        words2 = place([P, C], U32, "words2", SLOPE_AT[14])
+        scales2 = own([P, C], U8, "scales2")
+        quantise_da(da2, words2, scales2, 0)
+        nc.scalar.copy(dx_sb[:, 2 * C : 3 * C], multiply1(2, 0, words2, scales2, 0)[:])
         quantise_da(da_12_13, words03, scales03, C)
         quantise_da(da_14, words03, scales03, C + HALF)
-        dx_12_14 = multiply1(3, 3, words03, scales03, C - P)
+        dx_12_14 = multiply1(3, 4, words03, scales03, C - P)
         quantise_da(da_15, words03, scales03, 2 * C - P)
-        dx_15 = multiply1(3, 0, words03, scales03, C)
+        dx_15 = multiply1(3, 2, words03, scales03, C)
         nc.vector.tensor_copy(dx_sb[:, 3 * C : SLOTS - P], dx_12_14[:, P:C])
         nc.scalar.copy(dx_sb[:, SLOTS - P : SLOTS], dx_15[:, C - P : C])
 

@@ -37,12 +37,17 @@ ADD = mybir.AluOpType.add
 COPY = mybir.ActivationFunctionType.Copy
 RELU = mybir.ActivationFunctionType.Relu
 
-ROOM_BYTES = 4 * PACK * C
-SLOPE_BYTES = 4 * H
 KB = 1024
-ROOM = tuple(x * ROOM_BYTES for x in range(4))
-SLOPE_AT = tuple(4 * ROOM_BYTES + x * SLOPE_BYTES for x in range(E * GROUPS))
-A3_AT = SLOPE_AT[-1] + SLOPE_BYTES + 4 * KB
+ROOM0, ROOM1 = 0, 16 * KB
+WORDS0, WORDS1 = 32 * KB, 36 * KB
+PARKED_0 = 131 * KB
+PRODUCTS_1 = 44 * KB
+DA0 = 48 * KB
+A_AT = (52 * KB, 61 * KB, 69 * KB, 77 * KB)
+ROUNDED_01_0 = 85 * KB
+GATE0 = 93 * KB
+SLOPES = 99 * KB
+EXPERT_SLOPE_BYTES = 8 * KB
 
 
 def tile_moe_bdx_mlp_relu2_kernel(
@@ -54,32 +59,33 @@ def tile_moe_bdx_mlp_relu2_kernel(
         placed = ctx.enter_context(tc.tile_pool(name="placed", bufs=1))
         psum = ctx.enter_context(tc.psum_pool(name="psum", bufs=1))
 
-        def bank(b):
-            return psum.tile([P, 512], F32, name=f"bank{b}")
+        banks = [psum.tile([P, 512], F32, name=f"bank{b}") for b in range(8)]
 
-        def place(shape, dtype, name, at):
-            return placed.tile(shape, dtype, name=name, offset=at, align_bytes=ALIGN)
+        def place(width, dtype, name, at):
+            return placed.tile([P, width], dtype, name=name, offset=at, align_bytes=ALIGN)
 
-        def on_a(e, shape, dtype):
-            return keep.tile(shape, dtype, name=f"a{e}", align_bytes=ALIGN)
+        def on_plane(s, d, width, dtype):
+            return keep.tile([P, width], dtype, name=f"dy{s}_{d}", align_bytes=ALIGN)
 
-        def on_plane(s, d, shape, dtype):
-            return keep.tile(shape, dtype, name=f"dy{s}_{d}", align_bytes=ALIGN)
+        def own(width, dtype, name):
+            return keep.tile([P, width], dtype, name=name, align_bytes=ALIGN)
 
-        def own(shape, dtype, name):
-            return keep.tile(shape, dtype, name=name, align_bytes=ALIGN)
+        def by_plane(ap):
+            return ap.rearrange("p (d c) -> p d c", d=PACK)
 
         offs_sb = keep.tile([P, SLOTS // 16], U16, name="offs_sb")
         pos1_sb = keep.tile([P, T // 16], U16, name="pos1_sb")
         pos2_sb = keep.tile([P, T // 16], U16, name="pos2_sb")
-        gates = [own([P, PAIR], F32, f"gate{pair}") for pair in range(2)]
-        planes = [[on_plane(s, d, [P, T + PAD], F32) for d in range(PACK)] for s in range(PASSES)]
-        w2_sb = [keep.tile([P, PASSES * W2_PASS_BYTES], U8, name=f"w2_{e}", align_bytes=ALIGN) for e in range(E)]
-        w2_sc = keep.tile([P, E * PASSES * H], U8, name="w2_sc", align_bytes=ALIGN)
-        w1_sb = keep.tile([P, E * W1_BYTES], U8, name="w1_sb", align_bytes=ALIGN)
-        w1_sc = keep.tile([P, E * K], U8, name="w1_sc", align_bytes=ALIGN)
+        gates = [place(PAIR, F32, "gate0", GATE0), own(PAIR, F32, "gate1")]
+        gate_columns = own(2 * GROUPS, F32, "gate_columns")
+        planes = [[on_plane(s, d, T + PAD, F32) for d in range(PACK)] for s in range(PASSES)]
+        w2_sb = [own(PASSES * W2_PASS_BYTES, U8, f"w2_{e}") for e in range(E)]
+        w2_sc = own(E * PASSES * H, U8, "w2_sc")
+        w1_sb = own(E * W1_BYTES, U8, "w1_sb")
+        w1_sc = own(E * K, U8, "w1_sc")
         ident = keep.tile([P, P], F32, name="ident")
-        scales03 = keep.tile([P, 2 * C], U8, name="scales03", align_bytes=ALIGN)
+        a_sb = [place(PACK * C, F32, f"a{e}", A_AT[e]) for e in range(E)]
+        slopes = [place(GROUPS * H, F32, f"slopes{e}", SLOPES + e * EXPERT_SLOPE_BYTES) for e in range(E)]
 
         for s in range(PASSES):
             for d in range(PACK):
@@ -89,7 +95,6 @@ def tile_moe_bdx_mlp_relu2_kernel(
         make_identity(nc, ident[:])
 
         dy_rows = dyT.rearrange("(s p d) t -> s d p t", p=P, d=PACK)
-        a_sb = {}
 
         def load_plane(s, d):
             nc.sync.dma_start(out=planes[s][d][:, 0:T], in_=dy_rows[s, d])
@@ -105,9 +110,8 @@ def tile_moe_bdx_mlp_relu2_kernel(
             )
 
         def load_a(e):
-            a_sb[e] = on_a(e, [P, PACK, C], F32) if e < E - 1 else place([P, PACK, C], F32, "a3", A3_AT)
             nc.sync.dma_start(
-                out=a_sb[e][:], in_=a[:, e * C : (e + 1) * C].rearrange("(p d) c -> p d c", d=PACK)
+                out=by_plane(a_sb[e][:]), in_=a[:, e * C : (e + 1) * C].rearrange("(p d) c -> p d c", d=PACK)
             )
 
         def load_scales(tile, source, runs):
@@ -135,6 +139,8 @@ def tile_moe_bdx_mlp_relu2_kernel(
         load_scales(w2_sc, w2_scales, E * PASSES)
         for e in range(E):
             load_w2(e)
+        with nc.allow_non_contiguous_dma(reason="one gate value a partition"):
+            nc.sync.dma_start(out=gate_columns[:], in_=gate[P, PAIR:SLOTS].rearrange("(x p) -> p x", p=P))
         load_scales(w1_sc, w1_scales, E)
         nc.sync.dma_start(
             out=w1_sb[:].bitcast(I32).rearrange("p (e w) -> p e w", e=E),
@@ -145,76 +151,62 @@ def tile_moe_bdx_mlp_relu2_kernel(
 
         codes = {}
         dh = {}
-        slopes = {}
+        done = {}
         products = {}
-        parked = {}
 
-        def gather(g32, s, d, slot0, lo, hi):
-            start = slot0 + lo
-            base = start % PAIR
-            nc.vector.tensor_tensor(
-                g32[:, d, lo:hi],
-                planes[s][d][:].indirect(offs_sb[:, start // 16 : (slot0 + hi) // 16]),
-                gates[start // PAIR][:, base : base + hi - lo],
-                MULT,
-            )
-
-        def gathers(s, slot0, width, at):
-            g32 = place([P, PACK, width], F32, f"g32_{s}_{slot0}", at)
+        def gathers(s, slot0, room):
+            g32 = by_plane(room)
+            width = g32.shape[2]
             for d in range(PACK):
                 cuts = FIRST_CUTS if (s, slot0, d) == (0, 0, 0) else (0, width)
                 for lo, hi in zip(cuts, cuts[1:]):
-                    gather(g32, s, d, slot0, lo, hi)
+                    start = slot0 + lo
+                    base = start % PAIR
+                    nc.vector.tensor_tensor(
+                        g32[:, d, lo:hi],
+                        planes[s][d][:].indirect(offs_sb[:, start // 16 : (slot0 + hi) // 16]),
+                        gates[start // PAIR][:, base : base + hi - lo],
+                        MULT,
+                    )
             return g32
 
-        def plain_gathers(s, slot0, at):
-            g32 = place([P, PACK, C], F32, f"g32_{s}_{slot0}", at)
+        def plain_gathers(s, slot0, room):
+            g32 = by_plane(room)
+            width = g32.shape[2]
             for d in range(PACK):
                 nc.vector.tensor_copy(
-                    g32[:, d, :], planes[s][d][:].indirect(offs_sb[:, slot0 // 16 : (slot0 + C) // 16])
+                    g32[:, d, :], planes[s][d][:].indirect(offs_sb[:, slot0 // 16 : (slot0 + width) // 16])
                 )
             return g32
 
         def round_g(g32, rounded):
             nc.scalar.activation(
-                rounded.rearrange("p (c r) d -> p c d r", r=4),
-                g32[:].rearrange("p d (c r) -> p c d r", r=4),
+                rounded.rearrange("p (c r d) -> p c d r", r=4, d=PACK),
+                g32.rearrange("p d (c r) -> p c d r", r=4),
                 COPY,
             )
 
-        def rounded_piece(s, slot0, width, at, rounded):
-            round_g(gathers(s, slot0, width, at), rounded[:])
-            return rounded
-
-        def quantise_g(rounded, s, slot0, words, scales_at=None):
+        def quantise_g(rounded, s, slot0, words):
             width = words.shape[1]
-            name = f"g_scales_{s}_{slot0}"
-            scales = own([P, width], U8, name) if scales_at is None else place([P, width], U8, name, scales_at)
-            nc.vector.quantize_mx(out=words[:, 0:width].bitcast(E5M2), scales=scales[:], in_=rounded)
+            scales = own(width, U8, f"g_scales_{s}_{slot0}")
+            nc.vector.quantize_mx(out=words.bitcast(E5M2), scales=scales[:], in_=rounded)
             for x in range(width // P):
-                codes[slot0 // P + x, s] = (words, scales, x * P)
-
-        def flat(rounded):
-            return rounded[:].rearrange("p c d -> p (c d)")
+                codes[slot0 // P + x, s] = (words[:, x * P : (x + 1) * P], scales[:, x * P : (x + 1) * P])
 
         def multiply2(group, s):
             e = group // GROUPS
-            words, scales, base = codes[group, s]
-            cols = slice(base, base + P)
+            words, scales = codes[group, s]
+            before = done.get(group, 0)
+            done[group] = before + 1
             nc.tensor.matmul_mx(
                 out=dh[group][:],
-                lhsT=words[:, cols].bitcast(E5M2),
-                lhsT_scale=scales[:, cols],
+                lhsT=words.bitcast(E5M2),
+                lhsT_scale=scales,
                 rhs=w2_sb[e][:, s * W2_PASS_BYTES : (s + 1) * W2_PASS_BYTES].bitcast(E2M1),
                 rhs_scale=w2_sc[:, (e * PASSES + s) * H : (e * PASSES + s + 1) * H],
-                start=(s == 0),
-                stop=(s == PASSES - 1),
+                start=(before == 0),
+                stop=(before == PASSES - 1),
             )
-
-        def open_dh(group, b, passes):
-            dh[group] = bank(b)
-            for s in range(passes):
-                multiply2(group, s)
 
         def paired(ap):
             return ap.rearrange("p (u m v) -> p u m v", u=2, v=2)
@@ -222,17 +214,19 @@ def tile_moe_bdx_mlp_relu2_kernel(
         def dh_paired(group):
             return dh[group][:].rearrange("p (m u v) -> p u m v", u=2, v=2)
 
-        def slope(e):
+        def of_group(tile, within):
+            return tile[:, within * H : (within + 1) * H]
+
+        def slope(e, first_bank):
+            source = by_plane(a_sb[e][:])
             for within in range(GROUPS):
-                group = e * GROUPS + within
-                slopes[group] = place([P, H], F32, f"slope{group}", SLOPE_AT[group])
-                turned = bank(4 * (1 - e % 2) + within)
+                turned = banks[first_bank + within]
                 for d in range(PACK):
                     nc.tensor.transpose(
-                        turned[:, d * P : (d + 1) * P], a_sb[e][:, d, within * P : (within + 1) * P], ident[:]
+                        turned[:, d * P : (d + 1) * P], source[:, d, within * P : (within + 1) * P], ident[:]
                     )
                 nc.scalar.activation(
-                    paired(slopes[group][:]),
+                    paired(of_group(slopes[e], within)),
                     turned[:].rearrange("p (u v m) -> p u m v", u=2, v=2),
                     RELU,
                     scale=2.0,
@@ -240,18 +234,21 @@ def tile_moe_bdx_mlp_relu2_kernel(
 
         def times(group, dest):
             products[group] = dest
-            nc.vector.tensor_tensor(paired(dest), dh_paired(group), paired(slopes[group][:]), MULT)
+            nc.vector.tensor_tensor(
+                paired(dest), dh_paired(group), paired(of_group(slopes[group // GROUPS], group % GROUPS)), MULT
+            )
 
-        def park(group, dest):
-            nc.scalar.copy(paired(dest), dh_paired(group))
-            parked[group] = dest
+        def park(e, parked):
+            for within in range(GROUPS):
+                nc.scalar.copy(paired(of_group(parked, within)), dh_paired(e * GROUPS + within))
 
-        def times_on_gpsimd(group, dest):
-            products[group] = dest
-            nc.gpsimd.tensor_tensor(dest, parked[group], slopes[group][:], MULT)
+        def times_on_gpsimd(e, parked, dest):
+            for within in range(GROUPS):
+                products[e * GROUPS + within] = of_group(dest, within)
+            nc.gpsimd.tensor_tensor(dest[:], parked[:], slopes[e][:], MULT)
 
-        def turn(sources, b, da, lo):
-            turned = bank(b)
+        def turn(sources, b, dest):
+            turned = banks[b]
             for x, source in enumerate(sources):
                 pairs = source.bitcast(F32)
                 for u in range(2):
@@ -260,44 +257,45 @@ def tile_moe_bdx_mlp_relu2_kernel(
                     )
             width = len(sources) * P
             nc.scalar.copy(
-                da[:].bitcast(F32)[:, 2 * lo : 2 * (lo + width)].rearrange("p (x c u) -> p x c u", c=P, u=2),
+                dest.bitcast(F32).rearrange("p (x c u) -> p x c u", c=P, u=2),
                 turned[:, 0 : 2 * width].rearrange("p (x u c) -> p x c u", c=P, u=2),
             )
 
-        def turn_da(groups, b, da, lo):
-            turn([products[group] for group in groups], b, da, lo)
+        def turn_da(groups, b, dest):
+            turn([products[group] for group in groups], b, dest)
 
-        def gate_turned(g32, e, gated, rounded, there, back, order):
-            banks = [bank(b) for b in there]
+        def turn_slots(g32, there, order):
             for within, d in order:
                 nc.tensor.transpose(
-                    banks[within][:, d * P : (d + 1) * P], g32[:, d, within * P : (within + 1) * P], ident[:]
+                    banks[there[within]][:, d * P : (d + 1) * P], g32[:, d, within * P : (within + 1) * P], ident[:]
                 )
-            for within in range(GROUPS):
-                column = (e - 2) * GROUPS + within
+
+        def gate_slots(group0, there, gated):
+            for within, b in enumerate(there):
+                column = group0 - 2 * GROUPS + within
                 nc.scalar.activation(
-                    paired(gated[:, within, :]),
-                    banks[within][:].rearrange("p (u v m) -> p u m v", u=2, v=2),
+                    paired(of_group(gated, within)),
+                    banks[b][:].rearrange("p (u v m) -> p u m v", u=2, v=2),
                     COPY,
                     scale=gate_columns[:, column : column + 1],
                 )
-            for half in range(2):
-                turn([gated[:, 2 * half, :], gated[:, 2 * half + 1, :]], back[half], rounded, half * HALF)
-            return rounded
 
-        by_plane = [(within, d) for d in range(PACK) for within in range(GROUPS)]
-        by_group = [(within, d) for within in range(GROUPS) for d in range(PACK)]
+        def turn_back(gated, half, b, rounded):
+            turn([of_group(gated, 2 * half), of_group(gated, 2 * half + 1)], b, rounded[:, half * 2 * H : (half + 1) * 2 * H])
+
+        def plane_order(groups):
+            return [(within, d) for d in range(PACK) for within in range(groups)]
+
+        def group_order(groups):
+            return [(within, d) for within in range(groups) for d in range(PACK)]
 
         def quantise_da(da, words, scales, lo):
             hi = lo + da.shape[1] // PACK
-            nc.vector.quantize_mx(
-                out=words[:, lo:hi].bitcast(E5M2), scales=scales[:, lo:hi], in_=da[:]
-            )
+            nc.vector.quantize_mx(out=words[:, lo:hi].bitcast(E5M2), scales=scales[:, lo:hi], in_=da)
 
         def multiply1(e, b, words, scales, lo):
-            dx = bank(b)
             nc.tensor.matmul_mx(
-                out=dx[:],
+                out=banks[b][:],
                 lhsT=w1_sb[:, e * W1_BYTES : (e + 1) * W1_BYTES].bitcast(E2M1),
                 lhsT_scale=w1_sc[:, e * K : (e + 1) * K],
                 rhs=words[:, lo : lo + C].bitcast(E5M2),
@@ -305,142 +303,169 @@ def tile_moe_bdx_mlp_relu2_kernel(
                 start=True,
                 stop=True,
             )
-            return dx
+            return banks[b]
 
-        rounded_01_0 = rounded_piece(0, 0, PAIR, ROOM[0], place([P, PAIR, PACK], BF16, "rounded_01_0", A3_AT + 8 * KB))
-        slope(0)
-        slope(1)
-        rounded_01_1 = rounded_piece(1, 0, PAIR, ROOM[2], on_a(1, [P, PAIR, PACK], BF16))
-        quantise_g(flat(rounded_01_0), 0, 0, own([P, PAIR], U32, "words_01_0"))
-        gate_columns = keep.tile([P, 2 * GROUPS], F32, name="gate_columns")
-        for half in range(2):
-            turned = bank(4 + half)
-            for within in range(GROUPS):
-                at = (half * GROUPS + within) * P
-                nc.tensor.transpose(turned[:, within * P : (within + 1) * P], gates[1][:, at : at + P], ident[:])
-            nc.scalar.copy(gate_columns[:, half * GROUPS : (half + 1) * GROUPS], turned[:, 0:512:P])
-        slope(2)
-        slope(3)
-        rounded_01_2 = rounded_piece(2, 0, PAIR, ROOM[0], place([P, PAIR, PACK], BF16, "rounded_01_2", A3_AT - 4 * KB))
-        quantise_g(flat(rounded_01_1), 1, 0, own([P, PAIR], U32, "words_01_1"))
-        for group in range(2 * GROUPS):
-            open_dh(group, group, 2)
-        dx_sb = on_a(0, [P, SLOTS], F32)
+        def open_dh(group, b, passes):
+            dh[group] = banks[b]
+            for s in passes:
+                multiply2(group, s)
 
-        rounded_2_0 = rounded_piece(
-            0, 2 * C, C, ROOM[2], place([P, C, PACK], BF16, "rounded_2_0", A3_AT + 4 * KB)
-        )
-        quantise_g(flat(rounded_01_2), 2, 0, own([P, PAIR], U32, "words_01_2"))
-        g32_3_0 = gathers(0, 3 * C, C, ROOM[0])
-        parked_0 = on_a(2, [P, GROUPS * H], F32)
-        parked_1 = on_a(1, [P, 3 * H], F32)
-        for group in range(2 * GROUPS):
+        room0 = place(PACK * PAIR, F32, "room0", ROOM0)
+        room1 = place(PACK * PAIR, F32, "room1", ROOM1)
+        rounded_01_0 = place(PACK * PAIR, BF16, "rounded_01_0", ROUNDED_01_0)
+        round_g(gathers(0, 0, room0[:]), rounded_01_0[:])
+        slope(0, 0)
+        slope(1, 4)
+        rounded_01_1 = place(PACK * PAIR, BF16, "rounded_01_1", A_AT[1])
+        round_g(gathers(1, 0, room1[:]), rounded_01_1[:])
+        words_01_0 = place(PAIR, U32, "words_01_0", WORDS0)
+        quantise_g(rounded_01_0[:], 0, 0, words_01_0[:])
+
+        g32_0_2 = gathers(2, 0, room0[:, 0 : PACK * C])
+        slope(2, 0)
+        rounded_0_2 = place(PACK * C, BF16, "rounded_0_2", A_AT[2])
+        round_g(g32_0_2, rounded_0_2[:])
+        slope(3, 4)
+        quantise_g(rounded_01_1[:], 1, 0, place(PAIR, U32, "words_01_1", WORDS1)[:])
+        for group in range(4):
+            open_dh(group, group, (0, 1))
+
+        rounded_1_2 = place(PACK * C, BF16, "rounded_1_2", A_AT[3])
+        round_g(gathers(2, C, room1[:, 0 : PACK * C]), rounded_1_2[:])
+        quantise_g(rounded_0_2[:], 2, 0, place(C, U32, "words_0_2", A_AT[2] + 4 * KB)[:])
+        for group in range(4):
             multiply2(group, 2)
-        for group in range(GROUPS):
-            park(group, parked_0[:, group * H : (group + 1) * H])
-        for group in range(4, 7):
-            park(group, parked_1[:, (group - 4) * H : (group - 3) * H])
-        rounded_3_0 = own([P, C, PACK], BF16, "words_01_2")
+        for group in range(4, 8):
+            open_dh(group, group, (0, 1))
+        parked_0 = place(GROUPS * H, F32, "parked_0", PARKED_0)
+        park(0, parked_0)
+
+        g32_2_0 = gathers(0, 2 * C, room0[:, 0 : PACK * C])
+        rounded_2_0a = place(PACK * HALF, BF16, "rounded_2_0a", A_AT[2] + 4 * KB)
+        round_g(g32_2_0[:, :, 0:HALF], rounded_2_0a[:])
+        quantise_g(rounded_1_2[:], 2, C, place(C, U32, "words_1_2", A_AT[2] + 6 * KB)[:])
+        for group in range(4, 8):
+            multiply2(group, 2)
+        parked_1 = place(GROUPS * H, F32, "parked_1", ROUNDED_01_0)
+        park(1, parked_1)
+
+        g32_2_1 = plain_gathers(1, 2 * C, place(PACK * C, F32, "g32_2_1", ROOM1)[:])
+        g32_2_2 = plain_gathers(2, 2 * C, place(PACK * C, F32, "g32_2_2", ROOM1 + 8 * KB)[:])
+        times_on_gpsimd(0, parked_0, place(GROUPS * H, BF16, "products_0", A_AT[3]))
+        times_on_gpsimd(1, parked_1, place(GROUPS * H, BF16, "products_1", PRODUCTS_1))
+        gated_2_1 = a_sb[0][:, 0 : 2 * H].bitcast(BF16)
+        rounded_2_1 = place(PACK * C, BF16, "rounded_2_1", SLOPES)
+        turn_slots(g32_2_1, (0, 1, 2, 3), plane_order(4))
+        gate_slots(8, (0, 1, 2, 3), gated_2_1)
+        turn_back(gated_2_1, 0, 0, rounded_2_1)
+        turn_back(gated_2_1, 1, 2, rounded_2_1)
+        da0 = place(PACK * C, BF16, "da0", DA0)
+        turn_da((0, 1), 1, da0[:, 0 : 2 * H])
+        turn_da((2, 3), 3, da0[:, 2 * H : 4 * H])
+
+        quantise_g(rounded_2_0a[:], 0, 2 * C, place(HALF, U32, "words_2_0a", A_AT[0])[:])
+        quantise_g(rounded_2_1[:], 1, 2 * C, place(C, U32, "words_2_1", WORDS1)[:])
+        g32_3_0 = gathers(0, 3 * C, place(PACK * C, F32, "g32_3_0", A_AT[0] + KB)[:])
+        gated_2_2 = gates[0][:].bitcast(BF16)
+        rounded_2_2 = place(PACK * C, BF16, "rounded_2_2", SLOPES + 4 * KB)
+        turn_slots(g32_2_2, (0, 2, 1, 3), group_order(4))
+        gate_slots(8, (0, 2, 1, 3), gated_2_2)
+        turn_back(gated_2_2, 0, 4, rounded_2_2)
+        turn_back(gated_2_2, 1, 5, rounded_2_2)
+        rounded_2_0b = place(PACK * HALF, BF16, "rounded_2_0b", GATE0)
+        round_g(g32_2_0[:, :, HALF:C], rounded_2_0b[:])
+        da1 = place(PACK * C, BF16, "da1", GATE0 + 2 * KB)
+        turn_da((4, 5), 6, da1[:, 0 : 2 * H])
+        turn_da((6, 7), 7, da1[:, 2 * H : 4 * H])
+        open_dh(8, 0, (0, 1))
+        open_dh(9, 2, (0, 1))
+        open_dh(10, 1, (1,))
+        open_dh(11, 3, (1,))
+        quantise_g(rounded_2_2[:], 2, 2 * C, place(C, U32, "words_2_2", WORDS1 + 2 * KB)[:])
+        for group in range(8, 12):
+            multiply2(group, 2)
+        quantise_g(rounded_2_0b[:], 0, 2 * C + HALF, words_01_0[:, 0:HALF])
+        multiply2(10, 0)
+        multiply2(11, 0)
+        parked_2 = place(GROUPS * H, F32, "parked_2", ROUNDED_01_0)
+        park(2, parked_2)
+
+        g32_3a_2 = gathers(2, 3 * C, place(PACK * HALF, F32, "g32_3a_2", ROOM0 + 4 * KB)[:])
+        words0 = place(C, U32, "words0", ROOM0 + 8 * KB)
+        scales0 = own(C, U8, "scales0")
+        quantise_da(da0[:], words0, scales0, 0)
+        g32_3a_1 = plain_gathers(1, 3 * C, place(PACK * HALF, F32, "g32_3a_1", ROOM0)[:])
+        g32_3b_1 = plain_gathers(1, 3 * C + HALF, place(PACK * HALF, F32, "g32_3b_1", ROOM0 + 10 * KB)[:])
+        times_on_gpsimd(2, parked_2, place(GROUPS * H, BF16, "products_2", DA0))
+        rounded_3_0 = place(PACK * C, BF16, "rounded_3_0", WORDS0)
         round_g(g32_3_0, rounded_3_0[:])
+        dx_sb = place(SLOTS, F32, "dx_sb", A_AT[1])
+        nc.scalar.copy(dx_sb[:, 0:C], multiply1(0, 1, words0, scales0, 0)[:])
+        rounded_3a_2 = place(PACK * HALF, BF16, "rounded_3a_2", A_AT[0] + KB)
+        round_g(g32_3a_2, rounded_3a_2[:])
+        gated_3a = place(2 * H, BF16, "gated_3a", A_AT[0] + 3 * KB)
+        gated_3b = place(2 * H, BF16, "gated_3b", A_AT[0] + 5 * KB)
+        turn_slots(g32_3a_1, (4, 5), plane_order(2))
+        turn_slots(g32_3b_1, (6, 7), plane_order(2))
+        gate_slots(12, (4, 5), gated_3a)
+        gate_slots(14, (6, 7), gated_3b)
+        quantise_g(rounded_3_0[:], 0, 3 * C, place(C, U32, "words_3_0", A_AT[3] + 4 * KB)[:])
+        quantise_g(rounded_3a_2[:], 2, 3 * C, place(HALF, U32, "words_3a_2", A_AT[3] + 6 * KB)[:])
+        rounded_3a_1 = place(PACK * HALF, BF16, "rounded_3a_1", A_AT[3])
+        rounded_3b_1 = place(PACK * HALF, BF16, "rounded_3b_1", A_AT[3] + 2 * KB)
+        turn_back(gated_3a, 0, 0, rounded_3a_1)
+        turn_back(gated_3b, 0, 1, rounded_3b_1)
+        open_dh(12, 4, (0, 2))
+        open_dh(13, 5, (0, 2))
+        open_dh(14, 6, (0,))
+        open_dh(15, 7, (0,))
 
-        g32_2_1 = plain_gathers(1, 2 * C, ROOM[1])
-        g32_3_1 = plain_gathers(1, 3 * C, ROOM[2])
-        products_0 = on_plane(0, 3, [P, GROUPS * H], BF16)
-        products_1 = on_plane(0, 2, [P, GROUPS * H], BF16)
-        for group in range(GROUPS):
-            times_on_gpsimd(group, products_0[:, group * H : (group + 1) * H])
-        for group in range(4, 7):
-            times_on_gpsimd(group, products_1[:, (group - 4) * H : (group - 3) * H])
-        times(7, products_1[:, 3 * H : 4 * H])
-        rounded_2_1 = gate_turned(
-            g32_2_1, 2, on_plane(0, 0, [P, GROUPS, H], BF16),
-            place([P, C * PACK], BF16, "rounded_2_1", A3_AT - 4 * KB),
-            (0, 1, 2, 3), (4, 5), by_plane,
-        )
-        da0 = on_a(3, [P, C * PACK], BF16)
-        turn_da((0, 1), 1, da0, 0)
-        turn_da((2, 3), 0, da0, HALF)
-        rounded_3_1 = gate_turned(
-            g32_3_1, 3, place([P, GROUPS, H], BF16, "gated_3", ROOM[3]), own([P, C * PACK], BF16, "gate0"),
-            (4, 1, 5, 0), (6, 7), by_group,
-        )
-        da1 = on_plane(1, 1, [P, C * PACK], BF16)
-        turn_da((4, 5), 4, da1, 0)
-        turn_da((6, 7), 1, da1, HALF)
-
-        rounded_2 = rounded_piece(
-            2, 2 * C, C, ROOM[0], place([P, C, PACK], BF16, "rounded_2", ROOM[3] + 2 * KB)
-        )
-        words_23_0 = on_plane(1, 2, [P, PAIR], U32)
-        quantise_g(flat(rounded_2_0), 0, 2 * C, words_23_0[:, 0:C], ROOM[3] + KB)
-        quantise_g(flat(rounded_3_0), 0, 3 * C, words_23_0[:, C:PAIR], ROOM[3] + KB + C)
-        quantise_g(rounded_2_1[:], 1, 2 * C, on_plane(1, 3, [P, C], U32))
-        for group, b in zip(range(8, 12), (2, 3, 5, 0)):
-            open_dh(group, b, 2)
-        quantise_g(rounded_3_1[:], 1, 3 * C, own([P, C], U32, "words_3_1"))
-        for group, b in zip(range(12, 16), (4, 1, 6, 7)):
-            open_dh(group, b, 2)
-        rounded_3a = rounded_piece(
-            2, 3 * C, HALF, ROOM[3] - 3 * KB, place([P, HALF, PACK], BF16, "rounded_3a", ROOM[1])
-        )
-        quantise_g(flat(rounded_2), 2, 2 * C, own([P, C], U32, "words_2_2"))
-        for group in (11, 8, 9, 10):
-            multiply2(group, 2)
-        parked_23 = on_a(2, [P, 2 * H], F32)
-        park(11, parked_23[:, 0:H])
-        rounded_3b = rounded_piece(
-            2, 3 * C + HALF, HALF, ROOM[0], place([P, HALF, PACK], BF16, "rounded_3b", ROOM[1] + 2 * KB)
-        )
-        quantise_g(flat(rounded_3a), 2, 3 * C, own([P, HALF], U32, "words_3a"))
-        multiply2(12, 2)
-        multiply2(13, 2)
-        park(12, parked_23[:, H : 2 * H])
-        words03 = place([P, 2 * C], U32, "words03", ROOM[3] - 4 * KB)
-        words1 = place([P, C], U32, "words1", ROOM[3])
-        scales1 = own([P, C], U8, "scales1")
-        quantise_da(da0, words03, scales03, 0)
-        quantise_da(da1, words1, scales1, 0)
-        quantise_g(flat(rounded_3b), 2, 3 * C + HALF, own([P, HALF], U32, "words_3b"))
+        g32_3b_2 = gathers(2, 3 * C + HALF, place(PACK * HALF, F32, "g32_3b_2", ROOM0 + 4 * KB)[:])
+        rounded_3b_2 = place(PACK * HALF, BF16, "rounded_3b_2", A_AT[0] + 5 * KB)
+        round_g(g32_3b_2, rounded_3b_2[:])
+        words13 = on_plane(2, 2, 2 * C, U32)
+        scales13 = own(2 * C, U8, "scales13")
+        quantise_da(da1[:], words13, scales13, 0)
+        quantise_g(rounded_3a_1[:], 1, 3 * C, place(HALF, U32, "words_3a_1", A_AT[3] + 7 * KB)[:])
+        multiply2(12, 1)
+        multiply2(13, 1)
+        quantise_g(rounded_3b_1[:], 1, 3 * C + HALF, place(HALF, U32, "words_3b_1", A_AT[2] + 2 * KB)[:])
+        multiply2(14, 1)
+        multiply2(15, 1)
+        quantise_g(rounded_3b_2[:], 2, 3 * C + HALF, place(HALF, U32, "words_3b_2", A_AT[2] + 3 * KB)[:])
         multiply2(14, 2)
         multiply2(15, 2)
-        nc.scalar.copy(dx_sb[:, 0:C], multiply1(0, 0, words03, scales03, 0)[:])
-        nc.scalar.copy(dx_sb[:, C : 2 * C], multiply1(1, 4, words1, scales1, 0)[:])
+        da2 = place(PACK * C, BF16, "da2", ROOM0 + 2 * KB)
+        turn_da((8, 9), 2, da2[:, 0 : 2 * H])
+        turn_da((10, 11), 3, da2[:, 2 * H : 4 * H])
+        nc.scalar.copy(dx_sb[:, C : 2 * C], multiply1(1, 0, words13, scales13, 0)[:])
 
-        products_gpsimd = place([P, 2 * H], BF16, "products_gpsimd", ROOM[1] + 2 * KB)
-        times_on_gpsimd(11, products_gpsimd[:, 0:H])
-        times_on_gpsimd(12, products_gpsimd[:, H : 2 * H])
-        products_held = place([P, 4 * H], BF16, "products_held", ROOM[0])
-        products_last = place([P, 2 * H], BF16, "products_last", ROOM[0] + 4 * KB)
-        da2 = on_plane(2, 0, [P, C * PACK], BF16)
-        times(8, products_held[:, 0:H])
-        times(9, products_held[:, H : 2 * H])
-        turn_da((8, 9), 2, da2, 0)
-        times(10, products_held[:, 2 * H : 3 * H])
-        turn_da((10, 11), 3, da2, HALF)
-        times(13, products_held[:, 3 * H : 4 * H])
-        da_12_13 = on_plane(2, 1, [P, HALF * PACK], BF16)
-        turn_da((12, 13), 5, da_12_13, 0)
-        times(14, products_last[:, 0:H])
-        da_14 = on_plane(2, 2, [P, P * PACK], BF16)
-        turn_da((14,), 1, da_14, 0)
-        times(15, products_last[:, H : 2 * H])
-        da_15 = on_plane(2, 3, [P, P * PACK], BF16)
-        turn_da((15,), 6, da_15, 0)
+        products_3 = place(GROUPS * H, BF16, "products_3", ROOM0 + 6 * KB)
+        times(12, of_group(products_3, 0))
+        times(13, of_group(products_3, 1))
+        da_12_13 = on_plane(0, 1, PACK * HALF, BF16)
+        turn_da((12, 13), 1, da_12_13[:])
+        times(14, of_group(products_3, 2))
+        da_14 = on_plane(0, 2, PACK * P, BF16)
+        turn_da((14,), 3, da_14[:])
+        times(15, of_group(products_3, 3))
+        da_15 = on_plane(0, 3, PACK * P, BF16)
+        turn_da((15,), 4, da_15[:])
 
-        words2 = place([P, C], U32, "words2", SLOPE_AT[14])
-        scales2 = own([P, C], U8, "scales2")
-        quantise_da(da2, words2, scales2, 0)
-        nc.scalar.copy(dx_sb[:, 2 * C : 3 * C], multiply1(2, 0, words2, scales2, 0)[:])
-        quantise_da(da_12_13, words03, scales03, C)
-        quantise_da(da_14, words03, scales03, C + HALF)
-        dx_12_14 = multiply1(3, 4, words03, scales03, C - P)
-        quantise_da(da_15, words03, scales03, 2 * C - P)
-        dx_15 = multiply1(3, 2, words03, scales03, C)
+        words2 = on_plane(1, 0, C, U32)
+        scales2 = own(C, U8, "scales2")
+        quantise_da(da2[:], words2, scales2, 0)
+        nc.scalar.copy(dx_sb[:, 2 * C : 3 * C], multiply1(2, 2, words2, scales2, 0)[:])
+        quantise_da(da_12_13[:], words13, scales13, C)
+        quantise_da(da_14[:], words13, scales13, C + HALF)
+        dx_12_14 = multiply1(3, 5, words13, scales13, C - P)
+        quantise_da(da_15[:], words13, scales13, 2 * C - P)
+        dx_15 = multiply1(3, 6, words13, scales13, C)
         nc.vector.tensor_copy(dx_sb[:, 3 * C : SLOTS - P], dx_12_14[:, P:C])
         nc.scalar.copy(dx_sb[:, SLOTS - P : SLOTS], dx_15[:, C - P : C])
 
-        first = place([P, T], F32, "first", SLOPE_AT[6])
-        total = place([P, T], F32, "total", SLOPE_AT[8])
+        first = place(T, F32, "first", SLOPES + EXPERT_SLOPE_BYTES)
+        total = place(T, F32, "total", SLOPES + EXPERT_SLOPE_BYTES + 4 * KB)
         nc.vector.tensor_copy(first[:], dx_sb[:].indirect(pos1_sb[:]))
         for lo, hi in zip(OUT_CUTS, OUT_CUTS[1:]):
             nc.vector.tensor_tensor(

@@ -6,17 +6,14 @@ from concourse.masks import make_identity
 K, T, E, C, H, N = 128, 1024, 4, 512, 512, 1536
 P = 128
 PACK = 4
+RUN = 4
 SLOTS = E * C
 PASSES = N // 512
 GROUPS = C // P
-PAIR = 2 * C
-HALF = C // 2
-PAD = 8
 W2_PASS_BYTES = 2 * H
 W1_BYTES = 2 * K
 ALIGN = 64
-FIRST_CUTS = (0, 128, 384, PAIR)
-OUT_CUTS = (0, 512, 896, T)
+OUT_CUTS = (0, 256, 640, 896, T)
 
 FLOPS = 2 * SLOTS * (N * H + H * K)
 BYTES = (
@@ -34,20 +31,8 @@ E5M2 = mybir.dt.float8_e5m2_x4
 E2M1 = mybir.dt.float4_e2m1fn_x4
 MULT = mybir.AluOpType.mult
 ADD = mybir.AluOpType.add
+MAX = mybir.AluOpType.max
 COPY = mybir.ActivationFunctionType.Copy
-RELU = mybir.ActivationFunctionType.Relu
-
-KB = 1024
-ROOM0, ROOM1 = 0, 16 * KB
-WORDS0, WORDS1 = 32 * KB, 36 * KB
-PARKED_0 = 131 * KB
-PRODUCTS_1 = 44 * KB
-DA0 = 48 * KB
-A_AT = (52 * KB, 61 * KB, 69 * KB, 77 * KB)
-ROUNDED_01_0 = 85 * KB
-GATE0 = 93 * KB
-SLOPES = 99 * KB
-EXPERT_SLOPE_BYTES = 8 * KB
 
 
 def tile_moe_bdx_mlp_relu2_kernel(
@@ -56,16 +41,12 @@ def tile_moe_bdx_mlp_relu2_kernel(
     nc = tc.nc
     with ExitStack() as ctx:
         keep = ctx.enter_context(tc.tile_pool(name="keep", bufs=1))
-        placed = ctx.enter_context(tc.tile_pool(name="placed", bufs=1))
         psum = ctx.enter_context(tc.psum_pool(name="psum", bufs=1))
 
         banks = [psum.tile([P, 512], F32, name=f"bank{b}") for b in range(8)]
-
-        def place(width, dtype, name, at):
-            return placed.tile([P, width], dtype, name=name, offset=at, align_bytes=ALIGN)
-
-        def on_plane(s, d, width, dtype):
-            return keep.tile([P, width], dtype, name=f"dy{s}_{d}", align_bytes=ALIGN)
+        gate_banks = banks[0:2]
+        dx_banks = banks[2:4]
+        dh_banks = banks[4:8]
 
         def own(width, dtype, name):
             return keep.tile([P, width], dtype, name=name, align_bytes=ALIGN)
@@ -76,36 +57,41 @@ def tile_moe_bdx_mlp_relu2_kernel(
         offs_sb = keep.tile([P, SLOTS // 16], U16, name="offs_sb")
         pos1_sb = keep.tile([P, T // 16], U16, name="pos1_sb")
         pos2_sb = keep.tile([P, T // 16], U16, name="pos2_sb")
-        gates = [place(PAIR, F32, "gate0", GATE0), own(PAIR, F32, "gate1")]
-        gate_columns = own(2 * GROUPS, F32, "gate_columns")
-        planes = [[on_plane(s, d, T + PAD, F32) for d in range(PACK)] for s in range(PASSES)]
-        w2_sb = [own(PASSES * W2_PASS_BYTES, U8, f"w2_{e}") for e in range(E)]
-        w2_sc = own(E * PASSES * H, U8, "w2_sc")
+        planes = [[own(T, F32, f"plane{s}_{d}") for d in range(PACK)] for s in range(PASSES)]
+        gate_columns = own(SLOTS // P, F32, "gate_columns")
+        w2_raw = [own(PASSES * H, U16, f"w2_raw{e}") for e in range(E)]
+        w2_sb = [own(PASSES * H, U16, f"w2_{r}") for r in range(2)] * 2
+        sc_first = own(PASSES * H, U8, "sc_first")
+        sc_rest = own((E - 1) * PASSES * H, U8, "sc_rest")
+        w2_sc_raw = [sc_first[:]] + [sc_rest[:, r * PASSES * H : (r + 1) * PASSES * H] for r in range(E - 1)]
+        w2_sc = [own(PASSES * H, U8, f"w2_sc{r}") for r in range(2)] * 2
         w1_sb = own(E * W1_BYTES, U8, "w1_sb")
         w1_sc = own(E * K, U8, "w1_sc")
-        ident = keep.tile([P, P], F32, name="ident")
-        a_sb = [place(PACK * C, F32, f"a{e}", A_AT[e]) for e in range(E)]
-        slopes = [place(GROUPS * H, F32, f"slopes{e}", SLOPES + e * EXPERT_SLOPE_BYTES) for e in range(E)]
+        ident = own(P, F32, "ident")
+        a_sb = [own(PACK * C, F32, f"a{e}") for e in range(E)]
+        gate_rows = own(P, F32, "gate_rows")[:]
+        rooms = [own(PACK * C, F32, f"room{r}") for r in range(5)]
+        slopes = [rooms[0], rooms[3], rooms[4], rooms[3]]
+        rounded = own(PACK * C, BF16, "rounded")
+        da_sb = [own(PACK * C, BF16, f"da{r}") for r in range(2)]
+        g_words = [own(C, U32, f"g_words{r}") for r in range(5)]
+        g_scales = [own(C, U8, f"g_scales{r}") for r in range(5)]
+        da_words = [own(C, U32, f"da_words{r}") for r in range(2)]
+        da_scales = [own(C, U8, f"da_scales{r}") for r in range(2)]
+        dx_sb = own(SLOTS, F32, "dx_sb")
+        first = own(T, F32, "first")
+        total = own(T, F32, "total")
 
-        for s in range(PASSES):
-            for d in range(PACK):
-                nc.vector.memset(planes[s][d][:, T : T + PAD], 0.0)
-        nc.vector.memset(w2_sc[:].bitcast(I32), 0)
-        nc.vector.memset(w1_sc[:].bitcast(I32), 0)
+        nc.gpsimd.memset(sc_first[:].bitcast(I32), 0)
+        nc.vector.memset(sc_rest[:].bitcast(I32), 0)
+        nc.scalar.copy(w1_sc[:].bitcast(U32), sc_rest[:, 0 : E * K].bitcast(U32))
         make_identity(nc, ident[:])
 
         dy_rows = dyT.rearrange("(s p d) t -> s d p t", p=P, d=PACK)
 
-        def load_plane(s, d):
-            nc.sync.dma_start(out=planes[s][d][:, 0:T], in_=dy_rows[s, d])
-
-        def load_gate(lo, hi):
-            base = lo % PAIR
-            nc.sync.dma_start(out=gates[lo // PAIR][:, base : base + hi - lo], in_=gate[0:P, lo:hi])
-
         def load_w2(e):
             nc.sync.dma_start(
-                out=w2_sb[e][:].bitcast(I32).rearrange("p (s w) -> p s w", s=PASSES),
+                out=w2_raw[e][:].bitcast(I32).rearrange("p (s w) -> p s w", s=PASSES),
                 in_=w2_words.bitcast(I32)[e].rearrange("s p w -> p s w"),
             )
 
@@ -123,24 +109,20 @@ def tile_moe_bdx_mlp_relu2_kernel(
                 )
 
         nc.sync.dma_start(offs_sb[:], offs)
-        load_plane(0, 0)
-        for lo, hi in zip(FIRST_CUTS, FIRST_CUTS[1:]):
-            load_gate(lo, hi)
         for s in range(PASSES):
             for d in range(PACK):
-                if (s, d) != (0, 0):
-                    load_plane(s, d)
-            if s == 1:
-                load_a(0)
-                load_a(1)
-        load_gate(PAIR, SLOTS)
-        load_a(2)
-        load_a(3)
-        load_scales(w2_sc, w2_scales, E * PASSES)
-        for e in range(E):
+                nc.sync.dma_start(out=planes[s][d][:], in_=dy_rows[s, d])
+            if s == 0:
+                nc.sync.dma_start(
+                    out=gate_rows, in_=gate[0 : P * P // SLOTS, :].rearrange("r (x c) -> (r x) c", c=P)
+                )
+        load_w2(0)
+        load_scales(sc_first, w2_scales[0:1], PASSES)
+        load_a(0)
+        for e in range(1, E):
             load_w2(e)
-        with nc.allow_non_contiguous_dma(reason="one gate value a partition"):
-            nc.sync.dma_start(out=gate_columns[:], in_=gate[P, PAIR:SLOTS].rearrange("(x p) -> p x", p=P))
+            load_a(e)
+        load_scales(sc_rest, w2_scales[1:E], (E - 1) * PASSES)
         load_scales(w1_sc, w1_scales, E)
         nc.sync.dma_start(
             out=w1_sb[:].bitcast(I32).rearrange("p (e w) -> p e w", e=E),
@@ -149,325 +131,201 @@ def tile_moe_bdx_mlp_relu2_kernel(
         nc.sync.dma_start(pos1_sb[:], pos1)
         nc.sync.dma_start(pos2_sb[:], pos2)
 
-        codes = {}
-        dh = {}
-        done = {}
-        products = {}
-
-        def gathers(s, slot0, room):
-            g32 = by_plane(room)
-            width = g32.shape[2]
+        def gather(engine, e, s, room, lo=0, hi=C):
             for d in range(PACK):
-                cuts = FIRST_CUTS if (s, slot0, d) == (0, 0, 0) else (0, width)
-                for lo, hi in zip(cuts, cuts[1:]):
-                    start = slot0 + lo
-                    base = start % PAIR
-                    nc.vector.tensor_tensor(
-                        g32[:, d, lo:hi],
-                        planes[s][d][:].indirect(offs_sb[:, start // 16 : (slot0 + hi) // 16]),
-                        gates[start // PAIR][:, base : base + hi - lo],
-                        MULT,
-                    )
-            return g32
+                window = planes[s][d][:].indirect(offs_sb[:, (e * C + lo) // 16 : (e * C + hi) // 16])
+                if engine == "scalar":
+                    nc.scalar.activation(room[:, d * C + lo : d * C + hi], window, COPY)
+                else:
+                    nc.vector.tensor_copy(room[:, d * C + lo : d * C + hi], window)
 
-        def plain_gathers(s, slot0, room):
-            g32 = by_plane(room)
-            width = g32.shape[2]
-            for d in range(PACK):
-                nc.vector.tensor_copy(
-                    g32[:, d, :], planes[s][d][:].indirect(offs_sb[:, slot0 // 16 : (slot0 + width) // 16])
-                )
-            return g32
+        def in_runs(ap, lo, hi):
+            return by_plane(ap)[:, :, lo:hi].rearrange("p d (c r) -> p c d r", r=RUN)
 
-        def round_g(g32, rounded):
-            nc.scalar.activation(
-                rounded.rearrange("p (c r d) -> p c d r", r=4, d=PACK),
-                g32.rearrange("p d (c r) -> p c d r", r=4),
-                COPY,
-            )
+        def woven(ap, lo, hi):
+            return ap[:, PACK * lo : PACK * hi].rearrange("p (c r d) -> p c d r", r=RUN, d=PACK)
 
-        def quantise_g(rounded, s, slot0, words):
-            width = words.shape[1]
-            scales = own(width, U8, f"g_scales_{s}_{slot0}")
-            nc.vector.quantize_mx(out=words.bitcast(E5M2), scales=scales[:], in_=rounded)
-            for x in range(width // P):
-                codes[slot0 // P + x, s] = (words[:, x * P : (x + 1) * P], scales[:, x * P : (x + 1) * P])
-
-        def multiply2(group, s):
-            e = group // GROUPS
-            words, scales = codes[group, s]
-            before = done.get(group, 0)
-            done[group] = before + 1
-            nc.tensor.matmul_mx(
-                out=dh[group][:],
-                lhsT=words.bitcast(E5M2),
-                lhsT_scale=scales,
-                rhs=w2_sb[e][:, s * W2_PASS_BYTES : (s + 1) * W2_PASS_BYTES].bitcast(E2M1),
-                rhs_scale=w2_sc[:, (e * PASSES + s) * H : (e * PASSES + s + 1) * H],
-                start=(before == 0),
-                stop=(before == PASSES - 1),
-            )
-
-        def paired(ap):
-            return ap.rearrange("p (u m v) -> p u m v", u=2, v=2)
-
-        def dh_paired(group):
-            return dh[group][:].rearrange("p (m u v) -> p u m v", u=2, v=2)
-
-        def of_group(tile, within):
-            return tile[:, within * H : (within + 1) * H]
-
-        def slope(e, first_bank):
-            source = by_plane(a_sb[e][:])
-            for within in range(GROUPS):
-                turned = banks[first_bank + within]
-                for d in range(PACK):
-                    nc.tensor.transpose(
-                        turned[:, d * P : (d + 1) * P], source[:, d, within * P : (within + 1) * P], ident[:]
-                    )
-                nc.scalar.activation(
-                    paired(of_group(slopes[e], within)),
-                    turned[:].rearrange("p (u v m) -> p u m v", u=2, v=2),
-                    RELU,
-                    scale=2.0,
-                )
-
-        def times(group, dest):
-            products[group] = dest
-            nc.vector.tensor_tensor(
-                paired(dest), dh_paired(group), paired(of_group(slopes[group // GROUPS], group % GROUPS)), MULT
-            )
-
-        def park(e, parked):
-            for within in range(GROUPS):
-                nc.scalar.copy(paired(of_group(parked, within)), dh_paired(e * GROUPS + within))
-
-        def times_on_gpsimd(e, parked, dest):
-            for within in range(GROUPS):
-                products[e * GROUPS + within] = of_group(dest, within)
-            nc.gpsimd.tensor_tensor(dest[:], parked[:], slopes[e][:], MULT)
-
-        def turn(sources, b, dest):
-            turned = banks[b]
-            for x, source in enumerate(sources):
-                pairs = source.bitcast(F32)
-                for u in range(2):
-                    nc.tensor.transpose(
-                        turned[:, (2 * x + u) * P : (2 * x + u + 1) * P], pairs[:, u * P : (u + 1) * P], ident[:]
-                    )
-            width = len(sources) * P
-            nc.scalar.copy(
-                dest.bitcast(F32).rearrange("p (x c u) -> p x c u", c=P, u=2),
-                turned[:, 0 : 2 * width].rearrange("p (x u c) -> p x c u", c=P, u=2),
-            )
-
-        def turn_da(groups, b, dest):
-            turn([products[group] for group in groups], b, dest)
-
-        def turn_slots(g32, there, order):
-            for within, d in order:
+        def spread_gate(e, bank):
+            for x in range(GROUPS):
+                column = e * GROUPS + x
                 nc.tensor.transpose(
-                    banks[there[within]][:, d * P : (d + 1) * P], g32[:, d, within * P : (within + 1) * P], ident[:]
+                    gate_banks[bank][:, x * P : (x + 1) * P],
+                    gate_columns[:, column : column + 1].to_broadcast([P, P]),
+                    ident[:],
                 )
 
-        def gate_slots(group0, there, gated):
-            for within, b in enumerate(there):
-                column = group0 - 2 * GROUPS + within
-                nc.scalar.activation(
-                    paired(of_group(gated, within)),
-                    banks[b][:].rearrange("p (u v m) -> p u m v", u=2, v=2),
-                    COPY,
-                    scale=gate_columns[:, column : column + 1],
-                )
+        def times_gate(bank, room, lo=0, hi=C):
+            gates = gate_banks[bank][:, lo:hi].rearrange("p (c r) -> p c r", r=RUN)
+            nc.vector.tensor_tensor(
+                woven(rounded[:], lo, hi),
+                in_runs(room[:], lo, hi),
+                gates.unsqueeze(2).to_broadcast([P, (hi - lo) // RUN, PACK, RUN]),
+                MULT,
+            )
 
-        def turn_back(gated, half, b, rounded):
-            turn([of_group(gated, 2 * half), of_group(gated, 2 * half + 1)], b, rounded[:, half * 2 * H : (half + 1) * 2 * H])
+        def quantise(source, words, scales, lo=0, hi=C):
+            nc.vector.quantize_mx(
+                out=words[:, lo:hi].bitcast(E5M2), scales=scales[:, lo:hi], in_=source[:, PACK * lo : PACK * hi]
+            )
 
-        def plane_order(groups):
-            return [(within, d) for d in range(PACK) for within in range(groups)]
+        def permute_words(e):
+            nc.vector.tensor_copy(
+                w2_sb[e][:].rearrange("p (s t m) -> p t s m", s=PASSES, t=PACK),
+                w2_raw[e][:].rearrange("p (s m t) -> p t s m", s=PASSES, t=PACK),
+            )
 
-        def group_order(groups):
-            return [(within, d) for within in range(groups) for d in range(PACK)]
+        def permute_scales(e):
+            nc.vector.tensor_copy(
+                w2_sc[e][:].rearrange("p (s t m) -> p t s m", s=PASSES, t=PACK),
+                w2_sc_raw[e].rearrange("p (s m t) -> p t s m", s=PASSES, t=PACK),
+            )
 
-        def quantise_da(da, words, scales, lo):
-            hi = lo + da.shape[1] // PACK
-            nc.vector.quantize_mx(out=words[:, lo:hi].bitcast(E5M2), scales=scales[:, lo:hi], in_=da)
+        def make_slopes(e):
+            nc.vector.tensor_scalar(slopes[e][:], a_sb[e][:], 0.0, 2.0, MAX, MULT)
 
-        def multiply1(e, b, words, scales, lo):
+        def dh_bank(e, x):
+            return dh_banks[(e * GROUPS + x) % len(dh_banks)]
+
+        def multiply2(e, s, codes, groups, opens, closes):
+            words, scales = g_words[codes], g_scales[codes]
+            for x in groups:
+                for t in range(PACK):
+                    at = s * H + t * P
+                    nc.tensor.matmul_mx(
+                        out=dh_bank(e, x)[:, t * P : (t + 1) * P],
+                        lhsT=w2_sb[e][:, at : at + P].bitcast(U8).bitcast(E2M1),
+                        lhsT_scale=w2_sc[e][:, at : at + P],
+                        rhs=words[:, x * P : (x + 1) * P].bitcast(E5M2),
+                        rhs_scale=scales[:, x * P : (x + 1) * P],
+                        start=(opens and t == 0),
+                        stop=(closes and t == PACK - 1),
+                    )
+
+        def times_slope(e, x):
+            nc.vector.tensor_tensor(
+                woven(da_sb[e % 2][:], x * P, (x + 1) * P),
+                dh_bank(e, x)[:].rearrange("p (d c r) -> p c d r", d=PACK, r=RUN),
+                in_runs(slopes[e][:], x * P, (x + 1) * P),
+                MULT,
+            )
+
+        def multiply1(e, lo=0, hi=C):
             nc.tensor.matmul_mx(
-                out=banks[b][:],
+                out=dx_banks[e % 2][:, lo:hi],
                 lhsT=w1_sb[:, e * W1_BYTES : (e + 1) * W1_BYTES].bitcast(E2M1),
                 lhsT_scale=w1_sc[:, e * K : (e + 1) * K],
-                rhs=words[:, lo : lo + C].bitcast(E5M2),
-                rhs_scale=scales[:, lo : lo + C],
+                rhs=da_words[e % 2][:, lo:hi].bitcast(E5M2),
+                rhs_scale=da_scales[e % 2][:, lo:hi],
                 start=True,
                 stop=True,
             )
-            return banks[b]
+            nc.scalar.copy(dx_sb[:, e * C + lo : e * C + hi], dx_banks[e % 2][:, lo:hi])
 
-        def open_dh(group, b, passes):
-            dh[group] = banks[b]
-            for s in passes:
-                multiply2(group, s)
+        def finish(e):
+            quantise(da_sb[e % 2], da_words[e % 2], da_scales[e % 2])
+            multiply1(e)
 
-        room0 = place(PACK * PAIR, F32, "room0", ROOM0)
-        room1 = place(PACK * PAIR, F32, "room1", ROOM1)
-        rounded_01_0 = place(PACK * PAIR, BF16, "rounded_01_0", ROUNDED_01_0)
-        round_g(gathers(0, 0, room0[:]), rounded_01_0[:])
-        slope(0, 0)
-        slope(1, 4)
-        rounded_01_1 = place(PACK * PAIR, BF16, "rounded_01_1", A_AT[1])
-        round_g(gathers(1, 0, room1[:]), rounded_01_1[:])
-        words_01_0 = place(PAIR, U32, "words_01_0", WORDS0)
-        quantise_g(rounded_01_0[:], 0, 0, words_01_0[:])
+        every = range(GROUPS)
 
-        g32_0_2 = gathers(2, 0, room0[:, 0 : PACK * C])
-        slope(2, 0)
-        rounded_0_2 = place(PACK * C, BF16, "rounded_0_2", A_AT[2])
-        round_g(g32_0_2, rounded_0_2[:])
-        slope(3, 4)
-        quantise_g(rounded_01_1[:], 1, 0, place(PAIR, U32, "words_01_1", WORDS1)[:])
-        for group in range(4):
-            open_dh(group, group, (0, 1))
+        def quantise_g(codes, lo=0, hi=C):
+            quantise(rounded, g_words[codes], g_scales[codes], lo, hi)
 
-        rounded_1_2 = place(PACK * C, BF16, "rounded_1_2", A_AT[3])
-        round_g(gathers(2, C, room1[:, 0 : PACK * C]), rounded_1_2[:])
-        quantise_g(rounded_0_2[:], 2, 0, place(C, U32, "words_0_2", A_AT[2] + 4 * KB)[:])
-        for group in range(4):
-            multiply2(group, 2)
-        for group in range(4, 8):
-            open_dh(group, group, (0, 1))
-        parked_0 = place(GROUPS * H, F32, "parked_0", PARKED_0)
-        park(0, parked_0)
+        def products(e):
+            for x in every:
+                times_slope(e, x)
 
-        g32_2_0 = gathers(0, 2 * C, room0[:, 0 : PACK * C])
-        rounded_2_0a = place(PACK * HALF, BF16, "rounded_2_0a", A_AT[2] + 4 * KB)
-        round_g(g32_2_0[:, :, 0:HALF], rounded_2_0a[:])
-        quantise_g(rounded_1_2[:], 2, C, place(C, U32, "words_1_2", A_AT[2] + 6 * KB)[:])
-        for group in range(4, 8):
-            multiply2(group, 2)
-        parked_1 = place(GROUPS * H, F32, "parked_1", ROUNDED_01_0)
-        park(1, parked_1)
+        nc.tensor.transpose(dx_banks[0][:, 0:P], gate_rows, ident[:])
+        nc.vector.tensor_copy(gate_columns[:], dx_banks[0][:, 0 : SLOTS // P])
+        spread_gate(0, 0)
+        spread_gate(3, 1)
 
-        g32_2_1 = plain_gathers(1, 2 * C, place(PACK * C, F32, "g32_2_1", ROOM1)[:])
-        g32_2_2 = plain_gathers(2, 2 * C, place(PACK * C, F32, "g32_2_2", ROOM1 + 8 * KB)[:])
-        times_on_gpsimd(0, parked_0, place(GROUPS * H, BF16, "products_0", A_AT[3]))
-        times_on_gpsimd(1, parked_1, place(GROUPS * H, BF16, "products_1", PRODUCTS_1))
-        gated_2_1 = a_sb[0][:, 0 : 2 * H].bitcast(BF16)
-        rounded_2_1 = place(PACK * C, BF16, "rounded_2_1", SLOPES)
-        turn_slots(g32_2_1, (0, 1, 2, 3), plane_order(4))
-        gate_slots(8, (0, 1, 2, 3), gated_2_1)
-        turn_back(gated_2_1, 0, 0, rounded_2_1)
-        turn_back(gated_2_1, 1, 2, rounded_2_1)
-        da0 = place(PACK * C, BF16, "da0", DA0)
-        turn_da((0, 1), 1, da0[:, 0 : 2 * H])
-        turn_da((2, 3), 3, da0[:, 2 * H : 4 * H])
+        gather("scalar", 0, 0, rooms[0])
+        gather("vector", 3, 0, rooms[3])
+        gather("scalar", 0, 1, rooms[1])
+        gather("scalar", 0, 2, rooms[2])
+        times_gate(0, rooms[0])
+        quantise_g(0)
+        times_gate(1, rooms[3])
+        spread_gate(1, 1)
+        quantise_g(4)
+        times_gate(0, rooms[1])
+        permute_words(0)
+        quantise_g(1)
+        permute_scales(0)
+        multiply2(0, 0, 0, every, True, False)
+        multiply2(0, 1, 1, every, False, False)
+        times_gate(0, rooms[2])
+        spread_gate(2, 0)
+        make_slopes(0)
+        quantise_g(2)
+        multiply2(0, 2, 2, every, False, True)
 
-        quantise_g(rounded_2_0a[:], 0, 2 * C, place(HALF, U32, "words_2_0a", A_AT[0])[:])
-        quantise_g(rounded_2_1[:], 1, 2 * C, place(C, U32, "words_2_1", WORDS1)[:])
-        g32_3_0 = gathers(0, 3 * C, place(PACK * C, F32, "g32_3_0", A_AT[0] + KB)[:])
-        gated_2_2 = gates[0][:].bitcast(BF16)
-        rounded_2_2 = place(PACK * C, BF16, "rounded_2_2", SLOPES + 4 * KB)
-        turn_slots(g32_2_2, (0, 2, 1, 3), group_order(4))
-        gate_slots(8, (0, 2, 1, 3), gated_2_2)
-        turn_back(gated_2_2, 0, 4, rounded_2_2)
-        turn_back(gated_2_2, 1, 5, rounded_2_2)
-        rounded_2_0b = place(PACK * HALF, BF16, "rounded_2_0b", GATE0)
-        round_g(g32_2_0[:, :, HALF:C], rounded_2_0b[:])
-        da1 = place(PACK * C, BF16, "da1", GATE0 + 2 * KB)
-        turn_da((4, 5), 6, da1[:, 0 : 2 * H])
-        turn_da((6, 7), 7, da1[:, 2 * H : 4 * H])
-        open_dh(8, 0, (0, 1))
-        open_dh(9, 2, (0, 1))
-        open_dh(10, 1, (1,))
-        open_dh(11, 3, (1,))
-        quantise_g(rounded_2_2[:], 2, 2 * C, place(C, U32, "words_2_2", WORDS1 + 2 * KB)[:])
-        for group in range(8, 12):
-            multiply2(group, 2)
-        quantise_g(rounded_2_0b[:], 0, 2 * C + HALF, words_01_0[:, 0:HALF])
-        multiply2(10, 0)
-        multiply2(11, 0)
-        parked_2 = place(GROUPS * H, F32, "parked_2", ROUNDED_01_0)
-        park(2, parked_2)
+        gather("scalar", 1, 0, rooms[1])
+        times_gate(1, rooms[1])
+        products(0)
+        quantise_g(3)
+        gather("scalar", 1, 1, rooms[2])
+        times_gate(1, rooms[2])
+        finish(0)
+        permute_words(1)
+        permute_scales(1)
+        multiply2(1, 0, 3, every, True, False)
+        quantise_g(0)
+        multiply2(1, 1, 0, every, False, False)
+        gather("scalar", 1, 2, rooms[1])
+        times_gate(1, rooms[1])
+        spread_gate(3, 1)
+        make_slopes(1)
+        quantise_g(1)
+        multiply2(1, 2, 1, every, False, True)
 
-        g32_3a_2 = gathers(2, 3 * C, place(PACK * HALF, F32, "g32_3a_2", ROOM0 + 4 * KB)[:])
-        words0 = place(C, U32, "words0", ROOM0 + 8 * KB)
-        scales0 = own(C, U8, "scales0")
-        quantise_da(da0[:], words0, scales0, 0)
-        g32_3a_1 = plain_gathers(1, 3 * C, place(PACK * HALF, F32, "g32_3a_1", ROOM0)[:])
-        g32_3b_1 = plain_gathers(1, 3 * C + HALF, place(PACK * HALF, F32, "g32_3b_1", ROOM0 + 10 * KB)[:])
-        times_on_gpsimd(2, parked_2, place(GROUPS * H, BF16, "products_2", DA0))
-        rounded_3_0 = place(PACK * C, BF16, "rounded_3_0", WORDS0)
-        round_g(g32_3_0, rounded_3_0[:])
-        dx_sb = place(SLOTS, F32, "dx_sb", A_AT[1])
-        nc.scalar.copy(dx_sb[:, 0:C], multiply1(0, 1, words0, scales0, 0)[:])
-        rounded_3a_2 = place(PACK * HALF, BF16, "rounded_3a_2", A_AT[0] + KB)
-        round_g(g32_3a_2, rounded_3a_2[:])
-        gated_3a = place(2 * H, BF16, "gated_3a", A_AT[0] + 3 * KB)
-        gated_3b = place(2 * H, BF16, "gated_3b", A_AT[0] + 5 * KB)
-        turn_slots(g32_3a_1, (4, 5), plane_order(2))
-        turn_slots(g32_3b_1, (6, 7), plane_order(2))
-        gate_slots(12, (4, 5), gated_3a)
-        gate_slots(14, (6, 7), gated_3b)
-        quantise_g(rounded_3_0[:], 0, 3 * C, place(C, U32, "words_3_0", A_AT[3] + 4 * KB)[:])
-        quantise_g(rounded_3a_2[:], 2, 3 * C, place(HALF, U32, "words_3a_2", A_AT[3] + 6 * KB)[:])
-        rounded_3a_1 = place(PACK * HALF, BF16, "rounded_3a_1", A_AT[3])
-        rounded_3b_1 = place(PACK * HALF, BF16, "rounded_3b_1", A_AT[3] + 2 * KB)
-        turn_back(gated_3a, 0, 0, rounded_3a_1)
-        turn_back(gated_3b, 0, 1, rounded_3b_1)
-        open_dh(12, 4, (0, 2))
-        open_dh(13, 5, (0, 2))
-        open_dh(14, 6, (0,))
-        open_dh(15, 7, (0,))
+        gather("scalar", 2, 0, rooms[0])
+        times_gate(0, rooms[0])
+        products(1)
+        quantise_g(2)
+        gather("scalar", 2, 1, rooms[2])
+        times_gate(0, rooms[2])
+        finish(1)
+        permute_words(2)
+        permute_scales(2)
+        multiply2(2, 0, 2, every, True, False)
+        quantise_g(3)
+        multiply2(2, 1, 3, every, False, False)
+        gather("scalar", 2, 2, rooms[1])
+        times_gate(0, rooms[1])
+        make_slopes(2)
+        quantise_g(0)
+        multiply2(2, 2, 0, every, False, True)
 
-        g32_3b_2 = gathers(2, 3 * C + HALF, place(PACK * HALF, F32, "g32_3b_2", ROOM0 + 4 * KB)[:])
-        rounded_3b_2 = place(PACK * HALF, BF16, "rounded_3b_2", A_AT[0] + 5 * KB)
-        round_g(g32_3b_2, rounded_3b_2[:])
-        words13 = on_plane(2, 2, 2 * C, U32)
-        scales13 = own(2 * C, U8, "scales13")
-        quantise_da(da1[:], words13, scales13, 0)
-        quantise_g(rounded_3a_1[:], 1, 3 * C, place(HALF, U32, "words_3a_1", A_AT[3] + 7 * KB)[:])
-        multiply2(12, 1)
-        multiply2(13, 1)
-        quantise_g(rounded_3b_1[:], 1, 3 * C + HALF, place(HALF, U32, "words_3b_1", A_AT[2] + 2 * KB)[:])
-        multiply2(14, 1)
-        multiply2(15, 1)
-        quantise_g(rounded_3b_2[:], 2, 3 * C + HALF, place(HALF, U32, "words_3b_2", A_AT[2] + 3 * KB)[:])
-        multiply2(14, 2)
-        multiply2(15, 2)
-        da2 = place(PACK * C, BF16, "da2", ROOM0 + 2 * KB)
-        turn_da((8, 9), 2, da2[:, 0 : 2 * H])
-        turn_da((10, 11), 3, da2[:, 2 * H : 4 * H])
-        nc.scalar.copy(dx_sb[:, C : 2 * C], multiply1(1, 0, words13, scales13, 0)[:])
+        gather("scalar", 3, 1, rooms[0])
+        times_gate(1, rooms[0])
+        products(2)
+        quantise_g(1)
+        permute_words(3)
+        permute_scales(3)
+        multiply2(3, 0, 4, every, True, False)
+        multiply2(3, 1, 1, every, False, False)
+        gather("scalar", 3, 2, rooms[2])
+        half = C // 2
+        times_gate(1, rooms[2], 0, half)
+        finish(2)
+        quantise_g(2, 0, half)
+        multiply2(3, 2, 2, (0, 1), False, True)
+        times_gate(1, rooms[2], half, C)
+        make_slopes(3)
+        quantise_g(2, half, C)
+        multiply2(3, 2, 2, (2, 3), False, True)
+        times_slope(3, 0)
+        times_slope(3, 1)
+        times_slope(3, 2)
+        quantise(da_sb[1], da_words[1], da_scales[1], 0, half)
+        multiply1(3, 0, half)
+        times_slope(3, 3)
+        quantise(da_sb[1], da_words[1], da_scales[1], half, C)
+        multiply1(3, half, C)
 
-        products_3 = place(GROUPS * H, BF16, "products_3", ROOM0 + 6 * KB)
-        times(12, of_group(products_3, 0))
-        times(13, of_group(products_3, 1))
-        da_12_13 = on_plane(0, 1, PACK * HALF, BF16)
-        turn_da((12, 13), 1, da_12_13[:])
-        times(14, of_group(products_3, 2))
-        da_14 = on_plane(0, 2, PACK * P, BF16)
-        turn_da((14,), 3, da_14[:])
-        times(15, of_group(products_3, 3))
-        da_15 = on_plane(0, 3, PACK * P, BF16)
-        turn_da((15,), 4, da_15[:])
-
-        words2 = on_plane(1, 0, C, U32)
-        scales2 = own(C, U8, "scales2")
-        quantise_da(da2[:], words2, scales2, 0)
-        nc.scalar.copy(dx_sb[:, 2 * C : 3 * C], multiply1(2, 2, words2, scales2, 0)[:])
-        quantise_da(da_12_13[:], words13, scales13, C)
-        quantise_da(da_14[:], words13, scales13, C + HALF)
-        dx_12_14 = multiply1(3, 5, words13, scales13, C - P)
-        quantise_da(da_15[:], words13, scales13, 2 * C - P)
-        dx_15 = multiply1(3, 6, words13, scales13, C)
-        nc.vector.tensor_copy(dx_sb[:, 3 * C : SLOTS - P], dx_12_14[:, P:C])
-        nc.scalar.copy(dx_sb[:, SLOTS - P : SLOTS], dx_15[:, C - P : C])
-
-        first = place(T, F32, "first", SLOPES + EXPERT_SLOPE_BYTES)
-        total = place(T, F32, "total", SLOPES + EXPERT_SLOPE_BYTES + 4 * KB)
-        nc.vector.tensor_copy(first[:], dx_sb[:].indirect(pos1_sb[:]))
         for lo, hi in zip(OUT_CUTS, OUT_CUTS[1:]):
+            nc.scalar.activation(first[:, lo:hi], dx_sb[:].indirect(pos1_sb[:, lo // 16 : hi // 16]), COPY)
             nc.vector.tensor_tensor(
                 total[:, lo:hi], dx_sb[:].indirect(pos2_sb[:, lo // 16 : hi // 16]), first[:, lo:hi], ADD
             )

@@ -10,9 +10,11 @@ RUN = 4
 SLOTS = E * C
 PASSES = N // 512
 GROUPS = C // P
-W2_PASS_BYTES = 2 * H
+HALF = C // 2
+UNIT = PACK * C
 W1_BYTES = 2 * K
 ALIGN = 64
+KB = 1024
 OUT_CUTS = (0, 256, 640, 896, T)
 
 FLOPS = 2 * SLOTS * (N * H + H * K)
@@ -33,6 +35,7 @@ MULT = mybir.AluOpType.mult
 ADD = mybir.AluOpType.add
 MAX = mybir.AluOpType.max
 COPY = mybir.ActivationFunctionType.Copy
+RELU = mybir.ActivationFunctionType.Relu
 
 
 def tile_moe_bdx_mlp_relu2_kernel(
@@ -41,64 +44,80 @@ def tile_moe_bdx_mlp_relu2_kernel(
     nc = tc.nc
     with ExitStack() as ctx:
         keep = ctx.enter_context(tc.tile_pool(name="keep", bufs=1))
+        placed = ctx.enter_context(tc.tile_pool(name="placed", bufs=1))
         psum = ctx.enter_context(tc.psum_pool(name="psum", bufs=1))
 
         banks = [psum.tile([P, 512], F32, name=f"bank{b}") for b in range(8)]
-        gate_banks = banks[0:2]
-        dx_banks = banks[2:4]
-        dh_banks = banks[4:8]
+        gate_bank = banks[0]
+        last_gate_bank = banks[1]
+        dx_bank = banks[2]
+        dh_banks = banks[3:8]
 
         def own(width, dtype, name):
-            return keep.tile([P, width], dtype, name=name, align_bytes=ALIGN)
+            return keep.tile([P, width], dtype, name=name, align_bytes=ALIGN)[:]
+
+        def place(width, dtype, name, at):
+            return placed.tile([P, width], dtype, name=name, offset=at, align_bytes=ALIGN)[:]
 
         def by_plane(ap):
             return ap.rearrange("p (d c) -> p d c", d=PACK)
+
+        def halves(ap):
+            return ap.bitcast(BF16)
 
         offs_sb = keep.tile([P, SLOTS // 16], U16, name="offs_sb")
         pos1_sb = keep.tile([P, T // 16], U16, name="pos1_sb")
         pos2_sb = keep.tile([P, T // 16], U16, name="pos2_sb")
         planes = [[own(T, F32, f"plane{s}_{d}") for d in range(PACK)] for s in range(PASSES)]
+        gate_rows = own(P, F32, "gate_rows")
         gate_columns = own(SLOTS // P, F32, "gate_columns")
-        w2_raw = [own(PASSES * H, U16, f"w2_raw{e}") for e in range(E)]
-        w2_sb = [own(PASSES * H, U16, f"w2_{r}") for r in range(2)] * 2
+        gate_sb = {1: place(C, F32, "gate1", 10 * KB), 2: place(C, F32, "gate2", 20 * KB), 3: own(C, F32, "gate3")}
+        w2_raw = [
+            own(PASSES * H, U16, "w2_raw0"),
+            place(PASSES * H, U16, "w2_raw1", 15 * KB),
+            own(PASSES * H, U16, "w2_raw2"),
+            own(PASSES * H, U16, "w2_raw3"),
+        ]
+        w2_lead = place(H, U16, "w2_lead", 23 * KB)
         sc_first = own(PASSES * H, U8, "sc_first")
         sc_rest = own((E - 1) * PASSES * H, U8, "sc_rest")
-        w2_sc_raw = [sc_first[:]] + [sc_rest[:, r * PASSES * H : (r + 1) * PASSES * H] for r in range(E - 1)]
-        w2_sc = [own(PASSES * H, U8, f"w2_sc{r}") for r in range(2)] * 2
+        sc_raw = [sc_first] + [sc_rest[:, r * PASSES * H : (r + 1) * PASSES * H] for r in range(E - 1)]
         w1_sb = own(E * W1_BYTES, U8, "w1_sb")
         w1_sc = own(E * K, U8, "w1_sc")
         ident = own(P, F32, "ident")
-        a_sb = [own(PACK * C, F32, f"a{e}") for e in range(E)]
-        gate_rows = own(P, F32, "gate_rows")[:]
-        rooms = [own(PACK * C, F32, f"room{r}") for r in range(5)]
-        slopes = [rooms[0], rooms[3], rooms[4], rooms[3]]
-        rounded = own(PACK * C, BF16, "rounded")
-        da_sb = [own(PACK * C, BF16, f"da{r}") for r in range(2)]
-        g_words = [own(C, U32, f"g_words{r}") for r in range(5)]
-        g_scales = [own(C, U8, f"g_scales{r}") for r in range(5)]
+        da0_a0 = own(UNIT // 2 + UNIT, F32, "da0_a0")
+        a_sb = [da0_a0[:, UNIT // 2 :]] + [own(UNIT, F32, f"a{e}") for e in range(1, E)]
+        room_a, room_b, room_c = [own(UNIT, F32, f"room_{r}") for r in "abc"]
+        room_f = own(UNIT // 2, F32, "room_f")
+        room_d = place(UNIT, F32, "room_d", 0)
+        slopes = [room_a, a_sb[0], room_a, room_b]
+        da_sb = [halves(da0_a0[:, 0 : UNIT // 2])]
         da_words = [own(C, U32, f"da_words{r}") for r in range(2)]
         da_scales = [own(C, U8, f"da_scales{r}") for r in range(2)]
         dx_sb = own(SLOTS, F32, "dx_sb")
-        first = own(T, F32, "first")
-        total = own(T, F32, "total")
+        g_words, g_scales, w2_sb, w2_sc = {}, {}, {}, {}
 
-        nc.gpsimd.memset(sc_first[:].bitcast(I32), 0)
-        nc.vector.memset(sc_rest[:].bitcast(I32), 0)
-        nc.scalar.copy(w1_sc[:].bitcast(U32), sc_rest[:, 0 : E * K].bitcast(U32))
-        make_identity(nc, ident[:])
+        nc.gpsimd.memset(sc_first.bitcast(I32), 0)
+        nc.vector.memset(sc_rest.bitcast(I32), 0)
+        nc.vector.memset(w1_sc[:, 0 : 2 * K].bitcast(I32), 0)
+        nc.scalar.copy(w1_sc[:, 2 * K : 4 * K].bitcast(U32), w1_sc[:, 0 : 2 * K].bitcast(U32))
+        make_identity(nc, ident)
 
         dy_rows = dyT.rearrange("(s p d) t -> s d p t", p=P, d=PACK)
 
-        def load_w2(e):
+        def load_w2(e, first=0):
             nc.sync.dma_start(
-                out=w2_raw[e][:].bitcast(I32).rearrange("p (s w) -> p s w", s=PASSES),
-                in_=w2_words.bitcast(I32)[e].rearrange("s p w -> p s w"),
+                out=w2_raw[e].bitcast(I32).rearrange("p (s w) -> p s w", s=PASSES)[:, first:],
+                in_=w2_words.bitcast(I32)[e].rearrange("s p w -> p s w")[:, first:],
             )
 
         def load_a(e):
             nc.sync.dma_start(
-                out=by_plane(a_sb[e][:]), in_=a[:, e * C : (e + 1) * C].rearrange("(p d) c -> p d c", d=PACK)
+                out=by_plane(a_sb[e]), in_=a[:, e * C : (e + 1) * C].rearrange("(p d) c -> p d c", d=PACK)
             )
+
+        def load_gate(e):
+            nc.sync.dma_start(out=gate_sb[e], in_=gate[0:P, e * C : (e + 1) * C])
 
         def load_scales(tile, source, runs):
             src = source.bitcast(I32).rearrange("e s f w -> f (e s) w")
@@ -111,83 +130,116 @@ def tile_moe_bdx_mlp_relu2_kernel(
         nc.sync.dma_start(offs_sb[:], offs)
         for s in range(PASSES):
             for d in range(PACK):
-                nc.sync.dma_start(out=planes[s][d][:], in_=dy_rows[s, d])
+                nc.sync.dma_start(out=planes[s][d], in_=dy_rows[s, d])
+                if (s, d) == (0, 0):
+                    nc.sync.dma_start(
+                        out=gate_rows, in_=gate[0 : P * P // SLOTS, :].rearrange("r (x c) -> (r x) c", c=P)
+                    )
             if s == 0:
-                nc.sync.dma_start(
-                    out=gate_rows, in_=gate[0 : P * P // SLOTS, :].rearrange("r (x c) -> (r x) c", c=P)
-                )
-        load_w2(0)
+                load_gate(3)
+        nc.sync.dma_start(out=w2_lead.bitcast(I32), in_=w2_words.bitcast(I32)[0, 0])
+        load_w2(0, 1)
         load_scales(sc_first, w2_scales[0:1], PASSES)
         load_a(0)
-        for e in range(1, E):
-            load_w2(e)
-            load_a(e)
+        load_gate(1)
+        load_w2(1)
         load_scales(sc_rest, w2_scales[1:E], (E - 1) * PASSES)
+        load_a(1)
+        load_gate(2)
+        load_w2(2)
         load_scales(w1_sc, w1_scales, E)
         nc.sync.dma_start(
-            out=w1_sb[:].bitcast(I32).rearrange("p (e w) -> p e w", e=E),
+            out=w1_sb.bitcast(I32).rearrange("p (e w) -> p e w", e=E),
             in_=w1_words.bitcast(I32).rearrange("e s p w -> p (e s) w"),
         )
+        load_a(2)
+        load_w2(3)
+        load_a(3)
         nc.sync.dma_start(pos1_sb[:], pos1)
         nc.sync.dma_start(pos2_sb[:], pos2)
 
         def gather(engine, e, s, room, lo=0, hi=C):
+            width = hi - lo
             for d in range(PACK):
-                window = planes[s][d][:].indirect(offs_sb[:, (e * C + lo) // 16 : (e * C + hi) // 16])
+                window = planes[s][d].indirect(offs_sb[:, (e * C + lo) // 16 : (e * C + hi) // 16])
                 if engine == "scalar":
-                    nc.scalar.activation(room[:, d * C + lo : d * C + hi], window, COPY)
+                    nc.scalar.activation(room[:, d * width : (d + 1) * width], window, COPY)
                 else:
-                    nc.vector.tensor_copy(room[:, d * C + lo : d * C + hi], window)
+                    nc.vector.tensor_copy(room[:, d * width : (d + 1) * width], window)
 
-        def in_runs(ap, lo, hi):
-            return by_plane(ap)[:, :, lo:hi].rearrange("p d (c r) -> p c d r", r=RUN)
+        def in_runs(ap):
+            return ap.rearrange("p (d c r) -> p c d r", d=PACK, r=RUN)
 
-        def woven(ap, lo, hi):
-            return ap[:, PACK * lo : PACK * hi].rearrange("p (c r d) -> p c d r", r=RUN, d=PACK)
+        def woven(ap):
+            return ap.rearrange("p (c r d) -> p c d r", r=RUN, d=PACK)
 
         def spread_gate(e, bank):
             for x in range(GROUPS):
                 column = e * GROUPS + x
                 nc.tensor.transpose(
-                    gate_banks[bank][:, x * P : (x + 1) * P],
-                    gate_columns[:, column : column + 1].to_broadcast([P, P]),
-                    ident[:],
+                    bank[:, x * P : (x + 1) * P], gate_columns[:, column : column + 1].to_broadcast([P, P]), ident
                 )
 
-        def times_gate(bank, room, lo=0, hi=C):
-            gates = gate_banks[bank][:, lo:hi].rearrange("p (c r) -> p c r", r=RUN)
+        def times_gate(gates, room, dest):
+            width = gates.shape[1]
+            runs = gates.rearrange("p (c r) -> p c r", r=RUN)
             nc.vector.tensor_tensor(
-                woven(rounded[:], lo, hi),
-                in_runs(room[:], lo, hi),
-                gates.unsqueeze(2).to_broadcast([P, (hi - lo) // RUN, PACK, RUN]),
+                woven(dest), in_runs(room), runs.unsqueeze(2).to_broadcast([P, width // RUN, PACK, RUN]), MULT
+            )
+            return dest
+
+        def times_gate_on_gpsimd(gates, room, dest):
+            width = gates.shape[1]
+            nc.gpsimd.tensor_tensor(
+                dest.rearrange("p (c d) -> p c d", d=PACK),
+                room.rearrange("p (d c) -> p c d", d=PACK),
+                gates.unsqueeze(2).to_broadcast([P, width, PACK]),
                 MULT,
             )
+            return dest
 
-        def quantise(source, words, scales, lo=0, hi=C):
-            nc.vector.quantize_mx(
-                out=words[:, lo:hi].bitcast(E5M2), scales=scales[:, lo:hi], in_=source[:, PACK * lo : PACK * hi]
-            )
+        def quantise(source, words, scales, lo):
+            hi = lo + source.shape[1] // PACK
+            nc.vector.quantize_mx(out=words[:, lo:hi].bitcast(E5M2), scales=scales[:, lo:hi], in_=source)
 
-        def permute_words(e):
+        def quantise_g(e, s, source, lo=0):
+            if (e, s) not in g_scales:
+                g_scales[e, s] = own(C, U8, f"g_scales{e}_{s}")
+                if (e, s) not in g_words:
+                    g_words[e, s] = own(C, U32, f"g_words{e}_{s}")
+            quantise(source, g_words[e, s], g_scales[e, s], lo)
+
+        def permute_words(dest, source):
             nc.vector.tensor_copy(
-                w2_sb[e][:].rearrange("p (s t m) -> p t s m", s=PASSES, t=PACK),
-                w2_raw[e][:].rearrange("p (s m t) -> p t s m", s=PASSES, t=PACK),
+                dest.rearrange("p (s t m) -> p t s m", m=P, t=PACK),
+                source.rearrange("p (s m t) -> p t s m", m=P, t=PACK),
             )
 
-        def permute_scales(e):
+        def permute_scales(e, dest):
+            w2_sc[e] = dest
             nc.vector.tensor_copy(
-                w2_sc[e][:].rearrange("p (s t m) -> p t s m", s=PASSES, t=PACK),
-                w2_sc_raw[e].rearrange("p (s m t) -> p t s m", s=PASSES, t=PACK),
+                dest.rearrange("p (s t m) -> p t s m", s=PASSES, t=PACK),
+                sc_raw[e].rearrange("p (s m t) -> p t s m", s=PASSES, t=PACK),
             )
 
-        def make_slopes(e):
-            nc.vector.tensor_scalar(slopes[e][:], a_sb[e][:], 0.0, 2.0, MAX, MULT)
+        def by_group(e):
+            return (
+                slopes[e].rearrange("p (x d c) -> p x d c", x=GROUPS, d=PACK),
+                a_sb[e].rearrange("p (d x c) -> p x d c", x=GROUPS, d=PACK),
+            )
+
+        def slopes_on_vector(e):
+            dest, source = by_group(e)
+            nc.vector.tensor_scalar(dest, source, 0.0, 2.0, MAX, MULT)
+
+        def slopes_on_scalar(e, lo, hi):
+            dest, source = by_group(e)
+            nc.scalar.activation(dest[:, lo:hi], source[:, lo:hi], RELU, scale=2.0)
 
         def dh_bank(e, x):
             return dh_banks[(e * GROUPS + x) % len(dh_banks)]
 
-        def multiply2(e, s, codes, groups, opens, closes):
-            words, scales = g_words[codes], g_scales[codes]
+        def multiply2(e, s, groups, opens, closes):
             for x in groups:
                 for t in range(PACK):
                     at = s * H + t * P
@@ -195,23 +247,25 @@ def tile_moe_bdx_mlp_relu2_kernel(
                         out=dh_bank(e, x)[:, t * P : (t + 1) * P],
                         lhsT=w2_sb[e][:, at : at + P].bitcast(U8).bitcast(E2M1),
                         lhsT_scale=w2_sc[e][:, at : at + P],
-                        rhs=words[:, x * P : (x + 1) * P].bitcast(E5M2),
-                        rhs_scale=scales[:, x * P : (x + 1) * P],
+                        rhs=g_words[e, s][:, x * P : (x + 1) * P].bitcast(E5M2),
+                        rhs_scale=g_scales[e, s][:, x * P : (x + 1) * P],
                         start=(opens and t == 0),
                         stop=(closes and t == PACK - 1),
                     )
 
-        def times_slope(e, x):
-            nc.vector.tensor_tensor(
-                woven(da_sb[e % 2][:], x * P, (x + 1) * P),
-                dh_bank(e, x)[:].rearrange("p (d c r) -> p c d r", d=PACK, r=RUN),
-                in_runs(slopes[e][:], x * P, (x + 1) * P),
-                MULT,
-            )
+        def times_slope(e, groups):
+            for x in groups:
+                nc.vector.tensor_tensor(
+                    woven(da_sb[e % 2][:, x * H : (x + 1) * H]),
+                    in_runs(dh_bank(e, x)[:]),
+                    in_runs(slopes[e][:, x * H : (x + 1) * H]),
+                    MULT,
+                )
 
         def multiply1(e, lo=0, hi=C):
+            quantise(da_sb[e % 2][:, PACK * lo : PACK * hi], da_words[e % 2], da_scales[e % 2], lo)
             nc.tensor.matmul_mx(
-                out=dx_banks[e % 2][:, lo:hi],
+                out=dx_bank[:, lo:hi],
                 lhsT=w1_sb[:, e * W1_BYTES : (e + 1) * W1_BYTES].bitcast(E2M1),
                 lhsT_scale=w1_sc[:, e * K : (e + 1) * K],
                 rhs=da_words[e % 2][:, lo:hi].bitcast(E5M2),
@@ -219,114 +273,124 @@ def tile_moe_bdx_mlp_relu2_kernel(
                 start=True,
                 stop=True,
             )
-            nc.scalar.copy(dx_sb[:, e * C + lo : e * C + hi], dx_banks[e % 2][:, lo:hi])
 
-        def finish(e):
-            quantise(da_sb[e % 2], da_words[e % 2], da_scales[e % 2])
-            multiply1(e)
+        def empty_dx(e, lo=0, hi=C):
+            nc.scalar.copy(dx_sb[:, e * C + lo : e * C + hi], dx_bank[:, lo:hi])
 
         every = range(GROUPS)
+        rounded = UNIT // 2
 
-        def quantise_g(codes, lo=0, hi=C):
-            quantise(rounded, g_words[codes], g_scales[codes], lo, hi)
+        nc.tensor.transpose(dx_bank[:, 0:P], gate_rows, ident)
+        nc.vector.tensor_copy(gate_columns, dx_bank[:, 0 : SLOTS // P])
+        spread_gate(0, gate_bank)
+        spread_gate(3, last_gate_bank)
 
-        def products(e):
-            for x in every:
-                times_slope(e, x)
+        gather("scalar", 0, 0, room_a)
+        gather("vector", 3, 0, room_d)
+        g30 = times_gate_on_gpsimd(gate_sb[3], room_d, own(UNIT, BF16, "g30"))
+        gather("scalar", 0, 1, room_b)
+        gather("vector", 3, 1, room_f, 0, HALF)
+        gather("scalar", 0, 2, room_c)
+        g00 = times_gate(gate_bank[:], room_a, own(UNIT, BF16, "g00"))
+        g01 = times_gate(gate_bank[:], room_b, own(UNIT, BF16, "g01"))
+        g_words[0, 0] = place(C, U32, "g_words0_0", 0)
+        quantise_g(0, 0, g00)
+        quantise_g(0, 1, g01)
+        quantise_g(3, 0, g30)
+        w2_sb[0] = own(PASSES * H, U16, "w2_0")
+        permute_words(w2_sb[0][:, 0:H], w2_lead)
+        g02 = times_gate(gate_bank[:], room_c, halves(room_b[:, 0:rounded]))
+        spread_gate(1, gate_bank)
+        permute_words(w2_sb[0][:, H:], w2_raw[0][:, H:])
+        quantise_g(0, 2, g02)
+        permute_scales(0, own(PASSES * H, U8, "w2_sc0"))
+        for x in every:
+            for s in range(PASSES):
+                multiply2(0, s, (x,), s == 0, s == PASSES - 1)
+        slopes_on_vector(0)
 
-        nc.tensor.transpose(dx_banks[0][:, 0:P], gate_rows, ident[:])
-        nc.vector.tensor_copy(gate_columns[:], dx_banks[0][:, 0 : SLOTS // P])
-        spread_gate(0, 0)
-        spread_gate(3, 1)
+        room_g = place(UNIT, F32, "room_g", 23 * KB)
+        da_sb.append(halves(room_g[:, 0:rounded]))
+        gather("scalar", 1, 0, room_g)
+        g10 = times_gate_on_gpsimd(gate_sb[1], room_g, halves(a_sb[0][:, rounded:]))
+        gather("scalar", 1, 1, room_c)
+        g31a = times_gate(last_gate_bank[:, 0:HALF], room_f, halves(a_sb[0][:, 0 : rounded // 2]))
+        times_slope(0, (0, 1))
+        g11 = times_gate(gate_bank[:], room_c, halves(room_a[:, 0:rounded]))
+        times_slope(0, (2, 3))
+        quantise_g(1, 0, g10)
+        quantise_g(1, 1, g11)
+        quantise_g(3, 1, g31a)
+        multiply1(0)
+        w2_sb[1] = place(PASSES * H, U16, "w2_1", 8 * KB)
+        permute_words(w2_sb[1], w2_raw[1])
+        permute_scales(1, place(PASSES * H, U8, "w2_sc1", 11 * KB))
+        multiply2(1, 0, every, True, False)
+        multiply2(1, 1, every, False, False)
+        gather("scalar", 1, 2, room_b)
+        g12 = times_gate(gate_bank[:], room_b, halves(da0_a0[:, rounded // 2 : 3 * rounded // 2]))
+        spread_gate(2, gate_bank)
+        w2_sb[2] = place(PASSES * H, U16, "w2_2", 13 * KB + KB // 2)
+        permute_words(w2_sb[2], w2_raw[2])
+        permute_scales(2, place(PASSES * H, U8, "w2_sc2", 16 * KB + KB // 2))
+        quantise_g(1, 2, g12)
+        multiply2(1, 2, every, False, True)
+        slopes_on_vector(1)
 
-        gather("scalar", 0, 0, rooms[0])
-        gather("vector", 3, 0, rooms[3])
-        gather("scalar", 0, 1, rooms[1])
-        gather("scalar", 0, 2, rooms[2])
-        times_gate(0, rooms[0])
-        quantise_g(0)
-        times_gate(1, rooms[3])
-        spread_gate(1, 1)
-        quantise_g(4)
-        times_gate(0, rooms[1])
-        permute_words(0)
-        quantise_g(1)
-        permute_scales(0)
-        multiply2(0, 0, 0, every, True, False)
-        multiply2(0, 1, 1, every, False, False)
-        times_gate(0, rooms[2])
-        spread_gate(2, 0)
-        make_slopes(0)
-        quantise_g(2)
-        multiply2(0, 2, 2, every, False, True)
+        gather("scalar", 2, 0, room_c)
+        empty_dx(0)
+        g20 = times_gate_on_gpsimd(gate_sb[2], room_c, halves(a_sb[1][:, 0:rounded]))
+        gather("scalar", 2, 1, room_a)
+        times_slope(1, (0, 1))
+        g21 = times_gate(gate_bank[:], room_a, halves(a_sb[0][:, 0:rounded]))
+        times_slope(1, (2, 3))
+        quantise_g(2, 0, g20)
+        multiply2(2, 0, every, True, False)
+        quantise_g(2, 1, g21)
+        multiply2(2, 1, every, False, False)
+        multiply1(1)
+        gather("scalar", 2, 2, room_b)
+        g22 = times_gate(gate_bank[:], room_b, da_sb[1])
+        w2_sb[3] = place(PASSES * H, U16, "w2_3", 18 * KB)
+        permute_words(w2_sb[3], w2_raw[3])
+        quantise_g(2, 2, g22)
+        multiply2(2, 2, every, False, True)
+        permute_scales(3, place(PASSES * H, U8, "w2_sc3", 21 * KB))
 
-        gather("scalar", 1, 0, rooms[1])
-        times_gate(1, rooms[1])
-        products(0)
-        quantise_g(3)
-        gather("scalar", 1, 1, rooms[2])
-        times_gate(1, rooms[2])
-        finish(0)
-        permute_words(1)
-        permute_scales(1)
-        multiply2(1, 0, 3, every, True, False)
-        quantise_g(0)
-        multiply2(1, 1, 0, every, False, False)
-        gather("scalar", 1, 2, rooms[1])
-        times_gate(1, rooms[1])
-        spread_gate(3, 1)
-        make_slopes(1)
-        quantise_g(1)
-        multiply2(1, 2, 1, every, False, True)
+        gather("scalar", 3, 1, a_sb[1][:, rounded:], HALF, C)
+        empty_dx(1)
+        slopes_on_scalar(2, 0, GROUPS)
+        gather("scalar", 3, 2, room_c[:, 0:rounded], 0, HALF)
+        gather("scalar", 3, 2, room_c[:, rounded:], HALF, C)
+        slopes_on_scalar(3, 0, 2)
+        slopes_on_scalar(3, 2, GROUPS)
+        g31b = times_gate_on_gpsimd(gate_sb[3][:, HALF:C], a_sb[1][:, rounded:], da_sb[1][:, 0:rounded])
+        times_slope(2, (0, 1))
+        multiply2(3, 0, (0, 1), True, False)
+        multiply2(3, 1, (0, 1), False, False)
+        g32a = times_gate(last_gate_bank[:, 0:HALF], room_c[:, 0:rounded], halves(room_a[:, 0:H]))
+        times_slope(2, (2, 3))
+        quantise_g(3, 1, g31b, HALF)
+        multiply2(3, 0, (2, 3), True, False)
+        multiply2(3, 1, (2, 3), False, False)
+        quantise_g(3, 2, g32a)
+        multiply2(3, 2, (0, 1), False, True)
+        g32b = times_gate(last_gate_bank[:, HALF:C], room_c[:, rounded:], halves(room_a[:, 3 * H :]))
+        multiply1(2)
+        empty_dx(2)
+        quantise_g(3, 2, g32b, HALF)
+        multiply2(3, 2, (2, 3), False, True)
+        times_slope(3, (0, 1, 2))
+        multiply1(3, 0, HALF)
+        empty_dx(3, 0, HALF)
+        times_slope(3, (3,))
+        multiply1(3, HALF, C)
+        empty_dx(3, HALF, C)
 
-        gather("scalar", 2, 0, rooms[0])
-        times_gate(0, rooms[0])
-        products(1)
-        quantise_g(2)
-        gather("scalar", 2, 1, rooms[2])
-        times_gate(0, rooms[2])
-        finish(1)
-        permute_words(2)
-        permute_scales(2)
-        multiply2(2, 0, 2, every, True, False)
-        quantise_g(3)
-        multiply2(2, 1, 3, every, False, False)
-        gather("scalar", 2, 2, rooms[1])
-        times_gate(0, rooms[1])
-        make_slopes(2)
-        quantise_g(0)
-        multiply2(2, 2, 0, every, False, True)
-
-        gather("scalar", 3, 1, rooms[0])
-        times_gate(1, rooms[0])
-        products(2)
-        quantise_g(1)
-        permute_words(3)
-        permute_scales(3)
-        multiply2(3, 0, 4, every, True, False)
-        multiply2(3, 1, 1, every, False, False)
-        gather("scalar", 3, 2, rooms[2])
-        half = C // 2
-        times_gate(1, rooms[2], 0, half)
-        finish(2)
-        quantise_g(2, 0, half)
-        multiply2(3, 2, 2, (0, 1), False, True)
-        times_gate(1, rooms[2], half, C)
-        make_slopes(3)
-        quantise_g(2, half, C)
-        multiply2(3, 2, 2, (2, 3), False, True)
-        times_slope(3, 0)
-        times_slope(3, 1)
-        times_slope(3, 2)
-        quantise(da_sb[1], da_words[1], da_scales[1], 0, half)
-        multiply1(3, 0, half)
-        times_slope(3, 3)
-        quantise(da_sb[1], da_words[1], da_scales[1], half, C)
-        multiply1(3, half, C)
-
+        first, total = a_sb[2], a_sb[3]
         for lo, hi in zip(OUT_CUTS, OUT_CUTS[1:]):
-            nc.scalar.activation(first[:, lo:hi], dx_sb[:].indirect(pos1_sb[:, lo // 16 : hi // 16]), COPY)
+            nc.scalar.activation(first[:, lo:hi], dx_sb.indirect(pos1_sb[:, lo // 16 : hi // 16]), COPY)
             nc.vector.tensor_tensor(
-                total[:, lo:hi], dx_sb[:].indirect(pos2_sb[:, lo // 16 : hi // 16]), first[:, lo:hi], ADD
+                total[:, lo:hi], dx_sb.indirect(pos2_sb[:, lo // 16 : hi // 16]), first[:, lo:hi], ADD
             )
             nc.sync.dma_start(out=out[:, lo:hi], in_=total[:, lo:hi])

@@ -15,7 +15,8 @@ UNIT = PACK * C
 W1_BYTES = 2 * K
 ALIGN = 64
 KB = 1024
-OUT_CUTS = (0, 256, 640, 896, T)
+OUT_CUTS = (0, 192, 448, 704, 896, T)
+LAST_CUTS = (0, 256, 384, C)
 
 FLOPS = 2 * SLOTS * (N * H + H * K)
 BYTES = (
@@ -71,29 +72,29 @@ def tile_moe_bdx_mlp_relu2_kernel(
         planes = [[own(T, F32, f"plane{s}_{d}") for d in range(PACK)] for s in range(PASSES)]
         gate_rows = own(P, F32, "gate_rows")
         gate_columns = own(SLOTS // P, F32, "gate_columns")
-        gate_sb = {1: place(C, F32, "gate1", 10 * KB), 2: place(C, F32, "gate2", 20 * KB), 3: own(C, F32, "gate3")}
+        gate_sb = {0: own(P, F32, "gate0"), 1: own(P, F32, "gate1"), 2: own(C, F32, "gate2"), 3: own(C, F32, "gate3")}
         w2_raw = [
             own(PASSES * H, U16, "w2_raw0"),
-            place(PASSES * H, U16, "w2_raw1", 15 * KB),
+            place(PASSES * H, U16, "w2_raw1", 16 * KB),
             own(PASSES * H, U16, "w2_raw2"),
             own(PASSES * H, U16, "w2_raw3"),
         ]
-        w2_lead = place(H, U16, "w2_lead", 23 * KB)
+        w2_lead = place(H, U16, "w2_lead", 30 * KB)
         sc_first = own(PASSES * H, U8, "sc_first")
         sc_rest = own((E - 1) * PASSES * H, U8, "sc_rest")
         sc_raw = [sc_first] + [sc_rest[:, r * PASSES * H : (r + 1) * PASSES * H] for r in range(E - 1)]
         w1_sb = own(E * W1_BYTES, U8, "w1_sb")
         w1_sc = own(E * K, U8, "w1_sc")
         ident = own(P, F32, "ident")
-        da0_a0 = own(UNIT // 2 + UNIT, F32, "da0_a0")
-        a_sb = [da0_a0[:, UNIT // 2 :]] + [own(UNIT, F32, f"a{e}") for e in range(1, E)]
+        room_x = own(UNIT, F32, "room_x")
+        a_sb = [place(UNIT, F32, "a0", 22 * KB)] + [own(UNIT, F32, f"a{e}") for e in range(1, E)]
         room_a, room_b, room_c = [own(UNIT, F32, f"room_{r}") for r in "abc"]
-        room_f = own(UNIT // 2, F32, "room_f")
+        room_f = place(UNIT // 2, F32, "room_f", 9 * KB)
         room_d = place(UNIT, F32, "room_d", 0)
-        slopes = [room_a, a_sb[0], room_a, room_b]
-        da_sb = [halves(da0_a0[:, 0 : UNIT // 2])]
+        slopes = [room_a, room_x, room_x, room_c]
+        da_sb = [halves(room_x[:, 0 : UNIT // 2])]
         da_words = [own(C, U32, f"da_words{r}") for r in range(2)]
-        da_scales = [own(C, U8, f"da_scales{r}") for r in range(2)]
+        da_scales = [own(C, U8, "da_scales0")]
         dx_sb = own(SLOTS, F32, "dx_sb")
         g_words, g_scales, w2_sb, w2_sc = {}, {}, {}, {}
 
@@ -105,10 +106,10 @@ def tile_moe_bdx_mlp_relu2_kernel(
 
         dy_rows = dyT.rearrange("(s p d) t -> s d p t", p=P, d=PACK)
 
-        def load_w2(e, first=0):
+        def load_w2(e, passes=PASSES):
             nc.sync.dma_start(
-                out=w2_raw[e].bitcast(I32).rearrange("p (s w) -> p s w", s=PASSES)[:, first:],
-                in_=w2_words.bitcast(I32)[e].rearrange("s p w -> p s w")[:, first:],
+                out=w2_raw[e].bitcast(I32).rearrange("p (s w) -> p s w", s=PASSES)[:, 0:passes],
+                in_=w2_words.bitcast(I32)[e].rearrange("s p w -> p s w")[:, 0:passes],
             )
 
         def load_a(e):
@@ -117,7 +118,7 @@ def tile_moe_bdx_mlp_relu2_kernel(
             )
 
         def load_gate(e):
-            nc.sync.dma_start(out=gate_sb[e], in_=gate[0:P, e * C : (e + 1) * C])
+            nc.sync.dma_start(out=gate_sb[e], in_=gate[0:P, (e + 1) * C - gate_sb[e].shape[1] : (e + 1) * C])
 
         def load_scales(tile, source, runs):
             src = source.bitcast(I32).rearrange("e s f w -> f (e s) w")
@@ -130,6 +131,9 @@ def tile_moe_bdx_mlp_relu2_kernel(
         nc.sync.dma_start(offs_sb[:], offs)
         for s in range(PASSES):
             for d in range(PACK):
+                if (s, d) == (PASSES - 1, PACK - 1):
+                    load_w2(0, PASSES - 1)
+                    load_scales(sc_first, w2_scales[0:1], PASSES)
                 nc.sync.dma_start(out=planes[s][d], in_=dy_rows[s, d])
                 if (s, d) == (0, 0):
                     nc.sync.dma_start(
@@ -137,15 +141,15 @@ def tile_moe_bdx_mlp_relu2_kernel(
                     )
             if s == 0:
                 load_gate(3)
-        nc.sync.dma_start(out=w2_lead.bitcast(I32), in_=w2_words.bitcast(I32)[0, 0])
-        load_w2(0, 1)
-        load_scales(sc_first, w2_scales[0:1], PASSES)
+            if s == 1:
+                load_gate(0)
+        nc.sync.dma_start(out=w2_lead.bitcast(I32), in_=w2_words.bitcast(I32)[0, PASSES - 1])
         load_a(0)
+        load_gate(2)
         load_gate(1)
         load_w2(1)
         load_scales(sc_rest, w2_scales[1:E], (E - 1) * PASSES)
         load_a(1)
-        load_gate(2)
         load_w2(2)
         load_scales(w1_sc, w1_scales, E)
         nc.sync.dma_start(
@@ -198,6 +202,27 @@ def tile_moe_bdx_mlp_relu2_kernel(
             )
             return dest
 
+        def times_gate_shared(e, bank, room, dest, lo=0, hi=C):
+            width = hi - lo
+            cut = width - width // 4
+            planes_of_room = by_plane(room)
+            runs = bank[:, lo : lo + cut].rearrange("p (c r) -> p c r", r=RUN)
+            nc.gpsimd.tensor_tensor(
+                dest[:, PACK * cut :].rearrange("p (c d) -> p c d", d=PACK),
+                planes_of_room[:, :, cut:].rearrange("p d c -> p c d"),
+                gate_sb[e][:, gate_sb[e].shape[1] - C + lo + cut : gate_sb[e].shape[1] - C + hi]
+                .unsqueeze(2)
+                .to_broadcast([P, width - cut, PACK]),
+                MULT,
+            )
+            nc.vector.tensor_tensor(
+                woven(dest[:, 0 : PACK * cut]),
+                planes_of_room[:, :, 0:cut].rearrange("p d (c r) -> p c d r", r=RUN),
+                runs.unsqueeze(2).to_broadcast([P, cut // RUN, PACK, RUN]),
+                MULT,
+            )
+            return dest
+
         def quantise(source, words, scales, lo):
             hi = lo + source.shape[1] // PACK
             nc.vector.quantize_mx(out=words[:, lo:hi].bitcast(E5M2), scales=scales[:, lo:hi], in_=source)
@@ -205,8 +230,8 @@ def tile_moe_bdx_mlp_relu2_kernel(
         def quantise_g(e, s, source, lo=0):
             if (e, s) not in g_scales:
                 g_scales[e, s] = own(C, U8, f"g_scales{e}_{s}")
-                if (e, s) not in g_words:
-                    g_words[e, s] = own(C, U32, f"g_words{e}_{s}")
+            if (e, s) not in g_words:
+                g_words[e, s] = own(C, U32, f"g_words{e}_{s}")
             quantise(source, g_words[e, s], g_scales[e, s], lo)
 
         def permute_words(dest, source):
@@ -256,16 +281,16 @@ def tile_moe_bdx_mlp_relu2_kernel(
         def times_slope(e, groups):
             for x in groups:
                 nc.vector.tensor_tensor(
-                    woven(da_sb[e % 2][:, x * H : (x + 1) * H]),
+                    woven(da_sb[e][:, x * H : (x + 1) * H]),
                     in_runs(dh_bank(e, x)[:]),
                     in_runs(slopes[e][:, x * H : (x + 1) * H]),
                     MULT,
                 )
 
-        def multiply1(e, lo=0, hi=C):
-            quantise(da_sb[e % 2][:, PACK * lo : PACK * hi], da_words[e % 2], da_scales[e % 2], lo)
+        def multiply1(e, lo=0, hi=C, bank=dx_bank):
+            quantise(da_sb[e][:, PACK * lo : PACK * hi], da_words[e % 2], da_scales[e % 2], lo)
             nc.tensor.matmul_mx(
-                out=dx_bank[:, lo:hi],
+                out=bank[:, lo:hi],
                 lhsT=w1_sb[:, e * W1_BYTES : (e + 1) * W1_BYTES].bitcast(E2M1),
                 lhsT_scale=w1_sc[:, e * K : (e + 1) * K],
                 rhs=da_words[e % 2][:, lo:hi].bitcast(E5M2),
@@ -289,107 +314,115 @@ def tile_moe_bdx_mlp_relu2_kernel(
         gather("vector", 3, 0, room_d)
         g30 = times_gate_on_gpsimd(gate_sb[3], room_d, own(UNIT, BF16, "g30"))
         gather("scalar", 0, 1, room_b)
-        gather("vector", 3, 1, room_f, 0, HALF)
+        gather("vector", 2, 0, room_f, 0, HALF)
         gather("scalar", 0, 2, room_c)
         g00 = times_gate(gate_bank[:], room_a, own(UNIT, BF16, "g00"))
-        g01 = times_gate(gate_bank[:], room_b, own(UNIT, BF16, "g01"))
+        g01 = times_gate_shared(0, gate_bank, room_b, own(UNIT, BF16, "g01"))
         g_words[0, 0] = place(C, U32, "g_words0_0", 0)
         quantise_g(0, 0, g00)
         quantise_g(0, 1, g01)
-        quantise_g(3, 0, g30)
         w2_sb[0] = own(PASSES * H, U16, "w2_0")
-        permute_words(w2_sb[0][:, 0:H], w2_lead)
-        g02 = times_gate(gate_bank[:], room_c, halves(room_b[:, 0:rounded]))
-        spread_gate(1, gate_bank)
-        permute_words(w2_sb[0][:, H:], w2_raw[0][:, H:])
-        quantise_g(0, 2, g02)
+        permute_words(w2_sb[0][:, 0 : 2 * H], w2_raw[0][:, 0 : 2 * H])
         permute_scales(0, own(PASSES * H, U8, "w2_sc0"))
-        for x in every:
-            for s in range(PASSES):
-                multiply2(0, s, (x,), s == 0, s == PASSES - 1)
+        multiply2(0, 0, every, True, False)
+        multiply2(0, 1, every, False, False)
+        permute_words(w2_sb[0][:, 2 * H :], w2_lead)
+        g02 = times_gate_shared(0, gate_bank, room_c, halves(room_b[:, 0:rounded]))
+        quantise_g(3, 0, g30)
+        quantise_g(0, 2, g02)
+        multiply2(0, 2, every, False, True)
+        spread_gate(1, gate_bank)
         slopes_on_vector(0)
 
-        room_g = place(UNIT, F32, "room_g", 23 * KB)
-        da_sb.append(halves(room_g[:, 0:rounded]))
+        room_g = place(UNIT, F32, "room_g", 30 * KB)
+        middle, upper = halves(room_a[:, H : 3 * H]), halves(room_a[:, 2 * H :])
         gather("scalar", 1, 0, room_g)
-        g10 = times_gate_on_gpsimd(gate_sb[1], room_g, halves(a_sb[0][:, rounded:]))
+        g20a = times_gate_on_gpsimd(gate_sb[2][:, 0:HALF], room_f, halves(a_sb[0][:, rounded : rounded + H]))
+        gather("vector", 2, 0, a_sb[0][:, 0:rounded], HALF, C)
         gather("scalar", 1, 1, room_c)
-        g31a = times_gate(last_gate_bank[:, 0:HALF], room_f, halves(a_sb[0][:, 0 : rounded // 2]))
-        times_slope(0, (0, 1))
-        g11 = times_gate(gate_bank[:], room_c, halves(room_a[:, 0:rounded]))
-        times_slope(0, (2, 3))
-        quantise_g(1, 0, g10)
-        quantise_g(1, 1, g11)
-        quantise_g(3, 1, g31a)
-        multiply1(0)
+        gather("scalar", 1, 2, room_b)
+        times_slope(0, every)
+        quantise_g(2, 0, g20a)
         w2_sb[1] = place(PASSES * H, U16, "w2_1", 8 * KB)
         permute_words(w2_sb[1], w2_raw[1])
         permute_scales(1, place(PASSES * H, U8, "w2_sc1", 11 * KB))
-        multiply2(1, 0, every, True, False)
-        multiply2(1, 1, every, False, False)
-        gather("scalar", 1, 2, room_b)
-        g12 = times_gate(gate_bank[:], room_b, halves(da0_a0[:, rounded // 2 : 3 * rounded // 2]))
-        spread_gate(2, gate_bank)
         w2_sb[2] = place(PASSES * H, U16, "w2_2", 13 * KB + KB // 2)
         permute_words(w2_sb[2], w2_raw[2])
-        permute_scales(2, place(PASSES * H, U8, "w2_sc2", 16 * KB + KB // 2))
-        quantise_g(1, 2, g12)
-        multiply2(1, 2, every, False, True)
+        permute_scales(2, place(PASSES * H, U8, "w2_sc2", 17 * KB))
+        multiply1(0)
+        times_gate_shared(1, gate_bank, room_g, middle)
         slopes_on_vector(1)
+        quantise_g(1, 0, middle)
+        multiply2(1, 0, every, True, False)
+        times_gate_shared(1, gate_bank, room_c, middle)
+        quantise_g(1, 1, middle)
+        multiply2(1, 1, every, False, False)
+        times_gate_shared(1, gate_bank, room_b, middle)
+        spread_gate(2, gate_bank)
+        quantise_g(1, 2, middle)
+        multiply2(1, 2, every, False, True)
 
-        gather("scalar", 2, 0, room_c)
+        gather("scalar", 2, 1, room_g)
         empty_dx(0)
-        g20 = times_gate_on_gpsimd(gate_sb[2], room_c, halves(a_sb[1][:, 0:rounded]))
-        gather("scalar", 2, 1, room_a)
-        times_slope(1, (0, 1))
-        g21 = times_gate(gate_bank[:], room_a, halves(a_sb[0][:, 0:rounded]))
-        times_slope(1, (2, 3))
-        quantise_g(2, 0, g20)
+        gather("scalar", 2, 2, room_c)
+        times_gate_shared(2, gate_bank, room_g, upper)
+        g20b = times_gate_on_gpsimd(gate_sb[2][:, HALF:C], a_sb[0][:, 0:rounded], halves(room_a[:, H : 2 * H]))
+        da_sb.append(g30)
+        times_slope(1, every)
+        g_scales[2, 1] = place(C, U8, "g_scales2_1", 23 * KB)
+        quantise_g(2, 1, upper)
+        quantise_g(2, 0, g20b, HALF)
         multiply2(2, 0, every, True, False)
-        quantise_g(2, 1, g21)
         multiply2(2, 1, every, False, False)
+        da_scales.append(place(C, U8, "da_scales1", 23 * KB + KB // 2))
         multiply1(1)
-        gather("scalar", 2, 2, room_b)
-        g22 = times_gate(gate_bank[:], room_b, da_sb[1])
-        w2_sb[3] = place(PASSES * H, U16, "w2_3", 18 * KB)
+        w2_sb[3] = place(PASSES * H, U16, "w2_3", 24 * KB)
         permute_words(w2_sb[3], w2_raw[3])
-        quantise_g(2, 2, g22)
+        permute_scales(3, place(PASSES * H, U8, "w2_sc3", 27 * KB))
+        slopes_on_vector(2)
+        times_gate_shared(2, gate_bank, room_c, upper)
+        quantise_g(2, 2, upper)
         multiply2(2, 2, every, False, True)
-        permute_scales(3, place(PASSES * H, U8, "w2_sc3", 21 * KB))
 
-        gather("scalar", 3, 1, a_sb[1][:, rounded:], HALF, C)
+        gather("scalar", 3, 1, room_b)
         empty_dx(1)
-        slopes_on_scalar(2, 0, GROUPS)
-        gather("scalar", 3, 2, room_c[:, 0:rounded], 0, HALF)
-        gather("scalar", 3, 2, room_c[:, rounded:], HALF, C)
+        last = list(zip(LAST_CUTS, LAST_CUTS[1:]))
+        for lo, hi in last:
+            gather("scalar", 3, 2, room_g[:, PACK * lo : PACK * hi], lo, hi)
         slopes_on_scalar(3, 0, 2)
         slopes_on_scalar(3, 2, GROUPS)
-        g31b = times_gate_on_gpsimd(gate_sb[3][:, HALF:C], a_sb[1][:, rounded:], da_sb[1][:, 0:rounded])
-        times_slope(2, (0, 1))
-        multiply2(3, 0, (0, 1), True, False)
-        multiply2(3, 1, (0, 1), False, False)
-        g32a = times_gate(last_gate_bank[:, 0:HALF], room_c[:, 0:rounded], halves(room_a[:, 0:H]))
-        times_slope(2, (2, 3))
-        quantise_g(3, 1, g31b, HALF)
-        multiply2(3, 0, (2, 3), True, False)
-        multiply2(3, 1, (2, 3), False, False)
-        quantise_g(3, 2, g32a)
-        multiply2(3, 2, (0, 1), False, True)
-        g32b = times_gate(last_gate_bank[:, HALF:C], room_c[:, rounded:], halves(room_a[:, 3 * H :]))
+        times_gate_shared(3, last_gate_bank, room_b, upper)
+        da_sb.append(g00)
+        times_slope(2, every)
+        multiply2(3, 0, every, True, False)
+        quantise_g(3, 1, upper)
+        multiply2(3, 1, every, False, False)
         multiply1(2)
         empty_dx(2)
-        quantise_g(3, 2, g32b, HALF)
-        multiply2(3, 2, (2, 3), False, True)
-        times_slope(3, (0, 1, 2))
-        multiply1(3, 0, HALF)
-        empty_dx(3, 0, HALF)
-        times_slope(3, (3,))
-        multiply1(3, HALF, C)
-        empty_dx(3, HALF, C)
+        da_sb.append(g01)
+        for lo, hi in last:
+            piece = upper[:, PACK * lo : PACK * hi]
+            if lo == 0:
+                times_gate_shared(3, last_gate_bank, room_g[:, PACK * lo : PACK * hi], piece, lo, hi)
+            else:
+                times_gate(last_gate_bank[:, lo:hi], room_g[:, PACK * lo : PACK * hi], piece)
+            quantise_g(3, 2, piece, lo)
+            multiply2(3, 2, range(lo // P, hi // P), False, True)
+        for (lo, hi), bank in zip(last, (gate_bank, dx_bank, last_gate_bank)):
+            times_slope(3, range(lo // P, hi // P))
+            multiply1(3, lo, hi, bank)
+            if hi < C:
+                nc.scalar.copy(dx_sb[:, 3 * C + lo : 3 * C + hi], bank[:, lo:hi])
+            else:
+                nc.vector.tensor_copy(dx_sb[:, 3 * C + lo : 3 * C + hi], bank[:, lo:hi])
 
-        first, total = a_sb[2], a_sb[3]
+        first, total = a_sb[1], a_sb[3]
         for lo, hi in zip(OUT_CUTS, OUT_CUTS[1:]):
-            nc.scalar.activation(first[:, lo:hi], dx_sb.indirect(pos1_sb[:, lo // 16 : hi // 16]), COPY)
+            window = dx_sb.indirect(pos1_sb[:, lo // 16 : hi // 16])
+            if lo == 0:
+                nc.vector.tensor_copy(first[:, lo:hi], window)
+            else:
+                nc.scalar.activation(first[:, lo:hi], window, COPY)
             nc.vector.tensor_tensor(
                 total[:, lo:hi], dx_sb.indirect(pos2_sb[:, lo // 16 : hi // 16]), first[:, lo:hi], ADD
             )

@@ -16,6 +16,7 @@ W1_BYTES = 2 * K
 ALIGN = 64
 KB = 1024
 OUT_CUTS = (0, 192, 448, 704, 896, T)
+SHARE = 96
 LAST_CUTS = (0, 256, 384, C)
 
 FLOPS = 2 * SLOTS * (N * H + H * K)
@@ -72,29 +73,35 @@ def tile_moe_bdx_mlp_relu2_kernel(
         planes = [[own(T, F32, f"plane{s}_{d}") for d in range(PACK)] for s in range(PASSES)]
         gate_rows = own(P, F32, "gate_rows")
         gate_columns = own(SLOTS // P, F32, "gate_columns")
-        gate_sb = {0: own(P, F32, "gate0"), 1: own(P, F32, "gate1"), 2: own(C, F32, "gate2"), 3: own(C, F32, "gate3")}
+        gate_tail = [own(SHARE, F32, f"gate_tail{e}") for e in range(E - 1)]
+        gate_2a = own(HALF, F32, "gate_2a")
+        gate_2b = place(HALF, F32, "gate_2b", 27 * KB)
+        gate_3 = own(C, F32, "gate_3")
+        gate_1b = place(HALF, F32, "gate_1b", 10 * KB + KB // 2)
         w2_raw = [
             own(PASSES * H, U16, "w2_raw0"),
-            place(PASSES * H, U16, "w2_raw1", 16 * KB),
+            own(PASSES * H, U16, "w2_raw1"),
             own(PASSES * H, U16, "w2_raw2"),
             own(PASSES * H, U16, "w2_raw3"),
         ]
-        w2_lead = place(H, U16, "w2_lead", 30 * KB)
+        w2_lead = place(H, U16, "w2_lead", 32 * KB)
         sc_first = own(PASSES * H, U8, "sc_first")
         sc_rest = own((E - 1) * PASSES * H, U8, "sc_rest")
         sc_raw = [sc_first] + [sc_rest[:, r * PASSES * H : (r + 1) * PASSES * H] for r in range(E - 1)]
         w1_sb = own(E * W1_BYTES, U8, "w1_sb")
         w1_sc = own(E * K, U8, "w1_sc")
         ident = own(P, F32, "ident")
-        room_x = own(UNIT, F32, "room_x")
-        a_sb = [place(UNIT, F32, "a0", 22 * KB)] + [own(UNIT, F32, f"a{e}") for e in range(1, E)]
-        room_a, room_b, room_c = [own(UNIT, F32, f"room_{r}") for r in "abc"]
-        room_f = place(UNIT // 2, F32, "room_f", 9 * KB)
+        a0_room = own(UNIT + 3 * H, F32, "a0_room")
+        room_x = a0_room[:, 3 * H :]
+        a_sb = [a0_room[:, 0:UNIT]] + [own(UNIT, F32, f"a{e}") for e in range(1, E)]
+        room_a, room_b = [own(UNIT, F32, f"room_{r}") for r in "ab"]
+        room_c = place(UNIT, F32, "room_c", 16 * KB)
+        room_f = place(UNIT // 2, F32, "room_f", 40 * KB)
         room_d = place(UNIT, F32, "room_d", 0)
-        slopes = [room_a, room_x, room_x, room_c]
-        da_sb = [halves(room_x[:, 0 : UNIT // 2])]
+        slopes = [room_a, room_b, a_sb[1]]
+        da_sb = [halves(room_b[:, 0 : UNIT // 2])]
         da_words = [own(C, U32, f"da_words{r}") for r in range(2)]
-        da_scales = [own(C, U8, "da_scales0")]
+        da_scales = []
         dx_sb = own(SLOTS, F32, "dx_sb")
         g_words, g_scales, w2_sb, w2_sc = {}, {}, {}, {}
 
@@ -117,8 +124,8 @@ def tile_moe_bdx_mlp_relu2_kernel(
                 out=by_plane(a_sb[e]), in_=a[:, e * C : (e + 1) * C].rearrange("(p d) c -> p d c", d=PACK)
             )
 
-        def load_gate(e):
-            nc.sync.dma_start(out=gate_sb[e], in_=gate[0:P, (e + 1) * C - gate_sb[e].shape[1] : (e + 1) * C])
+        def load_gate(tile, end):
+            nc.sync.dma_start(out=tile, in_=gate[0:P, end - tile.shape[1] : end])
 
         def load_scales(tile, source, runs):
             src = source.bitcast(I32).rearrange("e s f w -> f (e s) w")
@@ -140,16 +147,19 @@ def tile_moe_bdx_mlp_relu2_kernel(
                         out=gate_rows, in_=gate[0 : P * P // SLOTS, :].rearrange("r (x c) -> (r x) c", c=P)
                     )
             if s == 0:
-                load_gate(3)
+                load_gate(gate_3, SLOTS)
             if s == 1:
-                load_gate(0)
+                load_gate(gate_tail[0], C)
         nc.sync.dma_start(out=w2_lead.bitcast(I32), in_=w2_words.bitcast(I32)[0, PASSES - 1])
         load_a(0)
-        load_gate(2)
-        load_gate(1)
+        load_gate(gate_2a, 2 * C + HALF)
+        load_gate(gate_1b, 2 * C)
+        load_gate(gate_tail[1], 2 * C)
         load_w2(1)
         load_scales(sc_rest, w2_scales[1:E], (E - 1) * PASSES)
         load_a(1)
+        load_gate(gate_2b, 3 * C)
+        load_gate(gate_tail[2], 3 * C)
         load_w2(2)
         load_scales(w1_sc, w1_scales, E)
         nc.sync.dma_start(
@@ -202,17 +212,15 @@ def tile_moe_bdx_mlp_relu2_kernel(
             )
             return dest
 
-        def times_gate_shared(e, bank, room, dest, lo=0, hi=C):
-            width = hi - lo
-            cut = width - width // 4
+        def times_gate_shared(gates, bank, room, dest):
+            share = gates.shape[1]
+            cut = C - share
             planes_of_room = by_plane(room)
-            runs = bank[:, lo : lo + cut].rearrange("p (c r) -> p c r", r=RUN)
+            runs = bank[:, 0:cut].rearrange("p (c r) -> p c r", r=RUN)
             nc.gpsimd.tensor_tensor(
                 dest[:, PACK * cut :].rearrange("p (c d) -> p c d", d=PACK),
                 planes_of_room[:, :, cut:].rearrange("p d c -> p c d"),
-                gate_sb[e][:, gate_sb[e].shape[1] - C + lo + cut : gate_sb[e].shape[1] - C + hi]
-                .unsqueeze(2)
-                .to_broadcast([P, width - cut, PACK]),
+                gates.unsqueeze(2).to_broadcast([P, share, PACK]),
                 MULT,
             )
             nc.vector.tensor_tensor(
@@ -312,12 +320,12 @@ def tile_moe_bdx_mlp_relu2_kernel(
 
         gather("scalar", 0, 0, room_a)
         gather("vector", 3, 0, room_d)
-        g30 = times_gate_on_gpsimd(gate_sb[3], room_d, own(UNIT, BF16, "g30"))
+        g30 = times_gate_on_gpsimd(gate_3, room_d, own(UNIT, BF16, "g30"))
         gather("scalar", 0, 1, room_b)
         gather("vector", 2, 0, room_f, 0, HALF)
         gather("scalar", 0, 2, room_c)
         g00 = times_gate(gate_bank[:], room_a, own(UNIT, BF16, "g00"))
-        g01 = times_gate_shared(0, gate_bank, room_b, own(UNIT, BF16, "g01"))
+        g01 = times_gate_shared(gate_tail[0], gate_bank, room_b, own(UNIT, BF16, "g01"))
         g_words[0, 0] = place(C, U32, "g_words0_0", 0)
         quantise_g(0, 0, g00)
         quantise_g(0, 1, g01)
@@ -327,85 +335,102 @@ def tile_moe_bdx_mlp_relu2_kernel(
         multiply2(0, 0, every, True, False)
         multiply2(0, 1, every, False, False)
         permute_words(w2_sb[0][:, 2 * H :], w2_lead)
-        g02 = times_gate_shared(0, gate_bank, room_c, halves(room_b[:, 0:rounded]))
+        g02 = times_gate(gate_bank[:], room_c, halves(room_a[:, 0:rounded]))
         quantise_g(3, 0, g30)
         quantise_g(0, 2, g02)
         multiply2(0, 2, every, False, True)
         spread_gate(1, gate_bank)
         slopes_on_vector(0)
 
-        room_g = place(UNIT, F32, "room_g", 30 * KB)
-        middle, upper = halves(room_a[:, H : 3 * H]), halves(room_a[:, 2 * H :])
+        room_g = place(UNIT, F32, "room_g", 32 * KB)
         gather("scalar", 1, 0, room_g)
-        g20a = times_gate_on_gpsimd(gate_sb[2][:, 0:HALF], room_f, halves(a_sb[0][:, rounded : rounded + H]))
+        g20a = times_gate_on_gpsimd(gate_2a, room_f, halves(a_sb[0][:, 2 * H : 3 * H]))
+        g10a, g10b = halves(a_sb[0][:, 3 * H :]), halves(room_f[:, 0:H])
+        nc.gpsimd.tensor_tensor(
+            g10b.rearrange("p (c d) -> p c d", d=PACK),
+            by_plane(room_g)[:, :, HALF:].rearrange("p d c -> p c d"),
+            gate_1b.unsqueeze(2).to_broadcast([P, HALF, PACK]),
+            MULT,
+        )
         gather("vector", 2, 0, a_sb[0][:, 0:rounded], HALF, C)
+        edge = ALIGN // 4
+        room_c = place(UNIT + 2 * edge, F32, "room_c_wide", 16 * KB - ALIGN)[:, edge : edge + UNIT]
         gather("scalar", 1, 1, room_c)
-        gather("scalar", 1, 2, room_b)
+        nc.vector.tensor_tensor(
+            woven(g10a),
+            by_plane(room_g)[:, :, 0:HALF].rearrange("p d (c r) -> p c d r", r=RUN),
+            gate_bank[:, 0:HALF].rearrange("p (c r) -> p c r", r=RUN).unsqueeze(2).to_broadcast([P, HALF // RUN, PACK, RUN]),
+            MULT,
+        )
+        gather("scalar", 1, 2, room_g)
         times_slope(0, every)
         quantise_g(2, 0, g20a)
-        w2_sb[1] = place(PASSES * H, U16, "w2_1", 8 * KB)
+        w2_sb[1] = place(PASSES * H, U16, "w2_1", 7 * KB + KB // 2 + ALIGN)
         permute_words(w2_sb[1], w2_raw[1])
-        permute_scales(1, place(PASSES * H, U8, "w2_sc1", 11 * KB))
-        w2_sb[2] = place(PASSES * H, U16, "w2_2", 13 * KB + KB // 2)
-        permute_words(w2_sb[2], w2_raw[2])
-        permute_scales(2, place(PASSES * H, U8, "w2_sc2", 17 * KB))
+        permute_scales(1, place(PASSES * H, U8, "w2_sc1", 11 * KB + ALIGN))
+        g_scales[1, 0] = place(C, U8, "g_scales1_0", 10 * KB + KB // 2 + ALIGN)
+        quantise_g(1, 0, g10a)
+        quantise_g(1, 0, g10b, HALF)
+        da_scales.append(place(C, U8, "da_scales0", 40 * KB))
         multiply1(0)
-        times_gate_shared(1, gate_bank, room_g, middle)
-        slopes_on_vector(1)
-        quantise_g(1, 0, middle)
+        ring = da_sb[0]
         multiply2(1, 0, every, True, False)
-        times_gate_shared(1, gate_bank, room_c, middle)
-        quantise_g(1, 1, middle)
+        times_gate_shared(gate_tail[1], gate_bank, room_c, ring)
+        w2_sb[2] = place(PASSES * H, U16, "w2_2", 13 * KB)
+        permute_words(w2_sb[2], w2_raw[2])
+        permute_scales(2, place(PASSES * H, U8, "w2_sc2", 24 * KB))
+        quantise_g(1, 1, ring)
         multiply2(1, 1, every, False, False)
-        times_gate_shared(1, gate_bank, room_b, middle)
+        times_gate_shared(gate_tail[1], gate_bank, room_g, ring)
         spread_gate(2, gate_bank)
-        quantise_g(1, 2, middle)
+        quantise_g(1, 2, ring)
         multiply2(1, 2, every, False, True)
+        slopes_on_vector(1)
 
-        gather("scalar", 2, 1, room_g)
+        gather("scalar", 2, 1, room_x)
         empty_dx(0)
+        room_c = place(UNIT, F32, "room_c_last", 16 * KB)
         gather("scalar", 2, 2, room_c)
-        times_gate_shared(2, gate_bank, room_g, upper)
-        g20b = times_gate_on_gpsimd(gate_sb[2][:, HALF:C], a_sb[0][:, 0:rounded], halves(room_a[:, H : 2 * H]))
+        g21 = times_gate_shared(gate_tail[2], gate_bank, room_x, halves(a_sb[1][:, 0:rounded]))
+        g20b = times_gate_on_gpsimd(gate_2b, a_sb[0][:, 0:rounded], halves(a_sb[1][:, rounded : rounded + H]))
         da_sb.append(g30)
         times_slope(1, every)
-        g_scales[2, 1] = place(C, U8, "g_scales2_1", 23 * KB)
-        quantise_g(2, 1, upper)
+        g_scales[2, 1] = place(C, U8, "g_scales2_1", 27 * KB + ALIGN)
+        quantise_g(2, 1, g21)
         quantise_g(2, 0, g20b, HALF)
         multiply2(2, 0, every, True, False)
         multiply2(2, 1, every, False, False)
-        da_scales.append(place(C, U8, "da_scales1", 23 * KB + KB // 2))
+        da_scales.append(own(C, U8, "da_scales1"))
         multiply1(1)
-        w2_sb[3] = place(PASSES * H, U16, "w2_3", 24 * KB)
+        w2_sb[3] = place(PASSES * H, U16, "w2_3", 28 * KB - ALIGN)
         permute_words(w2_sb[3], w2_raw[3])
-        permute_scales(3, place(PASSES * H, U8, "w2_sc3", 27 * KB))
+        permute_scales(3, place(PASSES * H, U8, "w2_sc3", 27 * KB + ALIGN - PASSES * H))
         slopes_on_vector(2)
-        times_gate_shared(2, gate_bank, room_c, upper)
-        quantise_g(2, 2, upper)
+        ring = halves(a_sb[2][:, 0:rounded])
+        times_gate_shared(gate_tail[2], gate_bank, room_c, ring)
+        quantise_g(2, 2, ring)
         multiply2(2, 2, every, False, True)
 
-        gather("scalar", 3, 1, room_b)
+        gather("scalar", 3, 1, room_g)
         empty_dx(1)
         last = list(zip(LAST_CUTS, LAST_CUTS[1:]))
         for lo, hi in last:
-            gather("scalar", 3, 2, room_g[:, PACK * lo : PACK * hi], lo, hi)
+            gather("scalar", 3, 2, room_x[:, PACK * lo : PACK * hi], lo, hi)
+        slopes.append(room_c)
         slopes_on_scalar(3, 0, 2)
         slopes_on_scalar(3, 2, GROUPS)
-        times_gate_shared(3, last_gate_bank, room_b, upper)
+        times_gate_shared(gate_3[:, HALF:], last_gate_bank, room_g, ring)
         da_sb.append(g00)
         times_slope(2, every)
         multiply2(3, 0, every, True, False)
-        quantise_g(3, 1, upper)
+        quantise_g(3, 1, ring)
         multiply2(3, 1, every, False, False)
         multiply1(2)
         empty_dx(2)
         da_sb.append(g01)
         for lo, hi in last:
-            piece = upper[:, PACK * lo : PACK * hi]
-            if lo == 0:
-                times_gate_shared(3, last_gate_bank, room_g[:, PACK * lo : PACK * hi], piece, lo, hi)
-            else:
-                times_gate(last_gate_bank[:, lo:hi], room_g[:, PACK * lo : PACK * hi], piece)
+            piece = halves(slopes[2][:, UNIT - 2 * hi : UNIT - 2 * lo])
+            times_gate(last_gate_bank[:, lo:hi], room_x[:, PACK * lo : PACK * hi], piece)
             quantise_g(3, 2, piece, lo)
             multiply2(3, 2, range(lo // P, hi // P), False, True)
         for (lo, hi), bank in zip(last, (gate_bank, dx_bank, last_gate_bank)):
@@ -416,7 +441,7 @@ def tile_moe_bdx_mlp_relu2_kernel(
             else:
                 nc.vector.tensor_copy(dx_sb[:, 3 * C + lo : 3 * C + hi], bank[:, lo:hi])
 
-        first, total = a_sb[1], a_sb[3]
+        first, total = room_a, a_sb[3]
         for lo, hi in zip(OUT_CUTS, OUT_CUTS[1:]):
             window = dx_sb.indirect(pos1_sb[:, lo // 16 : hi // 16])
             if lo == 0:

@@ -6,7 +6,7 @@ from concourse.masks import make_identity
 K, T, E, C, H, N = 128, 1024, 4, 512, 512, 1536
 P = 128
 PACK = 4
-RUN = 4
+RUN = 2
 SLOTS = E * C
 PASSES = N // 512
 GROUPS = C // P

@@ -17,6 +17,7 @@ ALIGN = 64
 KB = 1024
 OUT_CUTS = (0, 192, 448, 704, 896, T)
 SHARE = 96
+PAD = 8
 LAST_CUTS = (0, 256, 384, C)
 
 FLOPS = 2 * SLOTS * (N * H + H * K)
@@ -50,8 +51,7 @@ def tile_moe_bdx_mlp_relu2_kernel(
         psum = ctx.enter_context(tc.psum_pool(name="psum", bufs=1))
 
         banks = [psum.tile([P, 512], F32, name=f"bank{b}") for b in range(8)]
-        gate_bank = banks[0]
-        last_gate_bank = banks[1]
+        gate_banks = banks[0:2]
         dx_bank = banks[2]
         dh_banks = banks[3:8]
 
@@ -67,56 +67,60 @@ def tile_moe_bdx_mlp_relu2_kernel(
         def halves(ap):
             return ap.bitcast(BF16)
 
+        rounded = UNIT // 2
         offs_sb = keep.tile([P, SLOTS // 16], U16, name="offs_sb")
         pos1_sb = keep.tile([P, T // 16], U16, name="pos1_sb")
         pos2_sb = keep.tile([P, T // 16], U16, name="pos2_sb")
-        planes = [[own(T, F32, f"plane{s}_{d}") for d in range(PACK)] for s in range(PASSES)]
-        gate_rows = own(P, F32, "gate_rows")
-        gate_columns = own(SLOTS // P, F32, "gate_columns")
-        gate_tail = [own(SHARE, F32, f"gate_tail{e}") for e in range(E - 1)]
-        gate_2a = own(HALF, F32, "gate_2a")
-        gate_2b = place(HALF, F32, "gate_2b", 27 * KB)
-        gate_3 = own(C, F32, "gate_3")
-        gate_1b = place(HALF, F32, "gate_1b", 10 * KB + KB // 2)
-        w2_raw = [
-            own(PASSES * H, U16, "w2_raw0"),
-            own(PASSES * H, U16, "w2_raw1"),
-            own(PASSES * H, U16, "w2_raw2"),
-            own(PASSES * H, U16, "w2_raw3"),
+        planes = [
+            [own(T + PAD if s < PASSES - 1 else T, F32, f"plane{s}_{d}") for d in range(PACK)] for s in range(PASSES)
         ]
-        w2_lead = place(H, U16, "w2_lead", 32 * KB)
+        gate_rows = place(P, F32, "gate_rows", 0)
+        gate_columns = own(SLOTS // P, F32, "gate_columns")
+        gate_0_tail = own(SHARE, F32, "gate_0_tail")
+        gate_2_tail = own(SHARE, F32, "gate_2_tail")
+        gate_1b = place(HALF, F32, "gate_1b", 41 * KB)
+        gate_2a = own(C - P, F32, "gate_2a")
+        gate_2b = place(HALF, F32, "gate_2b", 47 * KB)
+        gate_3 = own(C, F32, "gate_3")
+        w2_raw = [own(PASSES * H, U16, f"w2_raw{e}") for e in range(E)]
         sc_first = own(PASSES * H, U8, "sc_first")
         sc_rest = own((E - 1) * PASSES * H, U8, "sc_rest")
         sc_raw = [sc_first] + [sc_rest[:, r * PASSES * H : (r + 1) * PASSES * H] for r in range(E - 1)]
         w1_sb = own(E * W1_BYTES, U8, "w1_sb")
         w1_sc = own(E * K, U8, "w1_sc")
         ident = own(P, F32, "ident")
-        a0_room = own(UNIT + 3 * H, F32, "a0_room")
-        room_x = a0_room[:, 3 * H :]
-        a_sb = [a0_room[:, 0:UNIT]] + [own(UNIT, F32, f"a{e}") for e in range(1, E)]
-        room_a, room_b = [own(UNIT, F32, f"room_{r}") for r in "ab"]
-        room_c = place(UNIT, F32, "room_c", 16 * KB)
-        room_f = place(UNIT // 2, F32, "room_f", 40 * KB)
-        room_d = place(UNIT, F32, "room_d", 0)
-        slopes = [room_a, room_b, a_sb[1]]
-        da_sb = [halves(room_b[:, 0 : UNIT // 2])]
+        a1_room = own(UNIT + rounded, F32, "a1_room")
+        room_x = a1_room[:, 0:UNIT]
+        a_sb = [own(UNIT, F32, "a0"), a1_room[:, rounded:], own(UNIT, F32, "a2"), own(UNIT, F32, "a3")]
+        wide_0 = own(2 * UNIT, F32, "wide_0")
+        edge = ALIGN // 4
+        wide_1 = place(2 * UNIT + 2 * edge, F32, "wide_1", 20 * KB - ALIGN)[:, edge : edge + 2 * UNIT]
+        room_a = wide_0[:, 0:UNIT]
+        room_30 = own(UNIT, F32, "room_30")
         da_words = [own(C, U32, f"da_words{r}") for r in range(2)]
-        da_scales = []
+        da_scales = [own(C, U8, f"da_scales{r}") for r in range(2)]
         dx_sb = own(SLOTS, F32, "dx_sb")
-        g_words, g_scales, w2_sb, w2_sc = {}, {}, {}, {}
+        g_words, g_scales, w2_sb, w2_sc, slopes, da_sb = {}, {}, {}, {}, {}, {}
 
         nc.gpsimd.memset(sc_first.bitcast(I32), 0)
         nc.vector.memset(sc_rest.bitcast(I32), 0)
         nc.vector.memset(w1_sc[:, 0 : 2 * K].bitcast(I32), 0)
         nc.scalar.copy(w1_sc[:, 2 * K : 4 * K].bitcast(U32), w1_sc[:, 0 : 2 * K].bitcast(U32))
+        for s in range(PASSES - 1):
+            for d in range(PACK):
+                nc.vector.memset(planes[s][d][:, T:], 0.0)
         make_identity(nc, ident)
 
         dy_rows = dyT.rearrange("(s p d) t -> s d p t", p=P, d=PACK)
 
-        def load_w2(e, passes=PASSES):
+        def load_planes(s):
+            for d in range(PACK):
+                nc.sync.dma_start(out=planes[s][d][:, 0:T], in_=dy_rows[s, d])
+
+        def load_w2(e):
             nc.sync.dma_start(
-                out=w2_raw[e].bitcast(I32).rearrange("p (s w) -> p s w", s=PASSES)[:, 0:passes],
-                in_=w2_words.bitcast(I32)[e].rearrange("s p w -> p s w")[:, 0:passes],
+                out=w2_raw[e].bitcast(I32).rearrange("p (s w) -> p s w", s=PASSES),
+                in_=w2_words.bitcast(I32)[e].rearrange("s p w -> p s w"),
             )
 
         def load_a(e):
@@ -136,30 +140,22 @@ def tile_moe_bdx_mlp_relu2_kernel(
                 )
 
         nc.sync.dma_start(offs_sb[:], offs)
-        for s in range(PASSES):
-            for d in range(PACK):
-                if (s, d) == (PASSES - 1, PACK - 1):
-                    load_w2(0, PASSES - 1)
-                    load_scales(sc_first, w2_scales[0:1], PASSES)
-                nc.sync.dma_start(out=planes[s][d], in_=dy_rows[s, d])
-                if (s, d) == (0, 0):
-                    nc.sync.dma_start(
-                        out=gate_rows, in_=gate[0 : P * P // SLOTS, :].rearrange("r (x c) -> (r x) c", c=P)
-                    )
-            if s == 0:
-                load_gate(gate_3, SLOTS)
-            if s == 1:
-                load_gate(gate_tail[0], C)
-        nc.sync.dma_start(out=w2_lead.bitcast(I32), in_=w2_words.bitcast(I32)[0, PASSES - 1])
+        load_planes(0)
+        nc.sync.dma_start(out=gate_rows, in_=gate[0 : P * P // SLOTS, :].rearrange("r (x c) -> (r x) c", c=P))
+        load_gate(gate_3, SLOTS)
+        load_planes(1)
+        load_gate(gate_2a, 3 * C - P)
+        load_w2(0)
+        load_scales(sc_first, w2_scales[0:1], PASSES)
         load_a(0)
-        load_gate(gate_2a, 2 * C + HALF)
         load_gate(gate_1b, 2 * C)
-        load_gate(gate_tail[1], 2 * C)
+        load_planes(2)
+        load_gate(gate_0_tail, C)
         load_w2(1)
         load_scales(sc_rest, w2_scales[1:E], (E - 1) * PASSES)
         load_a(1)
         load_gate(gate_2b, 3 * C)
-        load_gate(gate_tail[2], 3 * C)
+        load_gate(gate_2_tail, 3 * C)
         load_w2(2)
         load_scales(w1_sc, w1_scales, E)
         nc.sync.dma_start(
@@ -172,14 +168,15 @@ def tile_moe_bdx_mlp_relu2_kernel(
         nc.sync.dma_start(pos1_sb[:], pos1)
         nc.sync.dma_start(pos2_sb[:], pos2)
 
-        def gather(engine, e, s, room, lo=0, hi=C):
-            width = hi - lo
+        def gather(engine, s, slot0, room):
+            width = room.shape[1] // PACK
             for d in range(PACK):
-                window = planes[s][d].indirect(offs_sb[:, (e * C + lo) // 16 : (e * C + hi) // 16])
+                window = planes[s][d].indirect(offs_sb[:, slot0 // 16 : (slot0 + width) // 16])
                 if engine == "scalar":
                     nc.scalar.activation(room[:, d * width : (d + 1) * width], window, COPY)
                 else:
                     nc.vector.tensor_copy(room[:, d * width : (d + 1) * width], window)
+            return by_plane(room)
 
         def in_runs(ap):
             return ap.rearrange("p (d c r) -> p c d r", d=PACK, r=RUN)
@@ -187,73 +184,52 @@ def tile_moe_bdx_mlp_relu2_kernel(
         def woven(ap):
             return ap.rearrange("p (c r d) -> p c d r", r=RUN, d=PACK)
 
-        def spread_gate(e, bank):
-            for x in range(GROUPS):
-                column = e * GROUPS + x
-                nc.tensor.transpose(
-                    bank[:, x * P : (x + 1) * P], gate_columns[:, column : column + 1].to_broadcast([P, P]), ident
-                )
+        def spread_gate(group0, dest):
+            for x in range(dest.shape[1] // P):
+                column = gate_columns[:, group0 + x : group0 + x + 1]
+                nc.tensor.transpose(dest[:, x * P : (x + 1) * P], column.to_broadcast([P, P]), ident)
 
-        def times_gate(gates, room, dest):
+        def times_gate(gates, values, dest):
             width = gates.shape[1]
             runs = gates.rearrange("p (c r) -> p c r", r=RUN)
             nc.vector.tensor_tensor(
-                woven(dest), in_runs(room), runs.unsqueeze(2).to_broadcast([P, width // RUN, PACK, RUN]), MULT
+                woven(dest),
+                values.rearrange("p d (c r) -> p c d r", r=RUN),
+                runs.unsqueeze(2).to_broadcast([P, width // RUN, PACK, RUN]),
+                MULT,
             )
-            return dest
 
-        def times_gate_on_gpsimd(gates, room, dest):
-            width = gates.shape[1]
+        def times_gate_on_gpsimd(gates, values, dest):
             nc.gpsimd.tensor_tensor(
                 dest.rearrange("p (c d) -> p c d", d=PACK),
-                room.rearrange("p (d c) -> p c d", d=PACK),
-                gates.unsqueeze(2).to_broadcast([P, width, PACK]),
+                values.rearrange("p d c -> p c d"),
+                gates.unsqueeze(2).to_broadcast([P, gates.shape[1], PACK]),
                 MULT,
             )
-            return dest
 
-        def times_gate_shared(gates, bank, room, dest):
-            share = gates.shape[1]
-            cut = C - share
-            planes_of_room = by_plane(room)
-            runs = bank[:, 0:cut].rearrange("p (c r) -> p c r", r=RUN)
-            nc.gpsimd.tensor_tensor(
-                dest[:, PACK * cut :].rearrange("p (c d) -> p c d", d=PACK),
-                planes_of_room[:, :, cut:].rearrange("p d c -> p c d"),
-                gates.unsqueeze(2).to_broadcast([P, share, PACK]),
-                MULT,
-            )
-            nc.vector.tensor_tensor(
-                woven(dest[:, 0 : PACK * cut]),
-                planes_of_room[:, :, 0:cut].rearrange("p d (c r) -> p c d r", r=RUN),
-                runs.unsqueeze(2).to_broadcast([P, cut // RUN, PACK, RUN]),
-                MULT,
-            )
-            return dest
+        def times_gate_shared(bank, tail, values, dest):
+            cut = C - tail.shape[1]
+            times_gate_on_gpsimd(tail, values[:, :, cut:], dest[:, PACK * cut :])
+            times_gate(bank[:, 0:cut], values[:, :, 0:cut], dest[:, 0 : PACK * cut])
 
-        def quantise(source, words, scales, lo):
-            hi = lo + source.shape[1] // PACK
-            nc.vector.quantize_mx(out=words[:, lo:hi].bitcast(E5M2), scales=scales[:, lo:hi], in_=source)
+        def quantise(source, words, scales):
+            nc.vector.quantize_mx(out=words.bitcast(E5M2), scales=scales, in_=source)
 
         def quantise_g(e, s, source, lo=0):
-            if (e, s) not in g_scales:
-                g_scales[e, s] = own(C, U8, f"g_scales{e}_{s}")
-            if (e, s) not in g_words:
-                g_words[e, s] = own(C, U32, f"g_words{e}_{s}")
-            quantise(source, g_words[e, s], g_scales[e, s], lo)
+            hi = lo + source.shape[1] // PACK
+            quantise(source, g_words[e, s][:, lo:hi], g_scales[e, s][:, lo:hi])
 
-        def permute_words(dest, source):
-            nc.vector.tensor_copy(
-                dest.rearrange("p (s t m) -> p t s m", m=P, t=PACK),
-                source.rearrange("p (s m t) -> p t s m", m=P, t=PACK),
-            )
+        def codes(e, s, words, scales):
+            g_words[e, s], g_scales[e, s] = words, scales
 
-        def permute_scales(e, dest):
-            w2_sc[e] = dest
-            nc.vector.tensor_copy(
-                dest.rearrange("p (s t m) -> p t s m", s=PASSES, t=PACK),
-                sc_raw[e].rearrange("p (s m t) -> p t s m", s=PASSES, t=PACK),
-            )
+        def permute_weights(e, words_at, scales_at):
+            w2_sb[e] = place(PASSES * H, U16, f"w2_{e}", words_at)
+            w2_sc[e] = place(PASSES * H, U8, f"w2_sc{e}", scales_at)
+            for dest, source in ((w2_sb[e], w2_raw[e]), (w2_sc[e], sc_raw[e])):
+                nc.vector.tensor_copy(
+                    dest.rearrange("p (s t m) -> p t s m", s=PASSES, t=PACK),
+                    source.rearrange("p (s m t) -> p t s m", s=PASSES, t=PACK),
+                )
 
         def by_group(e):
             return (
@@ -296,7 +272,7 @@ def tile_moe_bdx_mlp_relu2_kernel(
                 )
 
         def multiply1(e, lo=0, hi=C, bank=dx_bank):
-            quantise(da_sb[e][:, PACK * lo : PACK * hi], da_words[e % 2], da_scales[e % 2], lo)
+            quantise(da_sb[e][:, PACK * lo : PACK * hi], da_words[e % 2][:, lo:hi], da_scales[e % 2][:, lo:hi])
             nc.tensor.matmul_mx(
                 out=bank[:, lo:hi],
                 lhsT=w1_sb[:, e * W1_BYTES : (e + 1) * W1_BYTES].bitcast(E2M1),
@@ -311,129 +287,116 @@ def tile_moe_bdx_mlp_relu2_kernel(
             nc.scalar.copy(dx_sb[:, e * C + lo : e * C + hi], dx_bank[:, lo:hi])
 
         every = range(GROUPS)
-        rounded = UNIT // 2
 
         nc.tensor.transpose(dx_bank[:, 0:P], gate_rows, ident)
         nc.vector.tensor_copy(gate_columns, dx_bank[:, 0 : SLOTS // P])
-        spread_gate(0, gate_bank)
-        spread_gate(3, last_gate_bank)
+        spread_gate(0, gate_banks[0][:])
+        spread_gate(GROUPS, gate_banks[1][:])
+        spread_gate(3 * GROUPS - 1, dx_bank[:, P : 2 * P])
 
-        gather("scalar", 0, 0, room_a)
-        gather("vector", 3, 0, room_d)
-        g30 = times_gate_on_gpsimd(gate_3, room_d, own(UNIT, BF16, "g30"))
-        gather("scalar", 0, 1, room_b)
-        gather("vector", 2, 0, room_f, 0, HALF)
-        gather("scalar", 0, 2, room_c)
-        g00 = times_gate(gate_bank[:], room_a, own(UNIT, BF16, "g00"))
-        g01 = times_gate_shared(gate_tail[0], gate_bank, room_b, own(UNIT, BF16, "g01"))
-        g_words[0, 0] = place(C, U32, "g_words0_0", 0)
-        quantise_g(0, 0, g00)
-        quantise_g(0, 1, g01)
-        w2_sb[0] = own(PASSES * H, U16, "w2_0")
-        permute_words(w2_sb[0][:, 0 : 2 * H], w2_raw[0][:, 0 : 2 * H])
-        permute_scales(0, own(PASSES * H, U8, "w2_sc0"))
+        pair_0 = gather("scalar", 0, 0, wide_0)
+        v30 = gather("vector", 0, 3 * C, room_30)
+        g30 = own(UNIT, BF16, "g30")
+        times_gate_on_gpsimd(gate_3, v30, g30)
+        v20 = gather("vector", 0, 2 * C, place(UNIT, F32, "room_20", 0))
+        g20 = own(UNIT, BF16, "g20")
+        times_gate_on_gpsimd(gate_2a, v20[:, :, 0 : C - P], g20[:, 0 : PACK * (C - P)])
+        pair_1 = gather("scalar", 1, 0, wide_1)
+        g_pair = own(2 * UNIT, BF16, "g_pair")
+        for e in range(2):
+            times_gate(gate_banks[e][:], pair_0[:, :, e * C : (e + 1) * C], g_pair[:, e * UNIT : (e + 1) * UNIT])
+        times_gate(dx_bank[:, P : 2 * P], v20[:, :, C - P :], g20[:, PACK * (C - P) :])
+
+        words_0, scales_0 = own(2 * C, U32, "words_0"), place(2 * C, U8, "scales_0", 0)
+        quantise(g_pair, words_0, scales_0)
+        codes(0, 0, words_0[:, 0:C], scales_0[:, 0:C])
+        codes(1, 0, words_0[:, C:], scales_0[:, C:])
+        permute_weights(0, KB + KB // 2, 4 * KB + KB // 2)
         multiply2(0, 0, every, True, False)
-        multiply2(0, 1, every, False, False)
-        permute_words(w2_sb[0][:, 2 * H :], w2_lead)
-        g02 = times_gate(gate_bank[:], room_c, halves(room_a[:, 0:rounded]))
+        codes(3, 0, own(C, U32, "words_30"), place(C, U8, "scales_30", KB))
         quantise_g(3, 0, g30)
-        quantise_g(0, 2, g02)
-        multiply2(0, 2, every, False, True)
-        spread_gate(1, gate_bank)
+        codes(2, 0, own(C, U32, "words_20"), own(C, U8, "scales_20"))
+        quantise_g(2, 0, g20)
+        slopes[0] = place(UNIT, F32, "slopes0", 7 * KB + KB // 2)
         slopes_on_vector(0)
 
-        room_g = place(UNIT, F32, "room_g", 32 * KB)
-        gather("scalar", 1, 0, room_g)
-        g20a = times_gate_on_gpsimd(gate_2a, room_f, halves(a_sb[0][:, 2 * H : 3 * H]))
-        g10a, g10b = halves(a_sb[0][:, 3 * H :]), halves(room_f[:, 0:H])
-        nc.gpsimd.tensor_tensor(
-            g10b.rearrange("p (c d) -> p c d", d=PACK),
-            by_plane(room_g)[:, :, HALF:].rearrange("p d c -> p c d"),
-            gate_1b.unsqueeze(2).to_broadcast([P, HALF, PACK]),
-            MULT,
-        )
-        gather("vector", 2, 0, a_sb[0][:, 0:rounded], HALF, C)
-        edge = ALIGN // 4
-        room_c = place(UNIT + 2 * edge, F32, "room_c_wide", 16 * KB - ALIGN)[:, edge : edge + UNIT]
-        gather("scalar", 1, 1, room_c)
-        nc.vector.tensor_tensor(
-            woven(g10a),
-            by_plane(room_g)[:, :, 0:HALF].rearrange("p d (c r) -> p c d r", r=RUN),
-            gate_bank[:, 0:HALF].rearrange("p (c r) -> p c r", r=RUN).unsqueeze(2).to_broadcast([P, HALF // RUN, PACK, RUN]),
-            MULT,
-        )
-        gather("scalar", 1, 2, room_g)
-        times_slope(0, every)
-        quantise_g(2, 0, g20a)
-        w2_sb[1] = place(PASSES * H, U16, "w2_1", 7 * KB + KB // 2 + ALIGN)
-        permute_words(w2_sb[1], w2_raw[1])
-        permute_scales(1, place(PASSES * H, U8, "w2_sc1", 11 * KB + ALIGN))
-        g_scales[1, 0] = place(C, U8, "g_scales1_0", 10 * KB + KB // 2 + ALIGN)
-        quantise_g(1, 0, g10a)
-        quantise_g(1, 0, g10b, HALF)
-        da_scales.append(place(C, U8, "da_scales0", 40 * KB))
-        multiply1(0)
-        ring = da_sb[0]
-        multiply2(1, 0, every, True, False)
-        times_gate_shared(gate_tail[1], gate_bank, room_c, ring)
-        w2_sb[2] = place(PASSES * H, U16, "w2_2", 13 * KB)
-        permute_words(w2_sb[2], w2_raw[2])
-        permute_scales(2, place(PASSES * H, U8, "w2_sc2", 24 * KB))
-        quantise_g(1, 1, ring)
-        multiply2(1, 1, every, False, False)
-        times_gate_shared(gate_tail[1], gate_bank, room_g, ring)
-        spread_gate(2, gate_bank)
-        quantise_g(1, 2, ring)
-        multiply2(1, 2, every, False, True)
+        g_pair_1 = halves(a_sb[0])
+        times_gate(gate_banks[0][:], pair_1[:, :, 0:C], g_pair_1[:, 0:UNIT])
+        times_gate_shared(gate_banks[1], gate_1b, pair_1[:, :, C:], g_pair_1[:, UNIT:])
+        v02 = gather("scalar", 2, 0, room_a)
+        permute_weights(1, 17 * KB, 36 * KB)
+        words_1, scales_1 = own(2 * C, U32, "words_1"), own(2 * C, U8, "scales_1")
+        quantise(g_pair_1, words_1, scales_1)
+        codes(0, 1, words_1[:, 0:C], scales_1[:, 0:C])
+        codes(1, 1, words_1[:, C:], scales_1[:, C:])
+        multiply2(0, 1, every, False, False)
+
+        room_w = place(UNIT, F32, "room_w", 20 * KB)
+        da_pair = place(2 * UNIT, BF16, "da_pair", 28 * KB)
+        da_sb[0], da_sb[1] = da_pair[:, 0:UNIT], da_pair[:, UNIT:]
+        v12 = gather("scalar", 2, C, room_w)
+        times_gate_shared(gate_banks[0], gate_0_tail, v02, g_pair_1[:, 0:UNIT])
+        spread_gate(2 * GROUPS, gate_banks[0][:])
+        codes(0, 2, own(C, U32, "words_02"), own(C, U8, "scales_02"))
+        quantise_g(0, 2, g_pair_1[:, 0:UNIT])
+        multiply2(0, 2, every, False, True)
+        slopes[1] = a_sb[0]
         slopes_on_vector(1)
 
-        gather("scalar", 2, 1, room_x)
+        v21 = gather("scalar", 1, 2 * C, room_a)
+        v22 = gather("scalar", 2, 2 * C, room_x)
+        g12 = halves(a1_room[:, UNIT:])
+        times_gate_shared(gate_banks[1], gate_1b, v12, g12)
+        spread_gate(3 * GROUPS, gate_banks[1][:])
+        times_slope(0, every)
+        multiply2(1, 0, every, True, False)
+        multiply2(1, 1, every, False, False)
+        codes(1, 2, own(C, U32, "words_12"), own(C, U8, "scales_12"))
+        quantise_g(1, 2, g12)
+        multiply2(1, 2, every, False, True)
+        permute_weights(2, 38 * KB + ALIGN, 42 * KB - ALIGN)
+        multiply1(0)
         empty_dx(0)
-        room_c = place(UNIT, F32, "room_c_last", 16 * KB)
-        gather("scalar", 2, 2, room_c)
-        g21 = times_gate_shared(gate_tail[2], gate_bank, room_x, halves(a_sb[1][:, 0:rounded]))
-        g20b = times_gate_on_gpsimd(gate_2b, a_sb[0][:, 0:rounded], halves(a_sb[1][:, rounded : rounded + H]))
-        da_sb.append(g30)
+
+        v31 = gather("scalar", 1, 3 * C, room_w)
+        times_gate_shared(gate_banks[0], gate_2b, v21, da_sb[0])
         times_slope(1, every)
-        g_scales[2, 1] = place(C, U8, "g_scales2_1", 27 * KB + ALIGN)
-        quantise_g(2, 1, g21)
-        quantise_g(2, 0, g20b, HALF)
         multiply2(2, 0, every, True, False)
+        codes(2, 1, words_0[:, 0:C], scales_0[:, 0:C])
+        quantise_g(2, 1, da_sb[0])
         multiply2(2, 1, every, False, False)
-        da_scales.append(own(C, U8, "da_scales1"))
+        permute_weights(3, 44 * KB + ALIGN, 48 * KB - ALIGN)
         multiply1(1)
-        w2_sb[3] = place(PASSES * H, U16, "w2_3", 28 * KB - ALIGN)
-        permute_words(w2_sb[3], w2_raw[3])
-        permute_scales(3, place(PASSES * H, U8, "w2_sc3", 27 * KB + ALIGN - PASSES * H))
-        slopes_on_vector(2)
-        ring = halves(a_sb[2][:, 0:rounded])
-        times_gate_shared(gate_tail[2], gate_bank, room_c, ring)
-        quantise_g(2, 2, ring)
+        empty_dx(1)
+        slopes[2] = a_sb[0]
+        slopes_on_scalar(2, 0, GROUPS)
+
+        times_gate_shared(gate_banks[0], gate_2_tail, v22, da_sb[1])
+        codes(2, 2, words_0[:, C:], scales_0[:, C:])
+        quantise_g(2, 2, da_sb[1])
         multiply2(2, 2, every, False, True)
 
-        gather("scalar", 3, 1, room_g)
-        empty_dx(1)
         last = list(zip(LAST_CUTS, LAST_CUTS[1:]))
-        for lo, hi in last:
-            gather("scalar", 3, 2, room_x[:, PACK * lo : PACK * hi], lo, hi)
-        slopes.append(room_c)
+        v32 = [gather("scalar", 2, 3 * C + lo, room_x[:, PACK * lo : PACK * hi]) for lo, hi in last]
+        times_gate_shared(gate_banks[1], gate_3[:, HALF:], v31, da_sb[1])
+        slopes[3] = room_w
         slopes_on_scalar(3, 0, 2)
         slopes_on_scalar(3, 2, GROUPS)
-        times_gate_shared(gate_3[:, HALF:], last_gate_bank, room_g, ring)
-        da_sb.append(g00)
+        da_sb[2], da_sb[3] = g_pair[:, 0:UNIT], g_pair[:, UNIT:]
         times_slope(2, every)
         multiply2(3, 0, every, True, False)
-        quantise_g(3, 1, ring)
+        codes(3, 1, words_1[:, 0:C], scales_1[:, 0:C])
+        quantise_g(3, 1, da_sb[1])
         multiply2(3, 1, every, False, False)
         multiply1(2)
         empty_dx(2)
-        da_sb.append(g01)
-        for lo, hi in last:
+        codes(3, 2, words_1[:, C:], scales_1[:, C:])
+        for (lo, hi), values in zip(last, v32):
             piece = halves(slopes[2][:, UNIT - 2 * hi : UNIT - 2 * lo])
-            times_gate(last_gate_bank[:, lo:hi], room_x[:, PACK * lo : PACK * hi], piece)
+            times_gate(gate_banks[1][:, lo:hi], values, piece)
             quantise_g(3, 2, piece, lo)
             multiply2(3, 2, range(lo // P, hi // P), False, True)
-        for (lo, hi), bank in zip(last, (gate_bank, dx_bank, last_gate_bank)):
+        for (lo, hi), bank in zip(last, (gate_banks[0], dx_bank, gate_banks[1])):
             times_slope(3, range(lo // P, hi // P))
             multiply1(3, lo, hi, bank)
             if hi < C:
@@ -441,7 +404,7 @@ def tile_moe_bdx_mlp_relu2_kernel(
             else:
                 nc.vector.tensor_copy(dx_sb[:, 3 * C + lo : 3 * C + hi], bank[:, lo:hi])
 
-        first, total = room_a, a_sb[3]
+        first, total = wide_0[:, UNIT:], a_sb[3]
         for lo, hi in zip(OUT_CUTS, OUT_CUTS[1:]):
             window = dx_sb.indirect(pos1_sb[:, lo // 16 : hi // 16])
             if lo == 0:

@@ -18,7 +18,7 @@ KB = 1024
 OUT_CUTS = (0, 192, 448, 704, 896, T)
 SHARE = 96
 PAD = 8
-LAST_CUTS = (0, 256, 384, C)
+LAST_CUTS = (0, HALF, C)
 
 FLOPS = 2 * SLOTS * (N * H + H * K)
 BYTES = (
@@ -52,8 +52,9 @@ def tile_moe_bdx_mlp_relu2_kernel(
 
         banks = [psum.tile([P, 512], F32, name=f"bank{b}") for b in range(8)]
         gate_banks = banks[0:2]
-        dx_bank = banks[2]
-        dh_banks = banks[3:8]
+        dx_bank = banks[6]
+        dh_banks = [banks[b] for b in (2, 3, 4, 5, 6, 7, 2, 3, 5, 0, 6, 7, 2, 4, 3, 5)]
+        dx_banks = [banks[4], banks[3], banks[0]]
 
         def own(width, dtype, name):
             return keep.tile([P, width], dtype, name=name, align_bytes=ALIGN)[:]
@@ -74,27 +75,24 @@ def tile_moe_bdx_mlp_relu2_kernel(
         planes = [
             [own(T + PAD if s < PASSES - 1 else T, F32, f"plane{s}_{d}") for d in range(PACK)] for s in range(PASSES)
         ]
-        gate_rows = place(P, F32, "gate_rows", 0)
+        gate_rows = place(P, F32, "gate_rows", 3 * KB + KB // 2)
         gate_columns = own(SLOTS // P, F32, "gate_columns")
-        gate_0_tail = own(SHARE, F32, "gate_0_tail")
-        gate_2_tail = own(SHARE, F32, "gate_2_tail")
-        gate_1b = place(HALF, F32, "gate_1b", 41 * KB)
-        gate_2a = own(C - P, F32, "gate_2a")
-        gate_2b = place(HALF, F32, "gate_2b", 47 * KB)
+        gate_0_tail = place(SHARE, F32, "gate_0_tail", 19 * KB)
+        gate_2_tail = place(SHARE, F32, "gate_2_tail", 46 * KB)
+        gate_1b = own(HALF, F32, "gate_1b")
+        gate_2a = own(HALF, F32, "gate_2a")
+        gate_2b = own(HALF, F32, "gate_2b")
         gate_3 = own(C, F32, "gate_3")
-        w2_raw = [own(PASSES * H, U16, f"w2_raw{e}") for e in range(E)]
-        sc_first = own(PASSES * H, U8, "sc_first")
+        w2_raw = [own(PASSES * H, U16, f"w2_raw{e}") for e in range(3)]
+        w2_raw = w2_raw + [place(PASSES * H, U16, "w2_raw3", 47 * KB)]
+        sc_raw = own(PASSES * H, U8, "sc_raw")
         sc_rest = own((E - 1) * PASSES * H, U8, "sc_rest")
-        sc_raw = [sc_first] + [sc_rest[:, r * PASSES * H : (r + 1) * PASSES * H] for r in range(E - 1)]
         w1_sb = own(E * W1_BYTES, U8, "w1_sb")
         w1_sc = own(E * K, U8, "w1_sc")
         ident = own(P, F32, "ident")
-        a1_room = own(UNIT + rounded, F32, "a1_room")
-        room_x = a1_room[:, 0:UNIT]
-        a_sb = [own(UNIT, F32, "a0"), a1_room[:, rounded:], own(UNIT, F32, "a2"), own(UNIT, F32, "a3")]
+        a_sb = [own(UNIT, F32, "a0"), place(UNIT, F32, "a1", 30 * KB), None, own(UNIT, F32, "a3")]
         wide_0 = own(2 * UNIT, F32, "wide_0")
-        edge = ALIGN // 4
-        wide_1 = place(2 * UNIT + 2 * edge, F32, "wide_1", 20 * KB - ALIGN)[:, edge : edge + 2 * UNIT]
+        wide_1 = place(2 * UNIT, F32, "wide_1", 56 * KB)
         room_a = wide_0[:, 0:UNIT]
         room_30 = own(UNIT, F32, "room_30")
         da_words = [own(C, U32, f"da_words{r}") for r in range(2)]
@@ -102,7 +100,7 @@ def tile_moe_bdx_mlp_relu2_kernel(
         dx_sb = own(SLOTS, F32, "dx_sb")
         g_words, g_scales, w2_sb, w2_sc, slopes, da_sb = {}, {}, {}, {}, {}, {}
 
-        nc.gpsimd.memset(sc_first.bitcast(I32), 0)
+        nc.gpsimd.memset(sc_raw.bitcast(I32), 0)
         nc.vector.memset(sc_rest.bitcast(I32), 0)
         nc.vector.memset(w1_sc[:, 0 : 2 * K].bitcast(I32), 0)
         nc.scalar.copy(w1_sc[:, 2 * K : 4 * K].bitcast(U32), w1_sc[:, 0 : 2 * K].bitcast(U32))
@@ -144,15 +142,19 @@ def tile_moe_bdx_mlp_relu2_kernel(
         nc.sync.dma_start(out=gate_rows, in_=gate[0 : P * P // SLOTS, :].rearrange("r (x c) -> (r x) c", c=P))
         load_gate(gate_3, SLOTS)
         load_planes(1)
-        load_gate(gate_2a, 3 * C - P)
+        load_gate(gate_2a, 2 * C + HALF)
         load_w2(0)
-        load_scales(sc_first, w2_scales[0:1], PASSES)
+        for q in range(4):
+            for s in range(PASSES):
+                nc.sync.dma_start(
+                    out=sc_raw[32 * q : 32 * q + 4 * E, s * H : (s + 1) * H].bitcast(I32),
+                    in_=w2_scales.bitcast(I32)[:, s, 4 * q : 4 * q + 4, :],
+                )
         load_a(0)
         load_gate(gate_1b, 2 * C)
         load_planes(2)
         load_gate(gate_0_tail, C)
         load_w2(1)
-        load_scales(sc_rest, w2_scales[1:E], (E - 1) * PASSES)
         load_a(1)
         load_gate(gate_2b, 3 * C)
         load_gate(gate_2_tail, 3 * C)
@@ -162,7 +164,6 @@ def tile_moe_bdx_mlp_relu2_kernel(
             out=w1_sb.bitcast(I32).rearrange("p (e w) -> p e w", e=E),
             in_=w1_words.bitcast(I32).rearrange("e s p w -> p (e s) w"),
         )
-        load_a(2)
         load_w2(3)
         load_a(3)
         nc.sync.dma_start(pos1_sb[:], pos1)
@@ -222,14 +223,26 @@ def tile_moe_bdx_mlp_relu2_kernel(
         def codes(e, s, words, scales):
             g_words[e, s], g_scales[e, s] = words, scales
 
-        def permute_weights(e, words_at, scales_at):
-            w2_sb[e] = place(PASSES * H, U16, f"w2_{e}", words_at)
-            w2_sc[e] = place(PASSES * H, U8, f"w2_sc{e}", scales_at)
-            for dest, source in ((w2_sb[e], w2_raw[e]), (w2_sc[e], sc_raw[e])):
-                nc.vector.tensor_copy(
-                    dest.rearrange("p (s t m) -> p t s m", s=PASSES, t=PACK),
-                    source.rearrange("p (s m t) -> p t s m", s=PASSES, t=PACK),
-                )
+        def permute(dest, source):
+            nc.vector.tensor_copy(
+                dest.rearrange("p (s t m) -> p t s m", s=PASSES, t=PACK),
+                source.rearrange("p (s m t) -> p t s m", s=PASSES, t=PACK),
+            )
+
+        def permute_words(e, at):
+            w2_sb[e] = place(PASSES * H, U16, f"w2_{e}", at)
+            permute(w2_sb[e], w2_raw[e])
+
+        def permute_scales(at):
+            w2_sc[0] = place(PASSES * H, U8, "w2_sc", at)
+            permute(w2_sc[0], sc_raw)
+            for e in range(1, E):
+                w2_sc[e] = sc_rest[:, (e - 1) * PASSES * H : e * PASSES * H]
+                for q in range(4):
+                    nc.sync.dma_start(
+                        out=w2_sc[e][32 * q : 32 * q + 4, :].bitcast(I32),
+                        in_=w2_sc[0][32 * q + 4 * e : 32 * q + 4 * e + 4, :].bitcast(I32),
+                    )
 
         def by_group(e):
             return (
@@ -246,7 +259,7 @@ def tile_moe_bdx_mlp_relu2_kernel(
             nc.scalar.activation(dest[:, lo:hi], source[:, lo:hi], RELU, scale=2.0)
 
         def dh_bank(e, x):
-            return dh_banks[(e * GROUPS + x) % len(dh_banks)]
+            return dh_banks[e * GROUPS + x]
 
         def multiply2(e, s, groups, opens, closes):
             for x in groups:
@@ -271,20 +284,25 @@ def tile_moe_bdx_mlp_relu2_kernel(
                     MULT,
                 )
 
-        def multiply1(e, lo=0, hi=C, bank=dx_bank):
-            quantise(da_sb[e][:, PACK * lo : PACK * hi], da_words[e % 2][:, lo:hi], da_scales[e % 2][:, lo:hi])
+        def multiply1(e, bank, lo=0, hi=C):
+            quantise(da_sb[e][:, PACK * lo : PACK * hi], da_words[e][:, lo:hi], da_scales[e % 2][:, lo:hi])
             nc.tensor.matmul_mx(
                 out=bank[:, lo:hi],
                 lhsT=w1_sb[:, e * W1_BYTES : (e + 1) * W1_BYTES].bitcast(E2M1),
                 lhsT_scale=w1_sc[:, e * K : (e + 1) * K],
-                rhs=da_words[e % 2][:, lo:hi].bitcast(E5M2),
+                rhs=da_words[e][:, lo:hi].bitcast(E5M2),
                 rhs_scale=da_scales[e % 2][:, lo:hi],
                 start=True,
                 stop=True,
             )
 
-        def empty_dx(e, lo=0, hi=C):
-            nc.scalar.copy(dx_sb[:, e * C + lo : e * C + hi], dx_bank[:, lo:hi])
+        def empty_dx(e):
+            nc.scalar.copy(dx_sb[:, e * C : (e + 1) * C], dx_banks[e][:])
+
+        def last_pass(e, source):
+            for lo in (0, HALF):
+                quantise_g(e, PASSES - 1, source[:, PACK * lo : PACK * (lo + HALF)], lo)
+                multiply2(e, PASSES - 1, range(lo // P, (lo + HALF) // P), False, True)
 
         every = range(GROUPS)
 
@@ -292,113 +310,122 @@ def tile_moe_bdx_mlp_relu2_kernel(
         nc.vector.tensor_copy(gate_columns, dx_bank[:, 0 : SLOTS // P])
         spread_gate(0, gate_banks[0][:])
         spread_gate(GROUPS, gate_banks[1][:])
-        spread_gate(3 * GROUPS - 1, dx_bank[:, P : 2 * P])
+        spread_gate(3 * GROUPS - 2, dx_bank[:, HALF:])
 
         pair_0 = gather("scalar", 0, 0, wide_0)
         v30 = gather("vector", 0, 3 * C, room_30)
         g30 = own(UNIT, BF16, "g30")
         times_gate_on_gpsimd(gate_3, v30, g30)
-        v20 = gather("vector", 0, 2 * C, place(UNIT, F32, "room_20", 0))
+        v20 = gather("vector", 0, 2 * C, place(UNIT, F32, "room_20", 3 * KB))
         g20 = own(UNIT, BF16, "g20")
-        times_gate_on_gpsimd(gate_2a, v20[:, :, 0 : C - P], g20[:, 0 : PACK * (C - P)])
+        times_gate_on_gpsimd(gate_2a, v20[:, :, 0:HALF], g20[:, 0:rounded])
         pair_1 = gather("scalar", 1, 0, wide_1)
         g_pair = own(2 * UNIT, BF16, "g_pair")
         for e in range(2):
             times_gate(gate_banks[e][:], pair_0[:, :, e * C : (e + 1) * C], g_pair[:, e * UNIT : (e + 1) * UNIT])
-        times_gate(dx_bank[:, P : 2 * P], v20[:, :, C - P :], g20[:, PACK * (C - P) :])
+        times_gate(dx_bank[:, HALF:], v20[:, :, HALF:], g20[:, rounded:])
 
-        words_0, scales_0 = own(2 * C, U32, "words_0"), place(2 * C, U8, "scales_0", 0)
+        words_0, scales_0 = own(2 * C, U32, "words_0"), place(2 * C, U8, "scales_0", 4 * KB)
         quantise(g_pair, words_0, scales_0)
         codes(0, 0, words_0[:, 0:C], scales_0[:, 0:C])
         codes(1, 0, words_0[:, C:], scales_0[:, C:])
-        permute_weights(0, KB + KB // 2, 4 * KB + KB // 2)
+        permute_scales(8 * KB + KB // 2)
+        permute_words(0, 5 * KB + KB // 2)
         multiply2(0, 0, every, True, False)
-        codes(3, 0, own(C, U32, "words_30"), place(C, U8, "scales_30", KB))
+        codes(3, 0, own(C, U32, "words_30"), place(C, U8, "scales_30", 5 * KB))
         quantise_g(3, 0, g30)
-        codes(2, 0, own(C, U32, "words_20"), own(C, U8, "scales_20"))
-        quantise_g(2, 0, g20)
-        slopes[0] = place(UNIT, F32, "slopes0", 7 * KB + KB // 2)
+        permute_words(1, ALIGN)
+        multiply2(1, 0, (0, 1), True, False)
+        slopes[0] = place(UNIT, F32, "slopes0", 10 * KB + KB // 2)
         slopes_on_vector(0)
+        codes(2, 0, own(C, U32, "words_20"), place(C, U8, "scales_20", 10 * KB))
+        quantise_g(2, 0, g20)
 
-        g_pair_1 = halves(a_sb[0])
-        times_gate(gate_banks[0][:], pair_1[:, :, 0:C], g_pair_1[:, 0:UNIT])
-        times_gate_shared(gate_banks[1], gate_1b, pair_1[:, :, C:], g_pair_1[:, UNIT:])
+        ring, g11 = halves(a_sb[0][:, 0:rounded]), halves(a_sb[0][:, rounded:])
+        times_gate(gate_banks[0][:], pair_1[:, :, 0:C], ring)
+        times_gate_shared(gate_banks[1], gate_1b, pair_1[:, :, C:], g11)
         v02 = gather("scalar", 2, 0, room_a)
-        permute_weights(1, 17 * KB, 36 * KB)
         words_1, scales_1 = own(2 * C, U32, "words_1"), own(2 * C, U8, "scales_1")
-        quantise(g_pair_1, words_1, scales_1)
         codes(0, 1, words_1[:, 0:C], scales_1[:, 0:C])
         codes(1, 1, words_1[:, C:], scales_1[:, C:])
+        quantise_g(0, 1, ring)
         multiply2(0, 1, every, False, False)
+        quantise_g(1, 1, g11)
+        multiply2(1, 1, (0, 1), False, False)
 
-        room_w = place(UNIT, F32, "room_w", 20 * KB)
-        da_pair = place(2 * UNIT, BF16, "da_pair", 28 * KB)
-        da_sb[0], da_sb[1] = da_pair[:, 0:UNIT], da_pair[:, UNIT:]
+        room_w = place(UNIT, F32, "room_w", 56 * KB)
+        da_sb[0], da_sb[1] = place(UNIT, BF16, "da0", 64 * KB), place(UNIT, BF16, "da1", 68 * KB)
         v12 = gather("scalar", 2, C, room_w)
-        times_gate_shared(gate_banks[0], gate_0_tail, v02, g_pair_1[:, 0:UNIT])
-        spread_gate(2 * GROUPS, gate_banks[0][:])
-        codes(0, 2, own(C, U32, "words_02"), own(C, U8, "scales_02"))
-        quantise_g(0, 2, g_pair_1[:, 0:UNIT])
-        multiply2(0, 2, every, False, True)
-        slopes[1] = a_sb[0]
+        times_gate_shared(gate_banks[0], gate_0_tail, v02, ring)
+        slopes[1] = place(UNIT, F32, "slopes1", 19 * KB)
         slopes_on_vector(1)
+        codes(0, 2, own(C, U32, "words_02"), own(C, U8, "scales_02"))
+        last_pass(0, ring)
+        permute_words(2, 35 * KB)
 
         v21 = gather("scalar", 1, 2 * C, room_a)
+        room_x = place(UNIT, F32, "room_x", 27 * KB)
         v22 = gather("scalar", 2, 2 * C, room_x)
-        g12 = halves(a1_room[:, UNIT:])
-        times_gate_shared(gate_banks[1], gate_1b, v12, g12)
-        spread_gate(3 * GROUPS, gate_banks[1][:])
+        times_gate_shared(gate_banks[1], gate_1b, v12, ring)
+        spread_gate(2 * GROUPS, gate_banks[1][:])
         times_slope(0, every)
-        multiply2(1, 0, every, True, False)
-        multiply2(1, 1, every, False, False)
+        a_sb[2] = slopes[0]
+        load_a(2)
+        multiply2(1, 0, (2, 3), True, False)
+        multiply2(1, 1, (2, 3), False, False)
         codes(1, 2, own(C, U32, "words_12"), own(C, U8, "scales_12"))
-        quantise_g(1, 2, g12)
-        multiply2(1, 2, every, False, True)
-        permute_weights(2, 38 * KB + ALIGN, 42 * KB - ALIGN)
-        multiply1(0)
+        last_pass(1, ring)
+        multiply1(0, dx_banks[0])
         empty_dx(0)
 
         v31 = gather("scalar", 1, 3 * C, room_w)
-        times_gate_shared(gate_banks[0], gate_2b, v21, da_sb[0])
+        times_gate_shared(gate_banks[1], gate_2b, v21, ring)
+        multiply2(2, 0, (0, 1), True, False)
         times_slope(1, every)
-        multiply2(2, 0, every, True, False)
+        multiply2(2, 0, (2, 3), True, False)
         codes(2, 1, words_0[:, 0:C], scales_0[:, 0:C])
-        quantise_g(2, 1, da_sb[0])
+        quantise_g(2, 1, ring)
         multiply2(2, 1, every, False, False)
-        permute_weights(3, 44 * KB + ALIGN, 48 * KB - ALIGN)
-        multiply1(1)
+        multiply1(1, dx_banks[1])
         empty_dx(1)
-        slopes[2] = a_sb[0]
-        slopes_on_scalar(2, 0, GROUPS)
 
-        times_gate_shared(gate_banks[0], gate_2_tail, v22, da_sb[1])
+        ring = halves(slopes[1][:, rounded:])
+        times_gate_shared(gate_banks[1], gate_2_tail, v22, ring)
+        spread_gate(3 * GROUPS, gate_banks[1][:])
+        permute_words(3, 43 * KB + ALIGN)
         codes(2, 2, words_0[:, C:], scales_0[:, C:])
-        quantise_g(2, 2, da_sb[1])
-        multiply2(2, 2, every, False, True)
+        last_pass(2, ring)
+        slopes[2] = place(UNIT, F32, "slopes2", 47 * KB)
+        slopes_on_vector(2)
+        multiply2(3, 0, (0, 1, 2), True, False)
 
         last = list(zip(LAST_CUTS, LAST_CUTS[1:]))
         v32 = [gather("scalar", 2, 3 * C + lo, room_x[:, PACK * lo : PACK * hi]) for lo, hi in last]
-        times_gate_shared(gate_banks[1], gate_3[:, HALF:], v31, da_sb[1])
+        g31 = ring
+        times_gate_shared(gate_banks[1], gate_3[:, HALF:], v31, g31)
         slopes[3] = room_w
         slopes_on_scalar(3, 0, 2)
         slopes_on_scalar(3, 2, GROUPS)
         da_sb[2], da_sb[3] = g_pair[:, 0:UNIT], g_pair[:, UNIT:]
         times_slope(2, every)
-        multiply2(3, 0, every, True, False)
+        multiply2(3, 0, (3,), True, False)
         codes(3, 1, words_1[:, 0:C], scales_1[:, 0:C])
-        quantise_g(3, 1, da_sb[1])
+        quantise_g(3, 1, g31)
         multiply2(3, 1, every, False, False)
-        multiply1(2)
-        empty_dx(2)
         codes(3, 2, words_1[:, C:], scales_1[:, C:])
         for (lo, hi), values in zip(last, v32):
-            piece = halves(slopes[2][:, UNIT - 2 * hi : UNIT - 2 * lo])
+            piece = halves(slopes[2][:, rounded + 2 * lo : rounded + 2 * hi])
             times_gate(gate_banks[1][:, lo:hi], values, piece)
             quantise_g(3, 2, piece, lo)
             multiply2(3, 2, range(lo // P, hi // P), False, True)
-        for (lo, hi), bank in zip(last, (gate_banks[0], dx_bank, gate_banks[1])):
+        da_words.append(place(C, U32, "da_words2", 27 * KB))
+        da_words.append(da_words[1])
+        multiply1(2, dx_banks[2])
+        empty_dx(2)
+        for lo, hi in last:
+            bank = dh_bank(3, lo // P)
             times_slope(3, range(lo // P, hi // P))
-            multiply1(3, lo, hi, bank)
+            multiply1(3, bank, lo, hi)
             if hi < C:
                 nc.scalar.copy(dx_sb[:, 3 * C + lo : 3 * C + hi], bank[:, lo:hi])
             else:

@@ -17,6 +17,7 @@ ALIGN = 64
 KB = 1024
 OUT_CUTS = (0, 192, 448, 704, 896, T)
 SHARE = 96
+LAST_SHARE = 48
 PAD = 8
 LAST_CUTS = (0, HALF, C)
 
@@ -53,8 +54,8 @@ def tile_moe_bdx_mlp_relu2_kernel(
         banks = [psum.tile([P, 512], F32, name=f"bank{b}") for b in range(8)]
         gate_banks = banks[0:2]
         dx_bank = banks[6]
-        dh_banks = [banks[b] for b in (2, 3, 4, 5, 6, 7, 2, 3, 5, 0, 6, 7, 2, 4, 3, 5)]
-        dx_banks = [banks[4], banks[3], banks[0]]
+        dh_banks = [banks[b] for b in (2, 3, 4, 5, 6, 7, 0, 2, 3, 5, 6, 7, 3, 5, 6, 7)]
+        dx_banks = [banks[4], banks[0], banks[2]]
 
         def own(width, dtype, name):
             return keep.tile([P, width], dtype, name=name, align_bytes=ALIGN)[:]
@@ -111,9 +112,15 @@ def tile_moe_bdx_mlp_relu2_kernel(
 
         dy_rows = dyT.rearrange("(s p d) t -> s d p t", p=P, d=PACK)
 
-        def load_planes(s):
-            for d in range(PACK):
-                nc.sync.dma_start(out=planes[s][d][:, 0:T], in_=dy_rows[s, d])
+        def load_plane(s, d):
+            nc.sync.dma_start(out=planes[s][d][:, 0:T], in_=dy_rows[s, d])
+
+        def load_w2_scales(q):
+            for s in range(PASSES):
+                nc.sync.dma_start(
+                    out=sc_raw[32 * q : 32 * q + 4 * E, s * H : (s + 1) * H].bitcast(I32),
+                    in_=w2_scales.bitcast(I32)[:, s, 4 * q : 4 * q + 4, :],
+                )
 
         def load_w2(e):
             nc.sync.dma_start(
@@ -138,24 +145,22 @@ def tile_moe_bdx_mlp_relu2_kernel(
                 )
 
         nc.sync.dma_start(offs_sb[:], offs)
-        load_planes(0)
+        for d in range(PACK):
+            load_plane(0, d)
         nc.sync.dma_start(out=gate_rows, in_=gate[0 : P * P // SLOTS, :].rearrange("r (x c) -> (r x) c", c=P))
         load_gate(gate_3, SLOTS)
-        load_planes(1)
+        for d in range(PACK):
+            load_plane(1, d)
+            load_w2_scales(d)
         load_gate(gate_2a, 2 * C + HALF)
         load_w2(0)
-        for q in range(4):
-            for s in range(PASSES):
-                nc.sync.dma_start(
-                    out=sc_raw[32 * q : 32 * q + 4 * E, s * H : (s + 1) * H].bitcast(I32),
-                    in_=w2_scales.bitcast(I32)[:, s, 4 * q : 4 * q + 4, :],
-                )
         load_a(0)
-        load_gate(gate_1b, 2 * C)
-        load_planes(2)
-        load_gate(gate_0_tail, C)
         load_w2(1)
+        load_gate(gate_1b, 2 * C)
+        for d in range(PACK):
+            load_plane(2, d)
         load_a(1)
+        load_gate(gate_0_tail, C)
         load_gate(gate_2b, 3 * C)
         load_gate(gate_2_tail, 3 * C)
         load_w2(2)
@@ -209,7 +214,7 @@ def tile_moe_bdx_mlp_relu2_kernel(
             )
 
         def times_gate_shared(bank, tail, values, dest):
-            cut = C - tail.shape[1]
+            cut = values.shape[2] - tail.shape[1]
             times_gate_on_gpsimd(tail, values[:, :, cut:], dest[:, PACK * cut :])
             times_gate(bank[:, 0:cut], values[:, :, 0:cut], dest[:, 0 : PACK * cut])
 
@@ -361,6 +366,8 @@ def tile_moe_bdx_mlp_relu2_kernel(
         slopes_on_vector(1)
         codes(0, 2, own(C, U32, "words_02"), own(C, U8, "scales_02"))
         last_pass(0, ring)
+        multiply2(1, 0, (2,), True, False)
+        multiply2(1, 1, (2,), False, False)
         permute_words(2, 35 * KB)
 
         v21 = gather("scalar", 1, 2 * C, room_a)
@@ -371,8 +378,8 @@ def tile_moe_bdx_mlp_relu2_kernel(
         times_slope(0, every)
         a_sb[2] = slopes[0]
         load_a(2)
-        multiply2(1, 0, (2, 3), True, False)
-        multiply2(1, 1, (2, 3), False, False)
+        multiply2(1, 0, (3,), True, False)
+        multiply2(1, 1, (3,), False, False)
         codes(1, 2, own(C, U32, "words_12"), own(C, U8, "scales_12"))
         last_pass(1, ring)
         multiply1(0, dx_banks[0])
@@ -397,7 +404,6 @@ def tile_moe_bdx_mlp_relu2_kernel(
         last_pass(2, ring)
         slopes[2] = place(UNIT, F32, "slopes2", 47 * KB)
         slopes_on_vector(2)
-        multiply2(3, 0, (0, 1, 2), True, False)
 
         last = list(zip(LAST_CUTS, LAST_CUTS[1:]))
         v32 = [gather("scalar", 2, 3 * C + lo, room_x[:, PACK * lo : PACK * hi]) for lo, hi in last]
@@ -408,14 +414,14 @@ def tile_moe_bdx_mlp_relu2_kernel(
         slopes_on_scalar(3, 2, GROUPS)
         da_sb[2], da_sb[3] = g_pair[:, 0:UNIT], g_pair[:, UNIT:]
         times_slope(2, every)
-        multiply2(3, 0, (3,), True, False)
+        multiply2(3, 0, every, True, False)
         codes(3, 1, words_1[:, 0:C], scales_1[:, 0:C])
         quantise_g(3, 1, g31)
         multiply2(3, 1, every, False, False)
         codes(3, 2, words_1[:, C:], scales_1[:, C:])
         for (lo, hi), values in zip(last, v32):
             piece = halves(slopes[2][:, rounded + 2 * lo : rounded + 2 * hi])
-            times_gate(gate_banks[1][:, lo:hi], values, piece)
+            times_gate_shared(gate_banks[1][:, lo:hi], gate_3[:, hi - LAST_SHARE : hi], values, piece)
             quantise_g(3, 2, piece, lo)
             multiply2(3, 2, range(lo // P, hi // P), False, True)
         da_words.append(place(C, U32, "da_words2", 27 * KB))

@@ -18,6 +18,7 @@ KB = 1024
 OUT_CUTS = (0, 192, 448, 704, 896, T)
 SHARE = 96
 LAST_SHARE = 48
+WIDE_SHARE = 224
 PAD = 8
 LAST_CUTS = (0, HALF, C)
 
@@ -80,9 +81,9 @@ def tile_moe_bdx_mlp_relu2_kernel(
         gate_columns = own(SLOTS // P, F32, "gate_columns")
         gate_0_tail = place(SHARE, F32, "gate_0_tail", 19 * KB)
         gate_2_tail = place(SHARE, F32, "gate_2_tail", 46 * KB)
-        gate_1b = own(HALF, F32, "gate_1b")
+        gate_1b = own(WIDE_SHARE, F32, "gate_1b")
         gate_2a = own(HALF, F32, "gate_2a")
-        gate_2b = own(HALF, F32, "gate_2b")
+        gate_2b = own(WIDE_SHARE, F32, "gate_2b")
         gate_3 = own(C, F32, "gate_3")
         w2_raw = [own(PASSES * H, U16, f"w2_raw{e}") for e in range(3)]
         w2_raw = w2_raw + [place(PASSES * H, U16, "w2_raw3", 47 * KB)]
@@ -380,7 +381,7 @@ def tile_moe_bdx_mlp_relu2_kernel(
         load_a(2)
         multiply2(1, 0, (3,), True, False)
         multiply2(1, 1, (3,), False, False)
-        codes(1, 2, own(C, U32, "words_12"), own(C, U8, "scales_12"))
+        codes(1, 2, g_words[0, 2], g_scales[0, 2])
         last_pass(1, ring)
         multiply1(0, dx_banks[0])
         empty_dx(0)
@@ -390,13 +391,12 @@ def tile_moe_bdx_mlp_relu2_kernel(
         multiply2(2, 0, (0, 1), True, False)
         times_slope(1, every)
         multiply2(2, 0, (2, 3), True, False)
-        codes(2, 1, words_0[:, 0:C], scales_0[:, 0:C])
+        codes(2, 1, g_words[0, 2], g_scales[0, 2])
         quantise_g(2, 1, ring)
         multiply2(2, 1, every, False, False)
         multiply1(1, dx_banks[1])
         empty_dx(1)
 
-        ring = halves(slopes[1][:, rounded:])
         times_gate_shared(gate_banks[1], gate_2_tail, v22, ring)
         spread_gate(3 * GROUPS, gate_banks[1][:])
         permute_words(3, 43 * KB + ALIGN)
@@ -408,14 +408,14 @@ def tile_moe_bdx_mlp_relu2_kernel(
         last = list(zip(LAST_CUTS, LAST_CUTS[1:]))
         v32 = [gather("scalar", 2, 3 * C + lo, room_x[:, PACK * lo : PACK * hi]) for lo, hi in last]
         g31 = ring
-        times_gate_shared(gate_banks[1], gate_3[:, HALF:], v31, g31)
+        times_gate_shared(gate_banks[1], gate_3[:, C - WIDE_SHARE :], v31, g31)
         slopes[3] = room_w
         slopes_on_scalar(3, 0, 2)
         slopes_on_scalar(3, 2, GROUPS)
         da_sb[2], da_sb[3] = g_pair[:, 0:UNIT], g_pair[:, UNIT:]
         times_slope(2, every)
         multiply2(3, 0, every, True, False)
-        codes(3, 1, words_1[:, 0:C], scales_1[:, 0:C])
+        codes(3, 1, g_words[2, 2], g_scales[2, 2])
         quantise_g(3, 1, g31)
         multiply2(3, 1, every, False, False)
         codes(3, 2, words_1[:, C:], scales_1[:, C:])

@@ -80,10 +80,10 @@ def tile_moe_bdx_mlp_relu2_kernel(
         gate_rows = place(P, F32, "gate_rows", 3 * KB + KB // 2)
         gate_columns = own(SLOTS // P, F32, "gate_columns")
         gate_0_tail = place(SHARE, F32, "gate_0_tail", 19 * KB)
-        gate_2_tail = place(SHARE, F32, "gate_2_tail", 46 * KB)
+        gate_2_tail = place(SHARE, F32, "gate_2_tail", 39 * KB)
         gate_1b = own(WIDE_SHARE, F32, "gate_1b")
         gate_2a = own(HALF, F32, "gate_2a")
-        gate_2b = own(WIDE_SHARE, F32, "gate_2b")
+        gate_2b = place(WIDE_SHARE, F32, "gate_2b", 46 * KB)
         gate_3 = own(C, F32, "gate_3")
         w2_raw = [own(PASSES * H, U16, f"w2_raw{e}") for e in range(3)]
         w2_raw = w2_raw + [place(PASSES * H, U16, "w2_raw3", 47 * KB)]
@@ -98,7 +98,7 @@ def tile_moe_bdx_mlp_relu2_kernel(
         room_a = wide_0[:, 0:UNIT]
         room_30 = own(UNIT, F32, "room_30")
         da_words = [own(C, U32, f"da_words{r}") for r in range(2)]
-        da_scales = [own(C, U8, f"da_scales{r}") for r in range(2)]
+        da_scales = [own(C, U8, "da_scales0")]
         dx_sb = own(SLOTS, F32, "dx_sb")
         g_words, g_scales, w2_sb, w2_sc, slopes, da_sb = {}, {}, {}, {}, {}, {}
 
@@ -388,21 +388,22 @@ def tile_moe_bdx_mlp_relu2_kernel(
 
         v31 = gather("scalar", 1, 3 * C, room_w)
         times_gate_shared(gate_banks[1], gate_2b, v21, ring)
+        permute_words(3, 43 * KB + ALIGN)
         multiply2(2, 0, (0, 1), True, False)
         times_slope(1, every)
         multiply2(2, 0, (2, 3), True, False)
         codes(2, 1, g_words[0, 2], g_scales[0, 2])
         quantise_g(2, 1, ring)
         multiply2(2, 1, every, False, False)
-        multiply1(1, dx_banks[1])
-        empty_dx(1)
 
         times_gate_shared(gate_banks[1], gate_2_tail, v22, ring)
         spread_gate(3 * GROUPS, gate_banks[1][:])
-        permute_words(3, 43 * KB + ALIGN)
+        da_scales.append(place(C, U8, "da_scales1", 39 * KB))
+        multiply1(1, dx_banks[1])
+        empty_dx(1)
         codes(2, 2, words_0[:, C:], scales_0[:, C:])
         last_pass(2, ring)
-        slopes[2] = place(UNIT, F32, "slopes2", 47 * KB)
+        slopes[2] = place(UNIT, F32, "slopes2", 64 * KB)
         slopes_on_vector(2)
 
         last = list(zip(LAST_CUTS, LAST_CUTS[1:]))

from contextlib import ExitStack

import concourse.mybir as mybir
from concourse.masks import make_identity

K, T, E, C, H, N = 128, 1024, 4, 512, 512, 1536
P = 128
PACK = 4
RUN = 2
SLOTS = E * C
PASSES = N // 512
GROUPS = C // P
HALF = C // 2
UNIT = PACK * C
W1_BYTES = 2 * K
ALIGN = 64
KB = 1024
OUT_CUTS = (0, 192, 448, 704, 896, T)
SHARE = 96
LAST_SHARE = 48
WIDE_SHARE = 224
PAD = 8
LAST_CUTS = (0, HALF, C)

FLOPS = 2 * SLOTS * (N * H + H * K)
BYTES = (
    4 * N * T + 4 * H * SLOTS + E * PASSES * (128 * 1024 + 16 * 512)
    + E * (128 * 256 + 16 * 128) + 4 * SLOTS + 2 * 128 * (128 + 64 + 64) + 4 * K * T
)

F32 = mybir.dt.float32
BF16 = mybir.dt.bfloat16
I32 = mybir.dt.int32
U32 = mybir.dt.uint32
U16 = mybir.dt.uint16
U8 = mybir.dt.uint8
E5M2 = mybir.dt.float8_e5m2_x4
E2M1 = mybir.dt.float4_e2m1fn_x4
MULT = mybir.AluOpType.mult
ADD = mybir.AluOpType.add
MAX = mybir.AluOpType.max
COPY = mybir.ActivationFunctionType.Copy
RELU = mybir.ActivationFunctionType.Relu


def tile_moe_bdx_mlp_relu2_kernel(
    tc, dyT, a, w2_words, w2_scales, w1_words, w1_scales, gate, offs, pos1, pos2, out
):
    nc = tc.nc
    with ExitStack() as ctx:
        keep = ctx.enter_context(tc.tile_pool(name="keep", bufs=1))
        placed = ctx.enter_context(tc.tile_pool(name="placed", bufs=1))
        psum = ctx.enter_context(tc.psum_pool(name="psum", bufs=1))

        banks = [psum.tile([P, 512], F32, name=f"bank{b}") for b in range(8)]
        gate_banks = banks[0:2]
        dx_bank = banks[6]
        dh_banks = [banks[b] for b in (2, 3, 4, 5, 6, 7, 0, 2, 3, 5, 6, 7, 3, 5, 6, 7)]
        dx_banks = [banks[4], banks[0], banks[2]]

        def own(width, dtype, name):
            return keep.tile([P, width], dtype, name=name, align_bytes=ALIGN)[:]

        def place(width, dtype, name, at):
            return placed.tile([P, width], dtype, name=name, offset=at, align_bytes=ALIGN)[:]

        def by_plane(ap):
            return ap.rearrange("p (d c) -> p d c", d=PACK)

        def halves(ap):
            return ap.bitcast(BF16)

        rounded = UNIT // 2
        offs_sb = keep.tile([P, SLOTS // 16], U16, name="offs_sb")
        pos1_sb = keep.tile([P, T // 16], U16, name="pos1_sb")
        pos2_sb = keep.tile([P, T // 16], U16, name="pos2_sb")
        planes = [
            [own(T + PAD if s < PASSES - 1 else T, F32, f"plane{s}_{d}") for d in range(PACK)] for s in range(PASSES)
        ]
        gate_rows = place(P, F32, "gate_rows", 3 * KB + KB // 2)
        gate_columns = own(SLOTS // P, F32, "gate_columns")
        gate_0_tail = place(SHARE, F32, "gate_0_tail", 19 * KB)
        gate_2_tail = place(SHARE, F32, "gate_2_tail", 39 * KB)
        gate_1b = own(WIDE_SHARE, F32, "gate_1b")
        gate_2a = own(HALF, F32, "gate_2a")
        gate_2b = place(WIDE_SHARE, F32, "gate_2b", 46 * KB)
        gate_3 = own(C, F32, "gate_3")
        w2_raw = [own(PASSES * H, U16, f"w2_raw{e}") for e in range(3)]
        w2_raw = w2_raw + [place(PASSES * H, U16, "w2_raw3", 47 * KB)]
        sc_raw = own(PASSES * H, U8, "sc_raw")
        sc_rest = own((E - 1) * PASSES * H, U8, "sc_rest")
        w1_sb = own(E * W1_BYTES, U8, "w1_sb")
        w1_sc = own(E * K, U8, "w1_sc")
        ident = own(P, F32, "ident")
        a_sb = [own(UNIT, F32, "a0"), place(UNIT, F32, "a1", 30 * KB), None, own(UNIT, F32, "a3")]
        wide_0 = own(2 * UNIT, F32, "wide_0")
        wide_1 = place(2 * UNIT, F32, "wide_1", 56 * KB)
        room_a = wide_0[:, 0:UNIT]
        room_30 = own(UNIT, F32, "room_30")
        da_words = [own(C, U32, f"da_words{r}") for r in range(2)]
        da_scales = [own(C, U8, "da_scales0")]
        dx_sb = own(SLOTS, F32, "dx_sb")
        g_words, g_scales, w2_sb, w2_sc, slopes, da_sb = {}, {}, {}, {}, {}, {}

        nc.gpsimd.memset(sc_raw.bitcast(I32), 0)
        nc.vector.memset(sc_rest.bitcast(I32), 0)
        nc.vector.memset(w1_sc[:, 0 : 2 * K].bitcast(I32), 0)
        nc.scalar.copy(w1_sc[:, 2 * K : 4 * K].bitcast(U32), w1_sc[:, 0 : 2 * K].bitcast(U32))
        for s in range(PASSES - 1):
            for d in range(PACK):
                nc.vector.memset(planes[s][d][:, T:], 0.0)
        make_identity(nc, ident)

        dy_rows = dyT.rearrange("(s p d) t -> s d p t", p=P, d=PACK)

        def load_plane(s, d):
            nc.sync.dma_start(out=planes[s][d][:, 0:T], in_=dy_rows[s, d])

        def load_w2_scales(q):
            for s in range(PASSES):
                nc.sync.dma_start(
                    out=sc_raw[32 * q : 32 * q + 4 * E, s * H : (s + 1) * H].bitcast(I32),
                    in_=w2_scales.bitcast(I32)[:, s, 4 * q : 4 * q + 4, :],
                )

        def load_w2(e):
            nc.sync.dma_start(
                out=w2_raw[e].bitcast(I32).rearrange("p (s w) -> p s w", s=PASSES),
                in_=w2_words.bitcast(I32)[e].rearrange("s p w -> p s w"),
            )

        def load_a(e):
            nc.sync.dma_start(
                out=by_plane(a_sb[e]), in_=a[:, e * C : (e + 1) * C].rearrange("(p d) c -> p d c", d=PACK)
            )

        def load_gate(tile, end):
            nc.sync.dma_start(out=tile, in_=gate[0:P, end - tile.shape[1] : end])

        def load_scales(tile, source, runs):
            src = source.bitcast(I32).rearrange("e s f w -> f (e s) w")
            for q in range(4):
                nc.sync.dma_start(
                    out=tile[32 * q : 32 * q + 4, :].bitcast(I32).rearrange("f (x w) -> f x w", x=runs),
                    in_=src[4 * q : 4 * q + 4],
                )

        nc.sync.dma_start(offs_sb[:], offs)
        for d in range(PACK):
            load_plane(0, d)
        nc.sync.dma_start(out=gate_rows, in_=gate[0 : P * P // SLOTS, :].rearrange("r (x c) -> (r x) c", c=P))
        load_gate(gate_3, SLOTS)
        for d in range(PACK):
            load_plane(1, d)
            load_w2_scales(d)
        load_gate(gate_2a, 2 * C + HALF)
        load_w2(0)
        load_a(0)
        load_w2(1)
        load_gate(gate_1b, 2 * C)
        for d in range(PACK):
            load_plane(2, d)
        load_a(1)
        load_gate(gate_0_tail, C)
        load_gate(gate_2b, 3 * C)
        load_gate(gate_2_tail, 3 * C)
        load_w2(2)
        load_scales(w1_sc, w1_scales, E)
        nc.sync.dma_start(
            out=w1_sb.bitcast(I32).rearrange("p (e w) -> p e w", e=E),
            in_=w1_words.bitcast(I32).rearrange("e s p w -> p (e s) w"),
        )
        load_w2(3)
        load_a(3)
        nc.sync.dma_start(pos1_sb[:], pos1)
        nc.sync.dma_start(pos2_sb[:], pos2)

        def gather(engine, s, slot0, room):
            width = room.shape[1] // PACK
            for d in range(PACK):
                window = planes[s][d].indirect(offs_sb[:, slot0 // 16 : (slot0 + width) // 16])
                if engine == "scalar":
                    nc.scalar.activation(room[:, d * width : (d + 1) * width], window, COPY)
                else:
                    nc.vector.tensor_copy(room[:, d * width : (d + 1) * width], window)
            return by_plane(room)

        def in_runs(ap):
            return ap.rearrange("p (d c r) -> p c d r", d=PACK, r=RUN)

        def woven(ap):
            return ap.rearrange("p (c r d) -> p c d r", r=RUN, d=PACK)

        def spread_gate(group0, dest):
            for x in range(dest.shape[1] // P):
                column = gate_columns[:, group0 + x : group0 + x + 1]
                nc.tensor.transpose(dest[:, x * P : (x + 1) * P], column.to_broadcast([P, P]), ident)

        def times_gate(gates, values, dest):
            width = gates.shape[1]
            runs = gates.rearrange("p (c r) -> p c r", r=RUN)
            nc.vector.tensor_tensor(
                woven(dest),
                values.rearrange("p d (c r) -> p c d r", r=RUN),
                runs.unsqueeze(2).to_broadcast([P, width // RUN, PACK, RUN]),
                MULT,
            )

        def times_gate_on_gpsimd(gates, values, dest):
            nc.gpsimd.tensor_tensor(
                dest.rearrange("p (c d) -> p c d", d=PACK),
                values.rearrange("p d c -> p c d"),
                gates.unsqueeze(2).to_broadcast([P, gates.shape[1], PACK]),
                MULT,
            )

        def times_gate_shared(bank, tail, values, dest):
            cut = values.shape[2] - tail.shape[1]
            times_gate_on_gpsimd(tail, values[:, :, cut:], dest[:, PACK * cut :])
            times_gate(bank[:, 0:cut], values[:, :, 0:cut], dest[:, 0 : PACK * cut])

        def quantise(source, words, scales):
            nc.vector.quantize_mx(out=words.bitcast(E5M2), scales=scales, in_=source)

        def quantise_g(e, s, source, lo=0):
            hi = lo + source.shape[1] // PACK
            quantise(source, g_words[e, s][:, lo:hi], g_scales[e, s][:, lo:hi])

        def codes(e, s, words, scales):
            g_words[e, s], g_scales[e, s] = words, scales

        def permute(dest, source):
            nc.vector.tensor_copy(
                dest.rearrange("p (s t m) -> p t s m", s=PASSES, t=PACK),
                source.rearrange("p (s m t) -> p t s m", s=PASSES, t=PACK),
            )

        def permute_words(e, at):
            w2_sb[e] = place(PASSES * H, U16, f"w2_{e}", at)
            permute(w2_sb[e], w2_raw[e])

        def permute_scales(at):
            w2_sc[0] = place(PASSES * H, U8, "w2_sc", at)
            permute(w2_sc[0], sc_raw)
            for e in range(1, E):
                w2_sc[e] = sc_rest[:, (e - 1) * PASSES * H : e * PASSES * H]
                for q in range(4):
                    nc.sync.dma_start(
                        out=w2_sc[e][32 * q : 32 * q + 4, :].bitcast(I32),
                        in_=w2_sc[0][32 * q + 4 * e : 32 * q + 4 * e + 4, :].bitcast(I32),
                    )

        def by_group(e):
            return (
                slopes[e].rearrange("p (x d c) -> p x d c", x=GROUPS, d=PACK),
                a_sb[e].rearrange("p (d x c) -> p x d c", x=GROUPS, d=PACK),
            )

        def slopes_on_vector(e):
            dest, source = by_group(e)
            nc.vector.tensor_scalar(dest, source, 0.0, 2.0, MAX, MULT)

        def slopes_on_scalar(e, lo, hi):
            dest, source = by_group(e)
            nc.scalar.activation(dest[:, lo:hi], source[:, lo:hi], RELU, scale=2.0)

        def dh_bank(e, x):
            return dh_banks[e * GROUPS + x]

        def multiply2(e, s, groups, opens, closes):
            for x in groups:
                for t in range(PACK):
                    at = s * H + t * P
                    nc.tensor.matmul_mx(
                        out=dh_bank(e, x)[:, t * P : (t + 1) * P],
                        lhsT=w2_sb[e][:, at : at + P].bitcast(U8).bitcast(E2M1),
                        lhsT_scale=w2_sc[e][:, at : at + P],
                        rhs=g_words[e, s][:, x * P : (x + 1) * P].bitcast(E5M2),
                        rhs_scale=g_scales[e, s][:, x * P : (x + 1) * P],
                        start=(opens and t == 0),
                        stop=(closes and t == PACK - 1),
                    )

        def times_slope(e, groups):
            for x in groups:
                nc.vector.tensor_tensor(
                    woven(da_sb[e][:, x * H : (x + 1) * H]),
                    in_runs(dh_bank(e, x)[:]),
                    in_runs(slopes[e][:, x * H : (x + 1) * H]),
                    MULT,
                )

        def multiply1(e, bank, lo=0, hi=C):
            quantise(da_sb[e][:, PACK * lo : PACK * hi], da_words[e][:, lo:hi], da_scales[e % 2][:, lo:hi])
            nc.tensor.matmul_mx(
                out=bank[:, lo:hi],
                lhsT=w1_sb[:, e * W1_BYTES : (e + 1) * W1_BYTES].bitcast(E2M1),
                lhsT_scale=w1_sc[:, e * K : (e + 1) * K],
                rhs=da_words[e][:, lo:hi].bitcast(E5M2),
                rhs_scale=da_scales[e % 2][:, lo:hi],
                start=True,
                stop=True,
            )

        def empty_dx(e):
            nc.scalar.copy(dx_sb[:, e * C : (e + 1) * C], dx_banks[e][:])

        def last_pass(e, source):
            for lo in (0, HALF):
                quantise_g(e, PASSES - 1, source[:, PACK * lo : PACK * (lo + HALF)], lo)
                multiply2(e, PASSES - 1, range(lo // P, (lo + HALF) // P), False, True)

        every = range(GROUPS)

        nc.tensor.transpose(dx_bank[:, 0:P], gate_rows, ident)
        nc.vector.tensor_copy(gate_columns, dx_bank[:, 0 : SLOTS // P])
        spread_gate(0, gate_banks[0][:])
        spread_gate(GROUPS, gate_banks[1][:])
        spread_gate(3 * GROUPS - 2, dx_bank[:, HALF:])

        pair_0 = gather("scalar", 0, 0, wide_0)
        v30 = gather("vector", 0, 3 * C, room_30)
        g30 = own(UNIT, BF16, "g30")
        times_gate_on_gpsimd(gate_3, v30, g30)
        v20 = gather("vector", 0, 2 * C, place(UNIT, F32, "room_20", 3 * KB))
        g20 = own(UNIT, BF16, "g20")
        times_gate_on_gpsimd(gate_2a, v20[:, :, 0:HALF], g20[:, 0:rounded])
        pair_1 = gather("scalar", 1, 0, wide_1)
        g_pair = own(2 * UNIT, BF16, "g_pair")
        for e in range(2):
            times_gate(gate_banks[e][:], pair_0[:, :, e * C : (e + 1) * C], g_pair[:, e * UNIT : (e + 1) * UNIT])
        times_gate(dx_bank[:, HALF:], v20[:, :, HALF:], g20[:, rounded:])

        words_0, scales_0 = own(2 * C, U32, "words_0"), place(2 * C, U8, "scales_0", 4 * KB)
        quantise(g_pair, words_0, scales_0)
        codes(0, 0, words_0[:, 0:C], scales_0[:, 0:C])
        codes(1, 0, words_0[:, C:], scales_0[:, C:])
        permute_scales(8 * KB + KB // 2)
        permute_words(0, 5 * KB + KB // 2)
        multiply2(0, 0, every, True, False)
        codes(3, 0, own(C, U32, "words_30"), place(C, U8, "scales_30", 5 * KB))
        quantise_g(3, 0, g30)
        permute_words(1, ALIGN)
        multiply2(1, 0, (0, 1), True, False)
        slopes[0] = place(UNIT, F32, "slopes0", 10 * KB + KB // 2)
        slopes_on_vector(0)
        codes(2, 0, own(C, U32, "words_20"), place(C, U8, "scales_20", 10 * KB))
        quantise_g(2, 0, g20)

        ring, g11 = halves(a_sb[0][:, 0:rounded]), halves(a_sb[0][:, rounded:])
        times_gate(gate_banks[0][:], pair_1[:, :, 0:C], ring)
        times_gate_shared(gate_banks[1], gate_1b, pair_1[:, :, C:], g11)
        v02 = gather("scalar", 2, 0, room_a)
        words_1, scales_1 = own(2 * C, U32, "words_1"), own(2 * C, U8, "scales_1")
        codes(0, 1, words_1[:, 0:C], scales_1[:, 0:C])
        codes(1, 1, words_1[:, C:], scales_1[:, C:])
        quantise_g(0, 1, ring)
        multiply2(0, 1, every, False, False)
        quantise_g(1, 1, g11)
        multiply2(1, 1, (0, 1), False, False)

        room_w = place(UNIT, F32, "room_w", 56 * KB)
        da_sb[0], da_sb[1] = place(UNIT, BF16, "da0", 64 * KB), place(UNIT, BF16, "da1", 68 * KB)
        v12 = gather("scalar", 2, C, room_w)
        times_gate_shared(gate_banks[0], gate_0_tail, v02, ring)
        slopes[1] = place(UNIT, F32, "slopes1", 19 * KB)
        slopes_on_vector(1)
        codes(0, 2, own(C, U32, "words_02"), own(C, U8, "scales_02"))
        last_pass(0, ring)
        multiply2(1, 0, (2,), True, False)
        multiply2(1, 1, (2,), False, False)
        permute_words(2, 35 * KB)

        v21 = gather("scalar", 1, 2 * C, room_a)
        room_x = place(UNIT, F32, "room_x", 27 * KB)
        v22 = gather("scalar", 2, 2 * C, room_x)
        times_gate_shared(gate_banks[1], gate_1b, v12, ring)
        spread_gate(2 * GROUPS, gate_banks[1][:])
        times_slope(0, every)
        a_sb[2] = slopes[0]
        load_a(2)
        multiply2(1, 0, (3,), True, False)
        multiply2(1, 1, (3,), False, False)
        codes(1, 2, g_words[0, 2], g_scales[0, 2])
        last_pass(1, ring)
        multiply1(0, dx_banks[0])
        empty_dx(0)

        v31 = gather("scalar", 1, 3 * C, room_w)
        times_gate_shared(gate_banks[1], gate_2b, v21, ring)
        permute_words(3, 43 * KB + ALIGN)
        multiply2(2, 0, (0, 1), True, False)
        times_slope(1, every)
        multiply2(2, 0, (2, 3), True, False)
        codes(2, 1, g_words[0, 2], g_scales[0, 2])
        quantise_g(2, 1, ring)
        multiply2(2, 1, every, False, False)

        times_gate_shared(gate_banks[1], gate_2_tail, v22, ring)
        spread_gate(3 * GROUPS, gate_banks[1][:])
        da_scales.append(place(C, U8, "da_scales1", 39 * KB))
        multiply1(1, dx_banks[1])
        empty_dx(1)
        codes(2, 2, words_0[:, C:], scales_0[:, C:])
        last_pass(2, ring)
        slopes[2] = place(UNIT, F32, "slopes2", 64 * KB)
        slopes_on_vector(2)

        last = list(zip(LAST_CUTS, LAST_CUTS[1:]))
        v32 = [gather("scalar", 2, 3 * C + lo, room_x[:, PACK * lo : PACK * hi]) for lo, hi in last]
        g31 = ring
        times_gate_shared(gate_banks[1], gate_3[:, C - WIDE_SHARE :], v31, g31)
        slopes[3] = room_w
        slopes_on_scalar(3, 0, 2)
        slopes_on_scalar(3, 2, GROUPS)
        da_sb[2], da_sb[3] = g_pair[:, 0:UNIT], g_pair[:, UNIT:]
        times_slope(2, every)
        multiply2(3, 0, every, True, False)
        codes(3, 1, g_words[2, 2], g_scales[2, 2])
        quantise_g(3, 1, g31)
        multiply2(3, 1, every, False, False)
        codes(3, 2, words_1[:, C:], scales_1[:, C:])
        for (lo, hi), values in zip(last, v32):
            piece = halves(slopes[2][:, rounded + 2 * lo : rounded + 2 * hi])
            times_gate_shared(gate_banks[1][:, lo:hi], gate_3[:, hi - LAST_SHARE : hi], values, piece)
            quantise_g(3, 2, piece, lo)
            multiply2(3, 2, range(lo // P, hi // P), False, True)
        da_words.append(place(C, U32, "da_words2", 27 * KB))
        da_words.append(da_words[1])
        multiply1(2, dx_banks[2])
        empty_dx(2)
        for lo, hi in last:
            bank = dh_bank(3, lo // P)
            times_slope(3, range(lo // P, hi // P))
            multiply1(3, bank, lo, hi)
            if hi < C:
                nc.scalar.copy(dx_sb[:, 3 * C + lo : 3 * C + hi], bank[:, lo:hi])
            else:
                nc.vector.tensor_copy(dx_sb[:, 3 * C + lo : 3 * C + hi], bank[:, lo:hi])

        first, total = wide_0[:, UNIT:], a_sb[3]
        for lo, hi in zip(OUT_CUTS, OUT_CUTS[1:]):
            window = dx_sb.indirect(pos1_sb[:, lo // 16 : hi // 16])
            if lo == 0:
                nc.vector.tensor_copy(first[:, lo:hi], window)
            else:
                nc.scalar.activation(first[:, lo:hi], window, COPY)
            nc.vector.tensor_tensor(
                total[:, lo:hi], dx_sb.indirect(pos2_sb[:, lo // 16 : hi // 16]), first[:, lo:hi], ADD
            )
            nc.sync.dma_start(out=out[:, lo:hi], in_=total[:, lo:hi])
